import numpy as np, ml_dtypes
CORES = [9,25,41,57]
N = 4
import mx_ref
BF = ml_dtypes.bfloat16
def gcols(t, e):
    v = np.concatenate([t.reshape(8, 16, -1, 4), np.zeros((8, 16, 1, 4), BF)], axis=2)
    return np.ascontiguousarray(np.stack([v[g][:, e[g]] for g in range(8)])).reshape(128, -1)
def tile(rs):
    return np.stack(rs, axis=2).reshape(128, -1).astype(BF)
def pick(q, e):
    c = np.concatenate([q[0].reshape(128, -1, 4), np.zeros((128, 1, 4), np.uint8)], axis=1); s = np.concatenate([q[1], np.ones((16, 1), np.uint8)], axis=1)
    return (np.ascontiguousarray(c[:, e].reshape(128, -1)), np.ascontiguousarray(s[:, e]))
def join(*qs):
    return (np.concatenate([q[0] for q in qs], axis=1), np.concatenate([q[1] for q in qs], axis=1))
def put(q, e, v):
    c, s = q[0].reshape(128, -1, 4).copy(), q[1].copy(); c[:, e] = v[0].reshape(128, -1, 4); s[:, e] = v[1]
    return (c.reshape(128, -1), s)
def pk(c, s):
    return (np.ascontiguousarray(c), mx_ref.live(s))
def emit(q):
    return q[0], q[1]
def packed(v, rng):
    q = [mx_ref.quantize(np.ascontiguousarray(v[r])) for r in range(N)]
    return np.stack([a for a, b in q]), np.stack([mx_ref.plane(b, rng) for a, b in q])
def values_of_codes():
    e, c = np.zeros((128, 128, 4), np.float32), np.zeros((128, 2, 4), np.uint8)
    e[np.arange(128), np.arange(128), 0] = 1
    c[:127, :, 0] = np.arange(256).reshape(2, 128).T[:127]
    return mx_ref.matmul(mx_ref.quantize(e.reshape(128, 512).astype(BF)), (c.reshape(128, 8), np.full((16, 2), 127, np.uint8))).T.reshape(-1).astype(np.float64)
CODE_VALUE, SCALE_VALUE = values_of_codes(), 2.0 ** (np.arange(256) - 127.0)
def decode(q):
    return (CODE_VALUE[q[0]].reshape(16, 8, -1, 4) * SCALE_VALUE[q[1]][:, None, :, None] + 0.0).reshape(128, -1).astype(np.float32)
def f(rng, *shape):
    return mx_ref.flush((rng.standard_normal(shape, dtype=np.float32) * np.exp2(rng.integers(-2, 3, shape[:-1] + (1,)))).astype(BF))
def wide(rng, *shape, cols=0):
    v = rng.standard_normal(shape, dtype=np.float32) * np.exp2(rng.integers(-12, 13, shape)).astype(np.float32)
    if cols: v *= np.repeat(np.exp2(rng.integers(-cols, cols + 1, shape[:-2] + (1, shape[-1] // 4))) * (rng.random(shape[:-2] + (1, shape[-1] // 4)) > 0.0625), 4, axis=-1).astype(np.float32)
    return mx_ref.flush(v.astype(BF))
C, R = 448, 2
SETS = np.arange(256)
ONE = (1 << np.arange(8))[:, None]
DECIDE = [16 * g + k for g in range(8) for k in range(10)] + [15]
def bits(b):
    return np.packbits(b, axis=-2, bitorder="little")[..., 0, :].astype(np.int64)
def numbers_of(rng):
    return {"x": np.array(f(rng, N, 128, 4 * C)), "u": np.array(f(rng, N, 128, 512)), "v": np.array(f(rng, N, 128, 512))}
def same(rng, w):
    c, s = packed(np.stack([w] * N), rng)
    return {"wc": c, "ws": np.stack([s[0]] * N)}
def weights(rng, keep=np.ones((8, 16), bool)):
    w = f(rng, 128, 2048).astype(np.float32).reshape(8, 16, 4, 8, 16, 4)
    w = np.where(keep[:, :, None, None, None, None] & keep[:, :, None], w, np.float32(0.0))
    return same(rng, w.reshape(128, 2048).astype(BF))
def setup_inputs(rng):
    return {**numbers_of(rng), **weights(rng)}
def setup_inputs_ties(rng):
    d = numbers_of(rng)
    e = rng.permutation(N)
    x = d["x"].reshape(N, 8, 16, C, 4)
    x[:, :, 0] = rng.integers(0, 3, (N, 8, C, 4)).astype(np.float32).astype(BF)
    x[e[0], 0, 0, :, 3] = 2.0
    x[e[1]] = 0.0
    u = d["u"].reshape(N, 128, 128, 4)
    u[:, :, DECIDE] = 0.0
    for g in range(8):
        u[:, 16 * g, 16 * g, 0] = 1.0
        u[:, 16 * g, 16 * g + 1, 1] = 1.0
        for k in range(8): u[:, 16 * ((g + k) % 8), 16 * g + 2 + k, 2] = 1.0
    u[:, 0, 15, 3] = 1.0
    u[e[2], 0, 15, 3] = -1.0
    keep = np.ones((8, 16), bool)
    keep[:, 0] = False
    return {"x": x.reshape(N, 128, 4 * C), "u": u.reshape(N, 128, 512), "v": d["v"], **weights(rng, keep)}
def setup_inputs_near(rng):
    d = numbers_of(rng)
    x = d["x"].astype(np.float32).reshape(N, 8, 16, C, 4)
    digits = lambda a: ((a[..., None] >> np.arange(4)) & 1) * np.exp2(np.arange(4) - 23.0)
    o = rng.permutation(N)
    n = rng.integers(0, 16, (N, 8, 3, C))
    far = []
    for r in range(N):
        if o[r] % 2 == 0:
            j, g = int(rng.integers(C)), int(rng.integers(5))
            n[r, :, 0, j] = 0
            n[r, g, 0, j] = 15
            n[r, g, 1, j] = 0
            far.append((r, j))
    have = n[:, :, 0] > n[:, :, 1]
    kind = np.where(have[:, 7], np.where(have[:, 6], 2, 1), 0)
    s = digits(2 * (7 - np.count_nonzero(have[:, :7], axis=1)) + rng.integers(0, 2, (N, C)))
    x[:, :, 8:] = 0
    x[:, 5:, :8] = 0
    x[:, :, 8:11] = digits(n)
    x[:, :, 11, :, 0] = 2.0 ** -10
    x[:, 7, 0, :, 0] = 1.0
    for k in range(2):
        x[:, k, 12] = s * (kind == k)[:, :, None]
        x[:, k, 13, :, 0] = (kind == k) * 2.0 ** -10
        x[:, 7 - k, 1, :, 0] = kind == k
    x[:, 5, 1, :, 0] = np.where(kind == 2, -(1.0 + 0.125 * rng.integers(0, 3, (N, C))) * 2.0 ** -30, 0.0)
    for r, j in far: x[r, 7, 1, j, 0] = 2.0 ** 30
    u = d["u"].reshape(N, 128, 128, 4)
    u[:, :, DECIDE] = 0.0
    for r in range(N):
        k = 2.0 ** -30 if o[r] < N // 2 else 1.0
        for g in range(8):
            for i in range(10):
                h = 16 * g + i
                u[r, 112, h, 0] = k
                u[r, 16 * g + 11, h, 0] = k
                u[r, 16 * g + 8 + i if i < 2 else 16 * ((g + i - 2) % 8) + 10, h] = k
    for p, k in ((113, 1.0), (13, 1.0), (97, 2.0 ** -30), (29, 2.0 ** -30), (81, 2.0 ** -30)): u[:, p, 15, 0] = k
    u[:, 12, 15] = 1.0
    u[:, 28, 15] = 2.0 ** -30
    keep = np.zeros((8, 16), bool)
    keep[:5, :8] = True
    return {"x": x.reshape(N, 128, 4 * C).astype(BF), "u": u.reshape(N, 128, 512), "v": d["v"], **weights(rng, keep)}
def setup_inputs_huge(rng):
    d = numbers_of(rng)
    c = rng.integers(0, 2, (N, 1, 1, C, 1)) * 2.0 - 1.0
    x = (0.9 + 0.05 * rng.random((N, 8, 16, C, 4))) * 2.0 ** 30 * c
    u = d["u"].reshape(N, 128, 128, 4)
    u[:, :, DECIDE] = 0.0
    for r in range(N):
        for h in DECIDE[:-1]: u[r, rng.permutation(128)[:64], h] = 2.0 ** 30
        u[r, :, 112] = 0.0
        u[r, :, 15] = (2.0 ** 30 * (1.0 - 0.03 * rng.random((128, 4)))).astype(np.float32).astype(BF)
    w = np.zeros((128, 4, 128, 4), np.float32)
    i = np.arange(128)
    for b in range(4): w[i, b, i, b] = -0.5
    return {"x": x.astype(np.float32).reshape(N, 128, 4 * C).astype(BF), "u": u.reshape(N, 128, 512), "v": d["v"], **same(rng, w.reshape(128, 2048).astype(BF))}
def setup_inputs_few(rng):
    d = numbers_of(rng)
    e = rng.permutation(N)
    x = d["x"].reshape(N, 8, 16, C, 4)
    k = (1.0 + (2 * rng.integers(0, 64, (N, 8, 8, C, 4)) + 1) * 2.0 ** -7) * np.exp2(-rng.integers(8, 15, (N, 8, 8, C, 4)).astype(np.float32))
    x[:, :, 8:] = (k * rng.choice([-1.0, 1.0], (N, 8, 8, C, 4))).astype(np.float32).astype(BF)
    x[:, :, 8, :, 0] = 1.96875
    have = rng.random((N, 8, C)) < 0.5
    have[e[0]] = True
    have[e[1]] = False
    have[e[2]] = np.arange(8)[:, None] == rng.integers(0, 7, C)
    j = int(rng.integers(C))
    have[e[3], 0, j] = False
    have[e[3], 1:, j] = True
    have[:, 7] = False
    x[:, :, 0, :, 0] = np.where(have, 1.0, -1.0).astype(np.float32).astype(BF)
    x[e[3], 0, 2, :, 0] = np.where(have[e[3], 0], -1.0, 1.0).astype(np.float32).astype(BF)
    s = rng.integers(-8, 9, (N, C))
    s[e[0]] = 64 + 8 * rng.integers(0, 8, C)
    s[e[0], C - 1] = 128
    x[:, 0, 1, :, 0] = s.astype(np.float32).astype(BF)
    u = d["u"].reshape(N, 128, 128, 4)
    u[:, :, ::16] = 0.0
    u[:, :, 1::16] = 0.0
    u[:, :, 15] = 0.0
    for h in range(0, 128, 16): u[:, h, h, 0] = 1.0
    u[:, 1, 15, 0] = 1.0
    u[e[3], 112, 112, 0] = 0.0
    u[e[3], 2, 112, 0] = 1.0
    u[e[3], :, 9] = 0.0
    w = f(rng, 128, 2048).astype(np.float32).reshape(8, 16, 4, 8, 16, 4)
    w[:, :, :, :, 8:] = 0
    i = np.arange(8)
    for p in range(8, 16):
        for b in range(4): w[i, p, b, i, p, b] = 32.0
    w[:, 8, 0, :, 8, 0] = 0
    w[:, :, 0, 0, 2] = 0
    w[0, 0, 0, 0, 2, 0] = -64.0
    w[:, :, 0, 7, 0] = 0
    return {"x": x.reshape(N, 128, 4 * C), "u": u.reshape(N, 128, 512), "v": d["v"], **same(rng, w.reshape(128, 2048).astype(BF))}
def setup_inputs_spread(rng):
    d = setup_inputs(rng)
    d["x"] = wide(rng, N, 128, 4 * C, cols=6)
    return d
def check_inputs(d):
    b = []
    for k in ("x", "u", "v"):
        a = np.abs(d[k].astype(np.float32))
        if not (np.isfinite(a).all() and ((a == 0) | (a >= 2.0 ** -30) & (a <= 2.0 ** 30)).all()): b.append("a value of " + k)
    if ((d["wc"] & 0x7F) == 0x7F).any(): b.append("a code of wc that is no number")
    for k in ("wc", "ws"):
        if (d[k] != d[k][:1]).any(): b.append(k + " isn't the same on all ranks")
    none, least, most = [emit(mx_ref.quantize(np.full((128, 16), k, np.float32).astype(BF)))[1][0, 0] for k in (0.0, 2.0 ** -30, 2.0 ** 30)]
    for r in range(N):
        a = mx_ref.live(d["ws"][r])
        if not ((a == none) | (a >= least) & (a <= most)).all(): b.append("a scale of ws")
    return b
def reference(x, u, v, wc, ws):
    qu = [mx_ref.quantize(u[r]) for r in range(N)]
    lay = pk(wc[0], ws[0])
    now = [x[r] for r in range(N)]
    for t in range(R):
        q = [mx_ref.quantize(now[r]) for r in range(N)]
        best, rep = np.zeros((N, 256), np.float32), np.zeros((N, 256), np.int64)
        here, want = np.zeros((N, 8, C), bool), np.zeros((N, 8, C), np.int64)
        for r in range(N):
            s = mx_ref.matmul(qu[r], q[r]) + np.float32(0.0)
            a = s.reshape(8, 16, C)
            here[r] = a[:, 0] > a[:, 1]
            m = bits(here[r])
            want[r] = (m & bits(a[:, 2:10] > a[:, 1:2])) | ONE
            holds = (m & SETS[:, None]) == SETS[:, None]
            strong = np.where(holds, s[15], np.float32(-np.inf))
            rep[r] = np.argmax(strong, axis=1)
            best[r] = np.max(strong, axis=1)
        win = np.argmax(best, axis=0)
        got = pick(join(*q), np.where(np.isfinite(best[win, SETS]), C * win + rep[win, SETS], -1))
        made = tile([mx_ref.matmul(pick(lay, np.arange(128 * b, 128 * b + 128)), got) * np.float32(0.03125) for b in range(4)])
        table = decode(mx_ref.quantize(made)).astype(BF)
        for r in range(N):
            now[r] = (now[r].astype(np.float32) + gcols(table, np.where(here[r], -1, want[r])).astype(np.float32)).astype(BF)
    y, wl = np.zeros((N, 128, C), np.float32), np.zeros((N, 8, C), np.float32)
    oc, osc = np.zeros((N, 128, 4 * C), np.uint8), np.zeros((N, 16, C), np.uint8)
    for r in range(N):
        q = mx_ref.quantize(now[r])
        y[r] = mx_ref.matmul(mx_ref.quantize(v[r]), q)
        wl[r] = want[r]
        oc[r], osc[r] = emit(q)
    return {"y": y, "wl": wl, "oc": oc, "osc": osc}

@@ -1,0 +1,484 @@
+from concourse.bass import DstId, RemoteDMATransfer
+from concourse.mybir import dt, AluOpType, AxisListType, ActivationFunctionType
+
+F8, U8, U16, I32, F32, BF = "float8_e4m3fn_x4", "uint8", "uint16", "int32", "float32", "bfloat16"
+ROUNDS, COLS = 2, 448
+CUT, TAIL = 256, 320
+SMALL, NONE, LEAST = 2.0 ** -42, -2.0 ** 29, -2.0 ** 34
+SCRATCH = {}
+
+
+def buf(name, n, dtype, where="sbuf"):
+    SCRATCH[name] = (where, [128, n], dtype)
+
+
+for _k in range(3):
+    buf("xt%d" % _k, 1800, BF)
+    buf("x%d_q" % _k, 450, F8)
+    buf("x%d_s" % _k, 450, U8)
+for _k in range(2):
+    for _n, _w in (("c", 192), ("l", 256), ("t", 128), ("h", 128), ("z", 192)):
+        buf("%s%d_q" % (_n, _k), _w, F8)
+        buf("%s%d_s" % (_n, _k), _w, U8)
+    buf("wst%d" % _k, 16, F32)
+    buf("lst%d" % _k, 16, F32)
+    buf("mk%d" % _k, 456, F32)
+    buf("ru%d" % _k, 456, F32)
+    buf("jk%d" % _k, 448, BF)
+for _n, _w in (("u", 128), ("v", 128), ("up", 256), ("w", 512), ("f", CUT), ("i", 128), ("a", 128),
+               ("kh", 512), ("kx", 128), ("kb", 256), ("ko", 128), ("ke", 512), ("kw", 512)):
+    buf(_n + "_q", _w, F8)
+    buf(_n + "_s", _w, U8)
+for _n, _w in (("ut", 512), ("vt", 512), ("ft", 4 * CUT), ("id", 128), ("km", 128), ("vv", 512), ("hh", 512), ("yy", 1040),
+               ("ww", 448), ("an", 512), ("kh", 2048), ("kx", 512), ("kb", 1024), ("ko", 512), ("ke", 2048),
+               ("jb", 128), ("jq", 512), ("r16", 256), ("bt", 128)):
+    buf(_n, _w, BF)
+for _n, _w in (("bc", 448), ("sb", 456), ("ix", 2), ("xb", 16), ("gm", 256), ("gs", 256), ("sel", 8), ("mx8", 8), ("gg", 8),
+               ("f4", 4), ("e4", 4), ("o4", 4), ("yo", 448), ("wlb", 448), ("cf", 32), ("lm", 256), ("kp", 256), ("b8", 8),
+               ("ib8", 8), ("mk8", 8), ("tab", 112)):
+    buf(_n, _w, F32)
+for _n, _w in (("ci", 8), ("ij", 128), ("ijt", 128), ("iju", 128), ("iu", 16)):
+    buf(_n, _w, I32)
+for _n, _w in (("ou", 16), ("oz", 4), ("of1", 16), ("oft", 4), ("ofx", 112)):
+    buf(_n, _w, U16)
+PSUM = ["b%d" % _k for _k in range(8)]
+for _n in PSUM:
+    buf(_n, 512, F32, "psum")
+SEMAPHORES = (["v", "a", "t", "gp", "sent", "stored", "dx0", "dx1", "du", "dv", "dwc", "dws"]
+              + ["%s%d" % (n, k) for n in ("lc", "lp", "lt", "hc", "hp") for k in range(2)])
+
+
+def rank_program(g, core, T, topo):
+    r = T.rank_of(core)
+    if r is None:
+        return
+    A, ACT = AluOpType, ActivationFunctionType
+    queues = {"v": g.vector, "a": g.scalar, "t": g.tensor, "g": g, "s": g.sync}
+    own_sem = {"v": "v", "a": "a", "t": "t", "g": "gp"}
+    total, know, snap, acc = {}, {q: {} for q in queues}, {}, {}
+
+    def R(name, lo=0, hi=None, step=1):
+        return (name, lo, SCRATCH[name][1][1] if hi is None else hi, step)
+
+    def V(x):
+        return T[x[0]][:, x[1]:x[2]] if x[3] == 1 else T[x[0]][:, x[1]:x[2]:x[3]]
+
+    def hit(p, q):
+        if max(p[1], q[1]) >= min(p[2], q[2]):
+            return False
+        return p[3] != q[3] or (p[1] - q[1]) % p[3] == 0
+
+    def wait(q, tok):
+        sem, val = tok
+        if know[q].get(sem, 0) >= val:
+            return
+        queues[q].wait_ge(T.sem[sem], val)
+        for s, x in list(snap.get(tok, {}).items()) + [tok]:
+            know[q][s] = max(know[q].get(s, 0), x)
+
+    def deps(q, lane, reads, writes):
+        need = set()
+        for reg, isw in [(x, False) for x in reads] + [(x, True) for x in writes]:
+            for old, oldw, oldlane, tok in acc.get(reg[0], []):
+                if reg[0] in PSUM:
+                    if oldlane == lane:
+                        continue
+                elif not (isw or oldw) or not hit(old, reg):
+                    continue
+                need.add(tok)
+        for tok in sorted(need, key=lambda x: -x[1]):
+            wait(q, tok)
+
+    def note(lane, tok, reads, writes):
+        for reg, isw in [(x, False) for x in reads] + [(x, True) for x in writes]:
+            acc.setdefault(reg[0], []).append((reg, isw, lane, tok))
+
+    def op(q, fn, writes, reads):
+        deps(q, q, reads, writes)
+        s = own_sem[q]
+        total[s] = total.get(s, 0) + 1
+        tok = (s, total[s])
+        fn().then_inc(T.sem[s], 1)
+        snap[tok] = dict(know[q])
+        note(q, tok, reads, writes)
+
+    def dma(q, sem, out, in_, writes, reads):
+        deps(q, "dma", reads, writes)
+        total[sem] = total.get(sem, 0) + 16
+        queues[q].dma_start(out, in_).then_inc(T.sem[sem], 16)
+        tok = (sem, total[sem])
+        snap[tok] = dict(know[q])
+        note("dma", tok, reads, writes)
+
+    def memset(o, c):
+        op("v", lambda: g.vector.memset(V(o), c), [o], [])
+
+    def copy(o, i):
+        op("v", lambda: g.vector.tensor_copy(V(o), V(i)), [o], [i])
+
+    def tt(o, i, j, f):
+        op("v", lambda: g.vector.tensor_tensor(V(o), V(i), V(j), f), [o], [i, j])
+
+    def ts(o, i, s1, f1, s2=None, f2=None):
+        v = lambda s: V(s) if isinstance(s, tuple) else s
+        rd = [i] + [s for s in (s1, s2) if isinstance(s, tuple)]
+        if f2 is None:
+            op("v", lambda: g.vector.tensor_scalar(V(o), V(i), v(s1), None, f1), [o], rd)
+        else:
+            op("v", lambda: g.vector.tensor_scalar(V(o), V(i), v(s1), v(s2), f1, f2), [o], rd)
+
+    def red(o, i):
+        op("v", lambda: g.vector.tensor_reduce(V(o), V(i), AxisListType.X, A.add), [o], [i])
+
+    def scan(o, i, j, init, f1, f2):
+        op("v", lambda: g.vector.tensor_tensor_scan(V(o), V(i), V(j), init, f1, f2), [o], [i, j])
+
+    def act(o, i, scale=1.0, bias=0.0):
+        op("a", lambda: g.scalar.activation(V(o), V(i), ACT.Copy, bias=bias, scale=scale), [o], [i])
+
+    def iota(o, pattern, base, ch):
+        if SCRATCH[o[0]][2] == I32:
+            op("g", lambda: g.iota(V(o), pattern, base, ch), [o], [])
+        else:
+            op("g", lambda: g.iota(V(o), pattern, base, ch, allow_small_or_imprecise_dtypes=True), [o], [])
+
+    def quant(m, lo, hi, i):
+        q, s = R(m + "_q", lo, hi), R(m + "_s", lo, hi)
+        op("v", lambda: g.vector.quantize_mx(V(q), V(s), V(i)), [q, s], [i])
+
+    def mm(bank, w, wlo, m, mlo, n):
+        o = R(bank, 0, n)
+        i = [R(w + "_q", wlo, wlo + 128), R(w + "_s", wlo, wlo + 128), R(m + "_q", mlo, mlo + n), R(m + "_s", mlo, mlo + n)]
+        op("t", lambda: g.tensor.matmul_mx(V(o), V(i[0]), V(i[1]), V(i[2]), V(i[3]), True, True), [o], i)
+
+    def pick_codes(o, lo, hi, w, wide, f):
+        q, wq = R(o + "_q", lo, hi), R(w + "_q", 0, wide)
+        op("v", lambda: g.vector.tensor_copy(V(q).bitcast(dt.uint32), V(wq).bitcast(dt.uint32).indirect(V(f))), [q], [wq, f])
+
+    def pick_scales(o, lo, hi, w, wide, f):
+        s, wp = R(o + "_s", lo, hi), R(w + "_s", 0, wide)
+        op("a", lambda: g.scalar.activation(V(s), V(wp).indirect(V(f)), ACT.Copy), [s], [wp, f])
+
+    def pick(*a):
+        pick_codes(*a)
+        pick_scales(*a)
+
+    def cf(k):
+        return R("cf", k, k + 1)
+
+    def tab(k, n=8):
+        return R("tab", k, k + n)
+
+    others = [r ^ d for d in (1, 2, 3)]
+    eng = topo.engines(core, T.cores[others[0]])
+    bits = lambda es: sum(1 << e for e in es)
+    half, quarter = len(eng) // 2, len(eng) // 4
+    one, two = eng[:half], eng[half:]
+    cut = lambda es: [es[:quarter], es[quarter:]]
+    split = [[one] + cut(two), [cut(one)[0], two, cut(one)[1]], cut(one) + [two]]
+
+    def dest(o):
+        rid, pid, _ = topo.addr(T.cores[o])
+        return DstId(rid=rid, pnc=pid)
+
+    def view(x, codes):
+        return V(x).bitcast(dt.uint8) if codes else V(x)
+
+    def scatter(kind, src, dst, sem):
+        deps("g", "rem", [src(o) for o in others], [])
+        g.remote_dma_fused([RemoteDMATransfer(dst_ids=[dest(o)], dma_engine_mask=bits(split[kind][d]), remote_sem=T.sem[sem],
+                                              src=view(src(o), kind == 0), dst=view(dst, kind == 0))
+                            for d, o in enumerate(others)], local_sem=T.sem.sent)
+        total["sent"] = total.get("sent", 0) + len(eng)
+
+    def spread(codes, src, dst, sem):
+        deps("g", "rem", [src], [])
+        g.remote_dma_fused([RemoteDMATransfer(dst_ids=[dest(o) for o in others], dma_engine_mask=bits(eng), remote_sem=T.sem[sem],
+                                              srcs=[view(src, codes)], dsts=[view(dst(o), codes) for o in others])],
+                           local_sem=T.sem.sent)
+        total["sent"] = total.get("sent", 0) + len(eng)
+
+    STRONG = [0, 8, 4, 12]
+    for k in range(ROUNDS):
+        for sem, val, regs in (("lc%d", len(eng), [R("l%d_q" % k, 64 * o, 64 * o + 64) for o in others]),
+                               ("lp%d", len(eng), [R("l%d_s" % k, 64 * o, 64 * o + 64) for o in others]),
+                               ("lt%d", len(eng), [R("lst%d" % k, STRONG[o], STRONG[o] + 4) for o in others]),
+                               ("hc%d", 3 * len(eng), [R("z%d_q" % k)]),
+                               ("hp%d", 3 * len(eng), [R("z%d_s" % k)])):
+            total[sem % k] = val
+            note("rem", (sem % k, val), [], regs)
+
+    dma("s", "dx0", T.xt0[:, 0:4 * CUT], T.x[:, 0:4 * CUT], [R("xt0", 0, 4 * CUT)], [])
+    dma("a", "du", V(R("ut")), T.u[:, :], [R("ut")], [])
+    dma("s", "dx1", T.xt0[:, 4 * CUT:1792], T.x[:, 4 * CUT:1792], [R("xt0", 4 * CUT, 1792)], [])
+    wait("s", ("dx1", 16))
+    dma("s", "dwc", V(R("w_q")).bitcast(dt.uint8), T.wc[:, :], [R("w_q")], [])
+    dma("s", "dws", V(R("w_s")), T.ws[:, :], [R("w_s")], [])
+    dma("s", "dv", V(R("vt")), T.v[:, :], [R("vt")], [])
+
+    P, LANE, GRP, B4, IPW, HSC, C112, PWS, S1, S2, WG0, WG1, PLB, NZ, CAB, LM2, GRP4 = [cf(k) for k in range(17)]
+    iota(R("ci", 0, 1), [[0, 1]], 0, 1)
+    iota(P, [[0, 1]], 0, 1)
+    iota(R("jb"), [[1, 128]], 0, 0)
+    iota(R("iu", 0, 8), [[16, 8]], 1, 0)
+    iota(R("iu", 8, 16), [[0, 8]], 15, 0)
+    iota(R("ij"), [[-64, 2], [1, 64]] if r & 1 else [[64, 2], [1, 64]], 64 * (r & 1), 0)
+    iota(R("ft"), [[0, 4 * CUT]], 0, 0)
+    iota(R("r16"), [[0, 16], [1, 16]], 0, 0)
+    iota(R("ib8"), [[128, 2], [16, 4]], 0, 0)
+    iota(R("vv"), [[0, 512]], 0, 0)
+    iota(R("kb"), [[0, 1024]], 0, 0)
+
+    memset(R("kh", 0, 512), 0.0)
+    act(R("xt0", 1792, 1800), R("kh", 0, 8))
+    act(R("kh", 512, 1024), R("kh", 0, 512))
+    act(R("kh", 1024, 2048), R("kh", 0, 1024))
+    ts(R("ci", 2, 3), R("ci", 0, 1), 4, A.arith_shift_right)
+    memset(tab(80), 0.5)
+    copy(GRP, R("ci", 2, 3))
+    memset(tab(0, 16), 2.0)
+    memset(tab(16, 16), 0.0)
+    scan(tab(96), tab(80), tab(80), 256.0, A.mult, A.max)
+    scan(tab(32, 16), tab(0, 16), tab(16, 16), 0.5, A.mult, A.add)
+    ts(R("mk8"), R("jb", 0, 8), GRP, A.is_equal)
+    ts(LANE, GRP, -16.0, A.mult, P, A.add)
+    tt(tab(80), R("mk8"), tab(96), A.mult)
+    ts(HSC, LANE, 0.0, A.is_equal, -2.0 ** 23, A.mult)
+    red(IPW, tab(80))
+    ts(C112, P, 112.0, A.is_equal, -2.0 ** 30, A.mult)
+    ts(LM2, LANE, 2.0, A.subtract)
+    ts(CAB, LANE, 0.0, A.not_equal, 100.0, A.mult)
+    tt(NZ, LM2, GRP, A.not_equal)
+    ts(CAB, CAB, GRP, A.add, 2.0, A.add)
+    ts(R("ijt"), R("ij"), IPW, A.mult)
+    ts(R("iju"), R("ijt"), 128, A.bitwise_and)
+    copy(R("ou"), R("iu"))
+    ts(R("bt"), R("iju"), HSC, A.mult)
+    for h in range(2):
+        for e in range(2):
+            o = R("kh", 1024 * h + 513 * e, 1024 * h + 512 * e + 512, 4)
+            if h ^ r >> 1:
+                ts(o, R("bt"), C112, A.min)
+            else:
+                act(o, R("bt"))
+    quant("u", 0, 128, R("ut"))
+    pick("up", 0, 256, "u", 128, R("ou"))
+
+    def const_index():
+        ts(R("km"), R("r16", 0, 128), LANE, A.is_equal)
+        for e in range(4):
+            act(R("kx", e, 512, 4), R("km"))
+        for e in range(2):
+            act(R("lm", 128 * e, 128 * e + 128), R("km"))
+        op("a", lambda: g.scalar.activation(V(R("kp")), V(R("r16")), ACT.Sign), [R("kp")], [R("r16")])
+        for k in range(2):
+            memset(R("mk%d" % k, 448, 456), NONE)
+        memset(R("sb", 448, 456), NONE)
+
+    def const_flags():
+        memset(R("oz"), COLS)
+        memset(R("an", 448, 512), 0.0)
+        for e in range(2):
+            ts(R("kb", 512 * e + e, 512 * e + 512, 4), R("r16", 0, 128), CAB, A.is_equal)
+        quant("kb", 0, 256, R("kb"))
+
+    def diagonal():
+        for b in range(4):
+            act(R("ke", 512 * b + b, 512 * b + 512, 4), R("id"))
+
+    def const_weights():
+        copy(B4, R("ci", 3, 4))
+        pw = tab(32)
+        if r:
+            pw = tab(104)
+            copy(pw, tab(32))
+        copy(tab(64, 16), tab(32, 16))
+        for k in range(2):
+            if r >> k & 1:
+                ts(tab(72 + k, 1), tab(40 + k, 1), -1.0, A.mult)
+                ts(tab(110 + k, 1), tab(38 + k, 1), -1.0, A.mult)
+        memset(tab(64, 1), 2048.0)
+        tt(tab(96), R("mk8"), pw, A.mult)
+        tt(tab(0, 16), tab(80, 16), tab(64, 16), A.mult)
+        red(PWS, tab(96))
+        red(WG0, tab(0, 16))
+
+    def const_lists():
+        ts(S1, PWS, 4.0, A.mult, 256.0 * r, A.add)
+        tt(WG0, WG0, NZ, A.mult)
+        tt(S1, S1, B4, A.add)
+        ts(S2, B4, 1024.0, A.add)
+        ts(GRP4, GRP, 4.0, A.mult)
+        for e in range(4):
+            ts(R("ko", e, 512, 4), R("jq", 128 * e, 128 * e + 128), GRP4, A.is_equal, WG0, A.mult)
+        quant("ko", 0, 128, R("ko"))
+
+    def const_wl():
+        tt(tab(0, 16), tab(80, 16), tab(32, 16), A.mult)
+        ts(tab(96), R("jb", 0, 8), P, A.is_equal)
+        ts(NZ, LANE, 0.0, A.not_equal, NZ, A.mult)
+        red(WG1, tab(0, 16))
+        tt(tab(96), tab(96), tab(32), A.mult)
+        ts(WG1, WG1, NZ, A.mult, 0.25, A.mult)
+        red(PLB, tab(96))
+        ts(R("id"), R("jb"), GRP, A.is_equal, WG1, A.mult)
+        diagonal()
+
+    chunks = ((0, CUT), (CUT, COLS))
+    ends = ((0, TAIL), (TAIL, COLS))
+
+    def quant_state(k, c):
+        lo, hi = (ends if k == ROUNDS else chunks)[c]
+        hi += 2 * c
+        quant("x%d" % k, lo, hi, R("xt%d" % k, 4 * lo, 4 * hi))
+
+    for c in range(2):
+        quant_state(0, c)
+    quant("kh", 0, 512, R("kh"))
+
+    for k in range(ROUNDS):
+        X, state = "x%d" % k, "xt%d" % k
+        C, L, TT, H, Z = ["%s%d" % (n, k) for n in "clthz"]
+        W, S = "wst%d" % k, "lst%d" % k
+        last = k == ROUNDS - 1
+
+        def spread_strengths(c):
+            (lo, hi), bank = chunks[c], ("b4", "b7")[c]
+            mm(bank, "up", 128, X, lo, hi - lo)
+            act(R("sb", lo, hi), R(bank, 0, hi - lo), SMALL)
+
+        for c, (lo, hi) in enumerate(chunks):
+            mm("b%d" % (2 * c), "up", 0, X, lo, hi - lo)
+            mm("b%d" % (2 * c + 1), "u", 0, X, lo, hi - lo)
+            act(R("bc", lo, hi), R("b%d" % (2 * c), 0, hi - lo))
+            if k:
+                spread_strengths(c)
+        if k == 0:
+            for c in range(2):
+                spread_strengths(c)
+        for c, (lo, hi) in enumerate(chunks):
+            n = hi - lo
+            tt(R("ft", c, c + 4 * n - 3, 4), R("b%d" % (2 * c + 1), 0, n), R("bc", lo, hi), A.is_le)
+        quant("f", 0, CUT, R("ft"))
+        banks = [["b5", "b6"], ["b7", "b0"]]
+        for h in range(2):
+            for c, (lo, hi) in enumerate(chunks):
+                mm(banks[h][c], "kh", 128 * (2 * h + c), "f", 0, hi - lo)
+        if k == 0:
+            const_index()
+        for h in range(2):
+            m, u = "mk%d" % h, "ru%d" % h
+            for c, (lo, hi) in enumerate(chunks):
+                tt(R(m, lo, hi), R(banks[h][c], 0, hi - lo), R("sb", lo, hi), A.add)
+            scan(R(u, 0, 449), R(m, 0, 449), R(m, 0, 449), LEAST, A.max, A.max)
+            i, j = R("ix", h, h + 1), R("jk%d" % h)
+            op("a", lambda: g.scalar.activation(V(j), V(R(u, 0, COLS)), ACT.Sign, bias=V(R(u, COLS, COLS + 1)), scale=-1.0,
+                                                accum_out=V(i)), [j, i], [R(u, 0, 449)])
+        if k == 0:
+            quant("kx", 0, 128, R("kx"))
+            ts(R("b8"), R("ib8"), LANE, A.add, 0.015625, A.mult)
+        for h in range(2):
+            ts(R("xb", 8 * h, 8 * h + 8), R("mk8"), R("ix", h, h + 1), A.mult)
+        ts(R("vv", 0, 64, 4), R("xb"), 402653184.0, A.add, -402653184.0, A.add)
+        tt(R("vv", 1, 64, 4), R("xb"), R("vv", 0, 64, 4), A.subtract)
+        quant("i", 0, 128, R("vv"))
+        mm("b1", "kx", 0, "i", 0, 128)
+        if k == 0:
+            ts(R("ci", 3, 4), R("ci", 0, 1), 3, A.bitwise_and)
+            ts(tab(80, 16), R("r16", 0, 16), LANE, A.is_equal)
+            memset(tab(42, 6), 0.0)
+        copy(R("of1"), R("b1", 0, 16))
+        place = lambda o, n: n * (r ^ o)
+        pick_scales(C, 0, 192, X, 450, R("of1", 4, 16))
+        pick_codes(C, 0, 192, X, 450, R("of1", 4, 16))
+        op("v", lambda: g.vector.tensor_tensor(V(R("gm")), V(R("sb", 0, 450)).indirect(V(R("of1"))), V(R("lm")), A.mult),
+           [R("gm")], [R("sb", 0, 450), R("of1"), R("lm")])
+        scan(R("gs"), R("kp"), R("gm"), 0.0, A.mult, A.add)
+        copy(R(W), R("gs", 15, 256, 16))
+        scatter(0, lambda o: R(C + "_q", place(o, 64) - 64, place(o, 64)), R(L + "_q", 64 * r, 64 * r + 64), "lc%d" % k)
+        scatter(1, lambda o: R(W, place(o, 4), place(o, 4) + 4), R(S, STRONG[r], STRONG[r] + 4), "lt%d" % k)
+        scatter(2, lambda o: R(C + "_s", place(o, 64) - 64, place(o, 64)), R(L + "_s", 64 * r, 64 * r + 64), "lp%d" % k)
+        if k == 0:
+            iota(R("ke", 0, 1024), [[0, 1024]], 0, 0)
+            iota(R("jq"), [[-1, 4], [1, 32], [0, 4]], 0, 0)
+        pick(L, 64 * r, 64 * r + 64, X, 450, R("of1", 0, 4))
+        copy(R(S, STRONG[r], STRONG[r] + 4), R(W, 0, 4))
+        for c, (lo, hi) in enumerate(chunks):
+            act(R("ww", lo, hi), R("ft", c, c + 4 * (hi - lo) - 3, 4), -1.0, 1.0)
+        if k == 0:
+            act(R("ke", 1024, 2048), R("kh", 0, 1024), 0.0)
+            ts(R("id"), R("jb"), P, A.is_equal)
+            const_flags()
+        pick(TT, 64, 128, X, 450, R("oz"))
+        for c, (lo, hi) in enumerate(chunks):
+            mm("b%d" % (2 + c), "kb", 128 * c, "f", 0, hi - lo)
+            tt(R("an", lo, hi), R("ww", lo, hi), R("b%d" % (2 + c), 0, hi - lo), A.is_gt)
+        quant("a", 0, 128, R("an"))
+        if k == 0:
+            memset(R("hh", 256, 512), 0.0)
+            memset(R("yy", 1024, 1040), 0.0)
+        if last:
+            quant("v", 0, 128, R("vt"))
+            const_wl()
+        tt(R("sel"), R(S, 8, 16), R(S, 0, 8), A.is_gt)
+        tt(R("mx8"), R(S, 8, 16), R(S, 0, 8), A.max)
+        tt(R("gg"), R("sel"), R("b8"), A.add)
+        tt(R("f4"), R("mx8", 4, 8), R("mx8", 0, 4), A.is_gt)
+        tt(R("e4"), R("f4"), R("gg", 4, 8), A.mult)
+        tt(R("o4"), R("e4"), R("gg", 0, 4), A.max)
+        ts(R("oft"), R("o4"), 64.0, A.mult)
+        pick(TT, 0, 64, L, 256, R("oft"))
+        hb = ["b5", "b6", "b7", "b0"]
+        for b in range(4):
+            mm(hb[b], "w", 128 * b, TT, 0, 128)
+            o, i = R("hh", b, 256, 4), R(hb[b], 0, 64)
+            if b % 2:
+                ts(o, i, 0.03125, A.mult)
+            else:
+                act(o, i, 0.03125)
+        quant(H, 0, 128, R("hh"))
+        slot = lambda o: 64 * ((r ^ o) - 1)
+        spread(True, R(H + "_q", 0, 64), lambda o: R(Z + "_q", slot(o), slot(o) + 64), "hc%d" % k)
+        spread(False, R(H + "_s", 0, 64), lambda o: R(Z + "_s", slot(o), slot(o) + 64), "hp%d" % k)
+        if k == 0:
+            diagonal()
+            const_weights()
+            quant("ke", 0, 512, R("ke"))
+        memset(R("xt%d" % (k + 1), 1792, 1800), 0.0)
+        ob = ["b1", "b2", "b3", "b4"]
+        for b in range(4):
+            mm(ob[b], "ke", 128 * b, H, 0, 128)
+            act(R("yy", b, 256, 4), R(ob[b], 0, 64))
+        if k == 0:
+            const_lists()
+        mm("b4", "ko", 0, "a", 0, 128)
+        ts(R("ofx"), R("b4", 0, 112), S1, A.add, S2, A.min)
+        if last:
+            quant("kw", 0, 512, R("ke"))
+            for b in range(4):
+                mm(ob[b], "kw", 128 * b, "a", 0, 128)
+                o, i = R("wlb", b, COLS, 4), R(ob[b], 0, 112)
+                op("a", lambda: g.scalar.activation(V(o), V(i), ACT.Identity, bias=V(PLB)), [o], [i, PLB])
+            dma("s", "stored", T.wl[:, :], T.wlb[0:8, 0:COLS], [], [R("wlb")])
+        for b in range(4):
+            mm(hb[b], "ke", 128 * b, Z, 0, 192)
+            o, i = R("yy", 256 + b, 1024, 4), R(hb[b], 0, 192)
+            if b % 2:
+                copy(o, i)
+            else:
+                act(o, i)
+        for c, (lo, hi) in enumerate(ends if last else chunks):
+            o, i, f = R("xt%d" % (k + 1), 4 * lo, 4 * hi), R(state, 4 * lo, 4 * hi), R("ofx", lo // 4, hi // 4)
+            op("v", lambda: g.vector.tensor_tensor(V(o), V(R("yy")).indirect(V(f)), V(i), A.add), [o], [R("yy"), f, i])
+            quant_state(k + 1, c)
+
+    for c, (lo, hi) in enumerate(ends):
+        dma("s", "stored", T.oc[:, 4 * lo:4 * hi], V(R("x2_q", lo, hi)).bitcast(dt.uint8), [], [R("x2_q", lo, hi)])
+        mm("b%d" % c, "v", 0, "x2", lo, hi - lo)
+        act(R("yo", lo, hi), R("b%d" % c, 0, hi - lo))
+        if c:
+            for q in range(4):
+                dma("s", "stored", T.osc[4 * q:4 * q + 4, :], T.x2_s[32 * q:32 * q + 4, 0:COLS], [], [R("x2_s", 0, COLS)])
+        dma("s", "stored", T.y[:, lo:hi], V(R("yo", lo, hi)), [], [R("yo", lo, hi)])
+    for s in sorted(total):
+        wait("g", (s, total[s]))

@@ -4,6 +4,7 @@ from concourse.mybir import dt, AluOpType, AxisListType, ActivationFunctionType
 F8, U8, U16, I32, F32, BF = "float8_e4m3fn_x4", "uint8", "uint16", "int32", "float32", "bfloat16"
 ROUNDS, COLS = 2, 448
 CUT, TAIL = 256, 320
+PLANE = 464
 SMALL, NONE, LEAST = 2.0 ** -42, -2.0 ** 29, -2.0 ** 34
 SCRATCH = {}
 
@@ -17,35 +18,33 @@ for _k in range(3):
     buf("x%d_q" % _k, 450, F8)
     buf("x%d_s" % _k, 450, U8)
 for _k in range(2):
-    for _n, _w in (("c", 192), ("l", 256), ("t", 128), ("h", 128), ("z", 192)):
-        buf("%s%d_q" % (_n, _k), _w, F8)
-        buf("%s%d_s" % (_n, _k), _w, U8)
-    buf("wst%d" % _k, 16, F32)
-    buf("lst%d" % _k, 16, F32)
+    buf("z%d_q" % _k, 512, F8)
+    buf("z%d_s" % _k, 512, U8)
+    buf("lst%d" % _k, 32, F32)
     buf("mk%d" % _k, 456, F32)
     buf("ru%d" % _k, 456, F32)
     buf("jk%d" % _k, 448, BF)
-for _n, _w in (("u", 128), ("v", 128), ("up", 256), ("w", 512), ("f", CUT), ("i", 128), ("a", 128),
-               ("kh", 512), ("kx", 128), ("kb", 256), ("ko", 128), ("ke", 512), ("kw", 512)):
+for _n, _w in (("u", 128), ("v", 128), ("up", 256), ("w", 512), ("f", CUT), ("i", 136), ("a", 128),
+               ("kh", 512), ("kx", 256), ("kb", 256), ("ko", 128), ("ke", 512), ("kw", 512)):
     buf(_n + "_q", _w, F8)
     buf(_n + "_s", _w, U8)
-for _n, _w in (("ut", 512), ("vt", 512), ("ft", 4 * CUT), ("id", 128), ("km", 128), ("vv", 512), ("hh", 512), ("yy", 1040),
-               ("ww", 448), ("an", 512), ("kh", 2048), ("kx", 512), ("kb", 1024), ("ko", 512), ("ke", 2048),
-               ("jb", 128), ("jq", 512), ("r16", 256), ("bt", 128)):
+for _n, _w in (("ut", 512), ("vt", 512), ("ft", 4 * CUT), ("id", 128), ("vv", 544), ("hp", 4 * PLANE), ("hh", 512),
+               ("yp", 2048), ("yy", 528), ("ww", 448), ("an", 512), ("kh", 2048), ("kx", 1024), ("kb", 1024), ("ko", 512),
+               ("ke", 2048), ("jb", 256), ("jq", 512), ("r16", 128), ("rq", 128), ("cc", 32)):
     buf(_n, _w, BF)
-for _n, _w in (("bc", 448), ("sb", 456), ("ix", 2), ("xb", 16), ("gm", 256), ("gs", 256), ("sel", 8), ("mx8", 8), ("gg", 8),
-               ("f4", 4), ("e4", 4), ("o4", 4), ("yo", 448), ("wlb", 448), ("cf", 32), ("lm", 256), ("kp", 256), ("b8", 8),
-               ("ib8", 8), ("mk8", 8), ("tab", 112)):
+for _n, _w in (("bc", 448), ("sb", 456), ("ix", 2), ("xb", 32), ("gm", 128), ("gs", 128), ("sel", 16), ("mx", 16), ("gg", 16),
+               ("f8", 8), ("e8", 8), ("o8", 8), ("yo", 448), ("wlb", 448), ("cf", 32), ("lm", 128), ("kp", 128), ("b16", 16),
+               ("ib", 16), ("m32", 32), ("tab", 112)):
     buf(_n, _w, F32)
-for _n, _w in (("ci", 8), ("ij", 128), ("ijt", 128), ("iju", 128), ("iu", 16)):
+for _n, _w in (("ci", 8), ("ijt", 256), ("iju", 256), ("iu", 16)):
     buf(_n, _w, I32)
-for _n, _w in (("ou", 16), ("oz", 4), ("of1", 16), ("oft", 4), ("ofx", 112)):
+for _n, _w in (("ou", 16), ("of1", 8), ("oft", 8), ("ofx", 112)):
     buf(_n, _w, U16)
 PSUM = ["b%d" % _k for _k in range(8)]
 for _n in PSUM:
     buf(_n, 512, F32, "psum")
-SEMAPHORES = (["v", "a", "t", "gp", "sent", "stored", "dx0", "dx1", "du", "dv", "dwc", "dws"]
-              + ["%s%d" % (n, k) for n in ("lc", "lp", "lt", "hc", "hp") for k in range(2)])
+SEMAPHORES = (["v", "a", "t", "gp", "sent", "stored", "dx0", "dx1", "du", "dv", "dw0", "dw1", "dws", "dk0", "dk1"]
+              + ["%s%d" % (n, k) for n in ("lp", "lt", "la", "lb", "lc") for k in range(2)])
 
 
 def rank_program(g, core, T, topo):
@@ -127,14 +126,20 @@ def rank_program(g, core, T, topo):
         else:
             op("v", lambda: g.vector.tensor_scalar(V(o), V(i), v(s1), v(s2), f1, f2), [o], rd)
 
-    def red(o, i):
-        op("v", lambda: g.vector.tensor_reduce(V(o), V(i), AxisListType.X, A.add), [o], [i])
+    def red(o, i, f):
+        op("v", lambda: g.vector.tensor_reduce(V(o), V(i), AxisListType.X, f), [o], [i])
 
     def scan(o, i, j, init, f1, f2):
         op("v", lambda: g.vector.tensor_tensor_scan(V(o), V(i), V(j), init, f1, f2), [o], [i, j])
 
     def act(o, i, scale=1.0, bias=0.0):
         op("a", lambda: g.scalar.activation(V(o), V(i), ACT.Copy, bias=bias, scale=scale), [o], [i])
+
+    def gather(q, o, w, f):
+        if q == "v":
+            op("v", lambda: g.vector.tensor_copy(V(o), V(w).indirect(V(f))), [o], [w, f])
+        else:
+            op("a", lambda: g.scalar.activation(V(o), V(w).indirect(V(f)), ACT.Copy), [o], [w, f])
 
     def iota(o, pattern, base, ch):
         if SCRATCH[o[0]][2] == I32:
@@ -146,22 +151,15 @@ def rank_program(g, core, T, topo):
         q, s = R(m + "_q", lo, hi), R(m + "_s", lo, hi)
         op("v", lambda: g.vector.quantize_mx(V(q), V(s), V(i)), [q, s], [i])
 
-    def mm(bank, w, wlo, m, mlo, n):
+    def mm(bank, w, wlo, m, mlo, n, start=True, stop=True):
         o = R(bank, 0, n)
         i = [R(w + "_q", wlo, wlo + 128), R(w + "_s", wlo, wlo + 128), R(m + "_q", mlo, mlo + n), R(m + "_s", mlo, mlo + n)]
-        op("t", lambda: g.tensor.matmul_mx(V(o), V(i[0]), V(i[1]), V(i[2]), V(i[3]), True, True), [o], i)
+        op("t", lambda: g.tensor.matmul_mx(V(o), V(i[0]), V(i[1]), V(i[2]), V(i[3]), start, stop), [o], i)
 
-    def pick_codes(o, lo, hi, w, wide, f):
+    def pick(o, lo, hi, w, wide, f):
         q, wq = R(o + "_q", lo, hi), R(w + "_q", 0, wide)
         op("v", lambda: g.vector.tensor_copy(V(q).bitcast(dt.uint32), V(wq).bitcast(dt.uint32).indirect(V(f))), [q], [wq, f])
-
-    def pick_scales(o, lo, hi, w, wide, f):
-        s, wp = R(o + "_s", lo, hi), R(w + "_s", 0, wide)
-        op("a", lambda: g.scalar.activation(V(s), V(wp).indirect(V(f)), ACT.Copy), [s], [wp, f])
-
-    def pick(*a):
-        pick_codes(*a)
-        pick_scales(*a)
+        gather("a", R(o + "_s", lo, hi), R(w + "_s", 0, wide), f)
 
     def cf(k):
         return R("cf", k, k + 1)
@@ -171,115 +169,103 @@ def rank_program(g, core, T, topo):
 
     others = [r ^ d for d in (1, 2, 3)]
     eng = topo.engines(core, T.cores[others[0]])
-    bits = lambda es: sum(1 << e for e in es)
-    half, quarter = len(eng) // 2, len(eng) // 4
-    one, two = eng[:half], eng[half:]
-    cut = lambda es: [es[:quarter], es[quarter:]]
-    split = [[one] + cut(two), [cut(one)[0], two, cut(one)[1]], cut(one) + [two]]
 
-    def dest(o):
-        rid, pid, _ = topo.addr(T.cores[o])
-        return DstId(rid=rid, pnc=pid)
-
-    def view(x, codes):
-        return V(x).bitcast(dt.uint8) if codes else V(x)
-
-    def scatter(kind, src, dst, sem):
-        deps("g", "rem", [src(o) for o in others], [])
-        g.remote_dma_fused([RemoteDMATransfer(dst_ids=[dest(o)], dma_engine_mask=bits(split[kind][d]), remote_sem=T.sem[sem],
-                                              src=view(src(o), kind == 0), dst=view(dst, kind == 0))
-                            for d, o in enumerate(others)], local_sem=T.sem.sent)
+    def send(piece, codes, to, sem):
+        deps("g", "rem", [piece], [])
+        view = V(piece).bitcast(dt.uint8) if codes else V(piece)
+        ids = [DstId(rid=topo.addr(T.cores[o])[0], pnc=topo.addr(T.cores[o])[1]) for o in to]
+        g.remote_dma_fused([RemoteDMATransfer(dst_ids=ids, dma_engine_mask=sum(1 << e for e in eng), remote_sem=T.sem[sem],
+                                              srcs=[view], dsts=[view for o in to])], local_sem=T.sem.sent)
         total["sent"] = total.get("sent", 0) + len(eng)
 
-    def spread(codes, src, dst, sem):
-        deps("g", "rem", [src], [])
-        g.remote_dma_fused([RemoteDMATransfer(dst_ids=[dest(o) for o in others], dma_engine_mask=bits(eng), remote_sem=T.sem[sem],
-                                              srcs=[view(src, codes)], dsts=[view(dst(o), codes) for o in others])],
-                           local_sem=T.sem.sent)
-        total["sent"] = total.get("sent", 0) + len(eng)
-
-    STRONG = [0, 8, 4, 12]
+    STRONG = [0, 16, 8, 24]
     for k in range(ROUNDS):
-        for sem, val, regs in (("lc%d", len(eng), [R("l%d_q" % k, 64 * o, 64 * o + 64) for o in others]),
-                               ("lp%d", len(eng), [R("l%d_s" % k, 64 * o, 64 * o + 64) for o in others]),
-                               ("lt%d", len(eng), [R("lst%d" % k, STRONG[o], STRONG[o] + 4) for o in others]),
-                               ("hc%d", 3 * len(eng), [R("z%d_q" % k)]),
-                               ("hp%d", 3 * len(eng), [R("z%d_s" % k)])):
-            total[sem % k] = val
-            note("rem", (sem % k, val), [], regs)
+        lands = [("lp%d", 3, [R("z%d_s" % k, 128 * o, 128 * o + 128) for o in others]),
+                 ("lt%d", 3, [R("lst%d" % k, STRONG[o], STRONG[o] + 8) for o in others])]
+        lands += [(s, 1, [R("z%d_q" % k, 128 * o, 128 * o + 128)]) for s, o in zip(("la%d", "lb%d", "lc%d"), others)]
+        for sem, n, regs in lands:
+            total[sem % k] = n * len(eng)
+            note("rem", (sem % k, n * len(eng)), [], regs)
 
     dma("s", "dx0", T.xt0[:, 0:4 * CUT], T.x[:, 0:4 * CUT], [R("xt0", 0, 4 * CUT)], [])
     dma("a", "du", V(R("ut")), T.u[:, :], [R("ut")], [])
     dma("s", "dx1", T.xt0[:, 4 * CUT:1792], T.x[:, 4 * CUT:1792], [R("xt0", 4 * CUT, 1792)], [])
-    wait("s", ("dx1", 16))
-    dma("s", "dwc", V(R("w_q")).bitcast(dt.uint8), T.wc[:, :], [R("w_q")], [])
+    wait("s", ("dx0", 16))
     dma("s", "dws", V(R("w_s")), T.ws[:, :], [R("w_s")], [])
+    for e in range(2):
+        o = R("w_q", 256 * e, 256 * e + 256)
+        dma("s", "dw%d" % e, V(o).bitcast(dt.uint8), T.wc[:, 1024 * e:1024 * e + 1024], [o], [])
+    wait("s", ("dw1", 16))
     dma("s", "dv", V(R("vt")), T.v[:, :], [R("vt")], [])
 
-    P, LANE, GRP, B4, IPW, HSC, C112, PWS, S1, S2, WG0, WG1, PLB, NZ, CAB, LM2, GRP4 = [cf(k) for k in range(17)]
-    iota(R("ci", 0, 1), [[0, 1]], 0, 1)
+    (P, LANE, P31, P120, P96, P7, G16, B4, IPW, IS, GRP, GRP4, S2, WG0, WG1, PLB, NZ, CAB, LM2, ISB, F1, F2) = [cf(k) for k in range(22)]
     iota(P, [[0, 1]], 0, 1)
-    iota(R("jb"), [[1, 128]], 0, 0)
+    iota(R("jb"), [[1, 256]], 0, 0)
     iota(R("iu", 0, 8), [[16, 8]], 1, 0)
     iota(R("iu", 8, 16), [[0, 8]], 15, 0)
-    iota(R("ij"), [[-64, 2], [1, 64]] if r & 1 else [[64, 2], [1, 64]], 64 * (r & 1), 0)
+    iota(R("ci", 0, 1), [[0, 1]], 0, 1)
     iota(R("ft"), [[0, 4 * CUT]], 0, 0)
-    iota(R("r16"), [[0, 16], [1, 16]], 0, 0)
-    iota(R("ib8"), [[128, 2], [16, 4]], 0, 0)
-    iota(R("vv"), [[0, 512]], 0, 0)
+    for grp in range(8):
+        b, f = (grp, 1) if grp < 5 else (grp - 3, 8)
+        iota(R("rq", 16 * grp, 16 * grp + 16), [[f << b + 1, 16 >> b], [f, 1 << b]], f << b, 0)
+    iota(R("cc", 0, 16), [[-128, 2], [32, 8]], 0, 0)
+    iota(R("cc", 16, 32), [[0, 2], [1, 8]], 0, 0)
+    iota(R("r16"), [[0, 8], [1, 16]], 0, 0)
     iota(R("kb"), [[0, 1024]], 0, 0)
+    iota(R("vv", 64, 544), [[0, 480]], 0, 0)
+    iota(R("ib"), [[256, 2], [16, 8]], 0, 0)
+    for e in range(2):
+        dma("s", "dk%d" % e, V(R("ke", 1024 * e, 1024 * e + 1024)), V(R("kb")), [R("ke", 1024 * e, 1024 * e + 1024)], [R("kb")])
 
-    memset(R("kh", 0, 512), 0.0)
-    act(R("xt0", 1792, 1800), R("kh", 0, 8))
-    act(R("kh", 512, 1024), R("kh", 0, 512))
+    memset(R("kh", 0, 1024), 0.0)
     act(R("kh", 1024, 2048), R("kh", 0, 1024))
-    ts(R("ci", 2, 3), R("ci", 0, 1), 4, A.arith_shift_right)
-    memset(tab(80), 0.5)
-    copy(GRP, R("ci", 2, 3))
-    memset(tab(0, 16), 2.0)
-    memset(tab(16, 16), 0.0)
-    scan(tab(96), tab(80), tab(80), 256.0, A.mult, A.max)
-    scan(tab(32, 16), tab(0, 16), tab(16, 16), 0.5, A.mult, A.add)
-    ts(R("mk8"), R("jb", 0, 8), GRP, A.is_equal)
-    ts(LANE, GRP, -16.0, A.mult, P, A.add)
-    tt(tab(80), R("mk8"), tab(96), A.mult)
-    ts(HSC, LANE, 0.0, A.is_equal, -2.0 ** 23, A.mult)
-    red(IPW, tab(80))
-    ts(C112, P, 112.0, A.is_equal, -2.0 ** 30, A.mult)
-    ts(LM2, LANE, 2.0, A.subtract)
-    ts(CAB, LANE, 0.0, A.not_equal, 100.0, A.mult)
-    tt(NZ, LM2, GRP, A.not_equal)
-    ts(CAB, CAB, GRP, A.add, 2.0, A.add)
-    ts(R("ijt"), R("ij"), IPW, A.mult)
-    ts(R("iju"), R("ijt"), 128, A.bitwise_and)
+    act(R("kx", 0, 512), R("kh", 1024, 1536))
+    memset(R("xt0", 1792, 1800), 0.0)
+    for k in range(2):
+        memset(R("mk%d" % k, 448, 456), NONE)
+    ts(tab(0, 7), R("jb", 16, 128, 16), P, A.is_gt, 0.5, A.max)
+    ts(tab(8), R("jb", 0, 128, 16), P, A.is_equal, 128.0, A.mult)
+    red(IPW, tab(0, 7), A.mult)
+    red(IS, tab(8), A.max)
+    memset(R("sb", 448, 456), NONE)
+    ts(R("ijt"), R("jb"), IPW, A.mult, IS, A.mult)
     copy(R("ou"), R("iu"))
-    ts(R("bt"), R("iju"), HSC, A.mult)
-    for h in range(2):
-        for e in range(2):
-            o = R("kh", 1024 * h + 513 * e, 1024 * h + 512 * e + 512, 4)
-            if h ^ r >> 1:
-                ts(o, R("bt"), C112, A.min)
-            else:
-                act(o, R("bt"))
+    ts(R("iju"), R("ijt"), 128, A.bitwise_and)
     quant("u", 0, 128, R("ut"))
     pick("up", 0, 256, "u", 128, R("ou"))
+    ts(R("kh", 0, 1024, 4), R("iju"), -2.0 ** 23, A.mult)
+    act(R("kh", 1025, 2048, 4), R("kh", 0, 1024, 4))
 
-    def const_index():
-        ts(R("km"), R("r16", 0, 128), LANE, A.is_equal)
+    def const_lanes():
+        for k, bits in enumerate((15, 31, 120, 96, 7, 112, 3)):
+            ts(R("ci", k + 1, k + 2), R("ci", 0, 1), bits, A.bitwise_and)
+        copy(R("cf", 1, 8), R("ci", 1, 8))
+
+    def const_index(h):
+        if h == 0:
+            for e in range(2):
+                ts(R("kx", e, 320, 4), R("rq", 0, 80), P31, A.is_equal)
+            act(R("kx", 512, 1024), R("kx", 0, 512))
+            return
         for e in range(4):
-            act(R("kx", e, 512, 4), R("km"))
-        for e in range(2):
-            act(R("lm", 128 * e, 128 * e + 128), R("km"))
-        op("a", lambda: g.scalar.activation(V(R("kp")), V(R("r16")), ACT.Sign), [R("kp")], [R("r16")])
-        for k in range(2):
-            memset(R("mk%d" % k, 448, 456), NONE)
-        memset(R("sb", 448, 456), NONE)
+            lo = 512 * (e // 2)
+            ts(R("kx", lo + 322 + e % 2, lo + 512, 4), R("rq", 80, 128), 128.0 * (e // 2), A.subtract, P120, A.is_equal)
+
+    def const_columns():
+        ts(R("m32", 0, 32, 2), R("cc", 0, 16), P96, A.is_equal)
+        ts(R("m32", 1, 32, 2), R("cc", 16, 32), P7, A.is_equal)
+
+    def const_masks():
+        ts(R("lm"), R("r16"), LANE, A.is_equal)
+        ts(R("kp"), R("r16"), 1.0, A.min)
 
     def const_flags():
-        memset(R("oz"), COLS)
+        ts(GRP, G16, 0.0625, A.mult)
+        ts(CAB, LANE, 0.0, A.not_equal, 100.0, A.mult)
         memset(R("an", 448, 512), 0.0)
+        ts(CAB, CAB, GRP, A.add, 2.0, A.add)
         for e in range(2):
-            ts(R("kb", 512 * e + e, 512 * e + 512, 4), R("r16", 0, 128), CAB, A.is_equal)
+            ts(R("kb", 512 * e + e, 512 * e + 512, 4), R("r16"), CAB, A.is_equal)
         quant("kb", 0, 256, R("kb"))
 
     def diagonal():
@@ -287,41 +273,39 @@ def rank_program(g, core, T, topo):
             act(R("ke", 512 * b + b, 512 * b + 512, 4), R("id"))
 
     def const_weights():
-        copy(B4, R("ci", 3, 4))
-        pw = tab(32)
-        if r:
-            pw = tab(104)
-            copy(pw, tab(32))
+        memset(tab(0, 16), 2.0)
+        memset(tab(16, 16), 0.0)
+        ts(tab(80, 16), R("r16", 0, 16), LANE, A.is_equal)
+        scan(tab(32, 16), tab(0, 16), tab(16, 16), 0.5, A.mult, A.add)
+        ts(LM2, LANE, 2.0, A.subtract)
+        ts(ISB, P, 80.0, A.is_ge)
+        memset(tab(42, 6), 0.0)
+        ts(F2, LANE, 5.0, A.is_lt, 15.875, A.mult)
         copy(tab(64, 16), tab(32, 16))
-        for k in range(2):
-            if r >> k & 1:
-                ts(tab(72 + k, 1), tab(40 + k, 1), -1.0, A.mult)
-                ts(tab(110 + k, 1), tab(38 + k, 1), -1.0, A.mult)
-        memset(tab(64, 1), 2048.0)
-        tt(tab(96), R("mk8"), pw, A.mult)
+        ts(F1, LM2, GRP, A.is_gt, 0.5, A.mult)
+        memset(tab(64, 1), 512.0)
+        ts(F2, F2, 0.875, A.subtract, ISB, A.mult)
         tt(tab(0, 16), tab(80, 16), tab(64, 16), A.mult)
-        red(PWS, tab(96))
-        red(WG0, tab(0, 16))
-
-    def const_lists():
-        ts(S1, PWS, 4.0, A.mult, 256.0 * r, A.add)
-        tt(WG0, WG0, NZ, A.mult)
-        tt(S1, S1, B4, A.add)
-        ts(S2, B4, 1024.0, A.add)
+        ts(F1, LM2, GRP, A.is_lt, F1, A.add)
+        red(WG0, tab(0, 16), A.add)
+        ts(F1, F2, 1.0, A.add, F1, A.mult)
+        ts(S2, B4, 512.0, A.add)
         ts(GRP4, GRP, 4.0, A.mult)
+        tt(WG0, WG0, F1, A.mult)
         for e in range(4):
             ts(R("ko", e, 512, 4), R("jq", 128 * e, 128 * e + 128), GRP4, A.is_equal, WG0, A.mult)
         quant("ko", 0, 128, R("ko"))
 
     def const_wl():
+        tt(NZ, LM2, GRP, A.not_equal)
         tt(tab(0, 16), tab(80, 16), tab(32, 16), A.mult)
         ts(tab(96), R("jb", 0, 8), P, A.is_equal)
         ts(NZ, LANE, 0.0, A.not_equal, NZ, A.mult)
-        red(WG1, tab(0, 16))
+        red(WG1, tab(0, 16), A.add)
         tt(tab(96), tab(96), tab(32), A.mult)
         ts(WG1, WG1, NZ, A.mult, 0.25, A.mult)
-        red(PLB, tab(96))
-        ts(R("id"), R("jb"), GRP, A.is_equal, WG1, A.mult)
+        red(PLB, tab(96), A.add)
+        ts(R("id"), R("jb", 0, 128), GRP, A.is_equal, WG1, A.mult)
         diagonal()
 
     chunks = ((0, CUT), (CUT, COLS))
@@ -332,18 +316,23 @@ def rank_program(g, core, T, topo):
         hi += 2 * c
         quant("x%d" % k, lo, hi, R("xt%d" % k, 4 * lo, 4 * hi))
 
-    for c in range(2):
-        quant_state(0, c)
-    quant("kh", 0, 512, R("kh"))
+    quant_state(0, 0)
+    quant("kh", 0, 256, R("kh", 0, 1024))
+    quant_state(0, 1)
+    quant("kh", 256, 512, R("kh", 1024, 2048))
+    const_lanes()
 
     for k in range(ROUNDS):
-        X, state = "x%d" % k, "xt%d" % k
-        C, L, TT, H, Z = ["%s%d" % (n, k) for n in "clthz"]
-        W, S = "wst%d" % k, "lst%d" % k
+        X, state, Z, S = "x%d" % k, "xt%d" % k, "z%d" % k, "lst%d" % k
         last = k == ROUNDS - 1
 
-        def spread_strengths(c):
-            (lo, hi), bank = chunks[c], ("b4", "b7")[c]
+        def layer(b, bank, lo, hi):
+            mm(bank, "w", 128 * b, X, lo, hi - lo)
+
+        def scaled(b, bank, lo, hi):
+            act(R("hp", PLANE * b + lo, PLANE * b + hi), R(bank, 0, hi - lo), 0.03125)
+
+        def strengths(bank, lo, hi):
             mm(bank, "up", 128, X, lo, hi - lo)
             act(R("sb", lo, hi), R(bank, 0, hi - lo), SMALL)
 
@@ -352,121 +341,118 @@ def rank_program(g, core, T, topo):
             mm("b%d" % (2 * c + 1), "u", 0, X, lo, hi - lo)
             act(R("bc", lo, hi), R("b%d" % (2 * c), 0, hi - lo))
             if k:
-                spread_strengths(c)
+                strengths(("b4", "b7")[c], lo, hi)
+                for b in range(2):
+                    layer(b, "b%d" % (5 + b), lo, hi + 2 * c)
+                    scaled(b, "b%d" % (5 + b), lo, hi + 2 * c)
         if k == 0:
-            for c in range(2):
-                spread_strengths(c)
+            strengths("b4", 0, COLS)
         for c, (lo, hi) in enumerate(chunks):
             n = hi - lo
             tt(R("ft", c, c + 4 * n - 3, 4), R("b%d" % (2 * c + 1), 0, n), R("bc", lo, hi), A.is_le)
         quant("f", 0, CUT, R("ft"))
-        banks = [["b5", "b6"], ["b7", "b0"]]
+        banks = [["b0", "b2"], ["b4", "b7"]]
         for h in range(2):
             for c, (lo, hi) in enumerate(chunks):
-                mm(banks[h][c], "kh", 128 * (2 * h + c), "f", 0, hi - lo)
+                mm(banks[h][c], "kh", 128 * (2 * c + h), "f", 0, hi - lo)
         if k == 0:
-            const_index()
+            const_index(0)
+            for b in range(2):
+                layer(b, "b%d" % (5 + b), 0, 450)
+                scaled(b, "b%d" % (5 + b), 0, 450)
+        layer(2, "b1", 0, 450)
+        layer(3, "b3", 0, 450)
+        if k:
+            scaled(2, "b1", 0, 450)
         for h in range(2):
             m, u = "mk%d" % h, "ru%d" % h
             for c, (lo, hi) in enumerate(chunks):
                 tt(R(m, lo, hi), R(banks[h][c], 0, hi - lo), R("sb", lo, hi), A.add)
             scan(R(u, 0, 449), R(m, 0, 449), R(m, 0, 449), LEAST, A.max, A.max)
+            if k == 0 and h == 1:
+                const_index(1)
             i, j = R("ix", h, h + 1), R("jk%d" % h)
             op("a", lambda: g.scalar.activation(V(j), V(R(u, 0, COLS)), ACT.Sign, bias=V(R(u, COLS, COLS + 1)), scale=-1.0,
                                                 accum_out=V(i)), [j, i], [R(u, 0, 449)])
         if k == 0:
-            quant("kx", 0, 128, R("kx"))
-            ts(R("b8"), R("ib8"), LANE, A.add, 0.015625, A.mult)
+            scaled(2, "b1", 0, 450)
+            quant("kx", 0, 256, R("kx"))
+            const_columns()
+        scaled(3, "b3", 0, 450)
         for h in range(2):
-            ts(R("xb", 8 * h, 8 * h + 8), R("mk8"), R("ix", h, h + 1), A.mult)
-        ts(R("vv", 0, 64, 4), R("xb"), 402653184.0, A.add, -402653184.0, A.add)
-        tt(R("vv", 1, 64, 4), R("xb"), R("vv", 0, 64, 4), A.subtract)
-        quant("i", 0, 128, R("vv"))
-        mm("b1", "kx", 0, "i", 0, 128)
+            ts(R("xb", 16 * h, 16 * h + 16), R("m32", 16 * h, 16 * h + 16), R("ix", h, h + 1), A.mult)
+        ts(R("vv", 0, 64, 2), R("xb"), 402653184.0, A.add, -402653184.0, A.add)
+        tt(R("vv", 1, 64, 2), R("xb"), R("vv", 0, 64, 2), A.subtract)
+        quant("i", 0, 136, R("vv"))
+        mm("b5", "kx", 0, "i", 0, 128, True, False)
+        mm("b5", "kx", 128, "i", 8, 128, False, True)
         if k == 0:
-            ts(R("ci", 3, 4), R("ci", 0, 1), 3, A.bitwise_and)
-            ts(tab(80, 16), R("r16", 0, 16), LANE, A.is_equal)
-            memset(tab(42, 6), 0.0)
-        copy(R("of1"), R("b1", 0, 16))
-        place = lambda o, n: n * (r ^ o)
-        pick_scales(C, 0, 192, X, 450, R("of1", 4, 16))
-        pick_codes(C, 0, 192, X, 450, R("of1", 4, 16))
+            const_masks()
+        copy(R("of1"), R("b5", 0, 8))
+        for b in (0, 3, 1, 2):
+            gather("va"[b // 2], R("hh", b, 512, 4), R("hp", PLANE * b, PLANE * b + 450), R("of1"))
+        quant(Z, 128 * r, 128 * r + 128, R("hh"))
+        mine = R(S, STRONG[r], STRONG[r] + 8)
         op("v", lambda: g.vector.tensor_tensor(V(R("gm")), V(R("sb", 0, 450)).indirect(V(R("of1"))), V(R("lm")), A.mult),
            [R("gm")], [R("sb", 0, 450), R("of1"), R("lm")])
         scan(R("gs"), R("kp"), R("gm"), 0.0, A.mult, A.add)
-        copy(R(W), R("gs", 15, 256, 16))
-        scatter(0, lambda o: R(C + "_q", place(o, 64) - 64, place(o, 64)), R(L + "_q", 64 * r, 64 * r + 64), "lc%d" % k)
-        scatter(1, lambda o: R(W, place(o, 4), place(o, 4) + 4), R(S, STRONG[r], STRONG[r] + 4), "lt%d" % k)
-        scatter(2, lambda o: R(C + "_s", place(o, 64) - 64, place(o, 64)), R(L + "_s", 64 * r, 64 * r + 64), "lp%d" % k)
+        copy(mine, R("gs", 15, 128, 16))
+        codes = R(Z + "_q", 128 * r, 128 * r + 128)
+        send(R(Z + "_s", 128 * r, 128 * r + 128), False, others, "lp%d" % k)
+        send(codes, True, others[0:1], "la%d" % k)
+        send(mine, False, others, "lt%d" % k)
+        send(codes, True, others[1:2], "lb%d" % k)
+        send(codes, True, others[2:3], "lc%d" % k)
+
+        def unpack(o, first, queue):
+            for b in range(4):
+                bank = "b%d" % (first + b)
+                mm(bank, "ke", 128 * b, Z, 128 * o, 128)
+                (copy if queue[b] == "v" else act)(R("yp", 512 * b + 128 * o, 512 * b + 128 * o + 128), R(bank, 0, 128))
+
         if k == 0:
-            iota(R("ke", 0, 1024), [[0, 1024]], 0, 0)
             iota(R("jq"), [[-1, 4], [1, 32], [0, 4]], 0, 0)
-        pick(L, 64 * r, 64 * r + 64, X, 450, R("of1", 0, 4))
-        copy(R(S, STRONG[r], STRONG[r] + 4), R(W, 0, 4))
+            ts(R("id"), R("jb", 0, 128), P, A.is_equal)
+            diagonal()
+            const_flags()
         for c, (lo, hi) in enumerate(chunks):
             act(R("ww", lo, hi), R("ft", c, c + 4 * (hi - lo) - 3, 4), -1.0, 1.0)
         if k == 0:
-            act(R("ke", 1024, 2048), R("kh", 0, 1024), 0.0)
-            ts(R("id"), R("jb"), P, A.is_equal)
-            const_flags()
-        pick(TT, 64, 128, X, 450, R("oz"))
+            quant("ke", 0, 512, R("ke"))
         for c, (lo, hi) in enumerate(chunks):
-            mm("b%d" % (2 + c), "kb", 128 * c, "f", 0, hi - lo)
-            tt(R("an", lo, hi), R("ww", lo, hi), R("b%d" % (2 + c), 0, hi - lo), A.is_gt)
+            mm("b%d" % (6 + c), "kb", 128 * c, "f", 0, hi - lo)
+            tt(R("an", lo, hi), R("ww", lo, hi), R("b%d" % (6 + c), 0, hi - lo), A.is_gt)
         quant("a", 0, 128, R("an"))
+        unpack(r, 0, "aaaa")
         if k == 0:
-            memset(R("hh", 256, 512), 0.0)
-            memset(R("yy", 1024, 1040), 0.0)
+            const_weights()
+            memset(R("yy", 512, 528), 0.0)
+            ts(R("b16"), R("ib"), LANE, A.add, 0.0078125, A.mult)
+        memset(R("xt%d" % (k + 1), 1792, 1800), 0.0)
+        mm("b4", "ko", 0, "a", 0, 128)
+        ts(R("ofx"), R("b4", 0, 112), B4, A.add, S2, A.min)
         if last:
             quant("v", 0, 128, R("vt"))
             const_wl()
-        tt(R("sel"), R(S, 8, 16), R(S, 0, 8), A.is_gt)
-        tt(R("mx8"), R(S, 8, 16), R(S, 0, 8), A.max)
-        tt(R("gg"), R("sel"), R("b8"), A.add)
-        tt(R("f4"), R("mx8", 4, 8), R("mx8", 0, 4), A.is_gt)
-        tt(R("e4"), R("f4"), R("gg", 4, 8), A.mult)
-        tt(R("o4"), R("e4"), R("gg", 0, 4), A.max)
-        ts(R("oft"), R("o4"), 64.0, A.mult)
-        pick(TT, 0, 64, L, 256, R("oft"))
-        hb = ["b5", "b6", "b7", "b0"]
-        for b in range(4):
-            mm(hb[b], "w", 128 * b, TT, 0, 128)
-            o, i = R("hh", b, 256, 4), R(hb[b], 0, 64)
-            if b % 2:
-                ts(o, i, 0.03125, A.mult)
-            else:
-                act(o, i, 0.03125)
-        quant(H, 0, 128, R("hh"))
-        slot = lambda o: 64 * ((r ^ o) - 1)
-        spread(True, R(H + "_q", 0, 64), lambda o: R(Z + "_q", slot(o), slot(o) + 64), "hc%d" % k)
-        spread(False, R(H + "_s", 0, 64), lambda o: R(Z + "_s", slot(o), slot(o) + 64), "hp%d" % k)
-        if k == 0:
-            diagonal()
-            const_weights()
-            quant("ke", 0, 512, R("ke"))
-        memset(R("xt%d" % (k + 1), 1792, 1800), 0.0)
-        ob = ["b1", "b2", "b3", "b4"]
-        for b in range(4):
-            mm(ob[b], "ke", 128 * b, H, 0, 128)
-            act(R("yy", b, 256, 4), R(ob[b], 0, 64))
-        if k == 0:
-            const_lists()
-        mm("b4", "ko", 0, "a", 0, 128)
-        ts(R("ofx"), R("b4", 0, 112), S1, A.add, S2, A.min)
-        if last:
             quant("kw", 0, 512, R("ke"))
+        unpack(others[0], 0, "aaaa")
+        tt(R("sel"), R(S, 16, 32), R(S, 0, 16), A.is_gt)
+        tt(R("mx"), R(S, 16, 32), R(S, 0, 16), A.max)
+        tt(R("gg"), R("sel"), R("b16"), A.add)
+        tt(R("f8"), R("mx", 8, 16), R("mx", 0, 8), A.is_gt)
+        tt(R("e8"), R("f8"), R("gg", 8, 16), A.mult)
+        tt(R("o8"), R("e8"), R("gg", 0, 8), A.max)
+        ts(R("oft"), R("o8"), 128.0, A.mult)
+        unpack(others[1], 4, "vava")
+        unpack(others[2], 0, "vava")
+        for b in range(4):
+            gather("va"[b % 2], R("yy", b, 512, 4), R("yp", 512 * b, 512 * b + 512), R("oft"))
+        if last:
             for b in range(4):
-                mm(ob[b], "kw", 128 * b, "a", 0, 128)
-                o, i = R("wlb", b, COLS, 4), R(ob[b], 0, 112)
+                mm("b%d" % (4 + b), "kw", 128 * b, "a", 0, 128)
+                o, i = R("wlb", b, COLS, 4), R("b%d" % (4 + b), 0, 112)
                 op("a", lambda: g.scalar.activation(V(o), V(i), ACT.Identity, bias=V(PLB)), [o], [i, PLB])
             dma("s", "stored", T.wl[:, :], T.wlb[0:8, 0:COLS], [], [R("wlb")])
-        for b in range(4):
-            mm(hb[b], "ke", 128 * b, Z, 0, 192)
-            o, i = R("yy", 256 + b, 1024, 4), R(hb[b], 0, 192)
-            if b % 2:
-                copy(o, i)
-            else:
-                act(o, i)
         for c, (lo, hi) in enumerate(ends if last else chunks):
             o, i, f = R("xt%d" % (k + 1), 4 * lo, 4 * hi), R(state, 4 * lo, 4 * hi), R("ofx", lo // 4, hi // 4)
             op("v", lambda: g.vector.tensor_tensor(V(o), V(R("yy")).indirect(V(f)), V(i), A.add), [o], [R("yy"), f, i])

@@ -4,6 +4,7 @@ from concourse.mybir import dt, AluOpType, AxisListType, ActivationFunctionType
 F8, U8, U16, I32, F32, BF = "float8_e4m3fn_x4", "uint8", "uint16", "int32", "float32", "bfloat16"
 ROUNDS, COLS = 2, 448
 CUT, TAIL = 256, 320
+DIRECT = (128, 64)
 PLANE = 464
 SMALL, NONE, LEAST = 2.0 ** -42, -2.0 ** 29, -2.0 ** 34
 SCRATCH = {}
@@ -25,31 +26,61 @@ for _k in range(2):
     buf("ru%d" % _k, 456, F32)
     buf("jk%d" % _k, 448, BF)
 for _n, _w in (("u", 128), ("v", 128), ("up", 256), ("w", 512), ("f", CUT), ("i", 136), ("a", 128),
-               ("kh", 512), ("kx", 256), ("kb", 256), ("ko", 128), ("ke", 512), ("kw", 512)):
+               ("kh", 512), ("kx", 256), ("kb", 256), ("ko", 128), ("ke", 512), ("kw", 128)):
     buf(_n + "_q", _w, F8)
     buf(_n + "_s", _w, U8)
-for _n, _w in (("ut", 512), ("vt", 512), ("ft", 4 * CUT), ("id", 128), ("vv", 544), ("hp", 4 * PLANE), ("hh", 512),
-               ("yp", 2048), ("yy", 528), ("ww", 448), ("an", 512), ("kh", 2048), ("kx", 1024), ("kb", 1024), ("ko", 512),
-               ("ke", 2048), ("jb", 256), ("jq", 512), ("r16", 128), ("rq", 128), ("cc", 32)):
+for _n, _w in (("ut", 512), ("vt", 512), ("ft", 4 * CUT), ("vv", 544), ("hp", 4 * PLANE), ("hh", 512), ("yp", 2048),
+               ("yy", 528), ("an", 512), ("kh", 1028), ("kx", 1024), ("kb", 516), ("ko", 512), ("kw", 512), ("ke", 516),
+               ("jb", 256), ("jq", 144), ("jw", 224), ("r8", 128), ("rq", 128), ("cc", 32), ("lm", 128), ("kp", 128)):
     buf(_n, _w, BF)
 for _n, _w in (("bc", 448), ("sb", 456), ("ix", 2), ("xb", 32), ("gm", 128), ("gs", 128), ("sel", 16), ("mx", 16), ("gg", 16),
-               ("f8", 8), ("e8", 8), ("o8", 8), ("yo", 448), ("wlb", 448), ("cf", 32), ("lm", 128), ("kp", 128), ("b16", 16),
-               ("ib", 16), ("m32", 32), ("tab", 112)):
+               ("f8", 8), ("e8", 8), ("o8", 8), ("yo", 448), ("wlb", 448), ("cf", 32), ("b16", 16),
+               ("ib", 16), ("m32", 32), ("tab", 32)):
     buf(_n, _w, F32)
-for _n, _w in (("ci", 8), ("ijt", 256), ("iju", 256), ("iu", 16)):
+for _n, _w in (("ci", 24), ("ijt", 256), ("iju", 256), ("iu", 16)):
     buf(_n, _w, I32)
 for _n, _w in (("ou", 16), ("of1", 8), ("oft", 8), ("ofx", 112)):
     buf(_n, _w, U16)
 PSUM = ["b%d" % _k for _k in range(8)]
 for _n in PSUM:
     buf(_n, 512, F32, "psum")
-SEMAPHORES = (["v", "a", "t", "gp", "sent", "stored", "dx0", "dx1", "du", "dv", "dw0", "dw1", "dws", "dk0", "dk1"]
-              + ["%s%d" % (n, k) for n in ("lp", "lt", "la", "lb", "lc") for k in range(2)])
+SEMAPHORES = (["v", "a", "t", "gp", "sent", "stored", "dx0", "dx1", "du", "dv", "dw0", "dw1", "dws"]
+              + ["%s%d" % (n, k) for n in ("lp", "lt", "la", "lb", "lc", "lh") for k in range(2)])
+
+
+def helper_of(core, topo):
+    return [c for c in topo.cores_of(core) if topo.die(c) != topo.die(core)][0]
+
+
+def on_chip(core, T, topo):
+    far = topo.engines(core, [c for c in T.cores if c != core][0])
+    return [e for e in topo.engines(core, helper_of(core, topo)) if e not in far]
+
+
+def remote(g, T, topo, transfers):
+    g.remote_dma_fused([RemoteDMATransfer(dst_ids=[DstId(rid=topo.addr(c)[0], pnc=topo.addr(c)[1]) for c in to],
+                                          dma_engine_mask=sum(1 << e for e in engines), remote_sem=T.sem[sem],
+                                          srcs=[view], dsts=[view for c in to]) for view, to, engines, sem in transfers],
+                       local_sem=T.sem.sent)
+
+
+def helper_program(g, core, r, T, topo):
+    eng, sent = topo.engines(core, T.cores[r ^ 2]), 0
+    for k in range(ROUNDS):
+        g.wait_ge(T.sem["lh%d" % k], len(on_chip(T.cores[r], T, topo)))
+        for d, lo, sem in ((2, 0, "lb%d"), (3, DIRECT[k], "lc%d")):
+            if lo < 128:
+                remote(g, T, topo, [(T["z%d_q" % k][:, 128 * r + lo:128 * r + 128].bitcast(dt.uint8), [T.cores[r ^ d]], eng, sem % k)])
+                sent += len(eng)
+    g.wait_ge(T.sem.sent, sent)
 
 
 def rank_program(g, core, T, topo):
     r = T.rank_of(core)
     if r is None:
+        for o, c in enumerate(T.cores):
+            if helper_of(c, topo) == core:
+                helper_program(g, core, o, T, topo)
         return
     A, ACT = AluOpType, ActivationFunctionType
     queues = {"v": g.vector, "a": g.scalar, "t": g.tensor, "g": g, "s": g.sync}
@@ -170,19 +201,20 @@ def rank_program(g, core, T, topo):
     others = [r ^ d for d in (1, 2, 3)]
     eng = topo.engines(core, T.cores[others[0]])
 
+    helper = helper_of(core, topo)
+    rest = on_chip(core, T, topo)
+
     def send(piece, codes, to, sem):
         deps("g", "rem", [piece], [])
-        view = V(piece).bitcast(dt.uint8) if codes else V(piece)
-        ids = [DstId(rid=topo.addr(T.cores[o])[0], pnc=topo.addr(T.cores[o])[1]) for o in to]
-        g.remote_dma_fused([RemoteDMATransfer(dst_ids=ids, dma_engine_mask=sum(1 << e for e in eng), remote_sem=T.sem[sem],
-                                              srcs=[view], dsts=[view for o in to])], local_sem=T.sem.sent)
+        remote(g, T, topo, [(V(piece).bitcast(dt.uint8) if codes else V(piece), [T.cores[o] for o in to], eng, sem)])
         total["sent"] = total.get("sent", 0) + len(eng)
 
     STRONG = [0, 16, 8, 24]
     for k in range(ROUNDS):
         lands = [("lp%d", 3, [R("z%d_s" % k, 128 * o, 128 * o + 128) for o in others]),
                  ("lt%d", 3, [R("lst%d" % k, STRONG[o], STRONG[o] + 8) for o in others])]
-        lands += [(s, 1, [R("z%d_q" % k, 128 * o, 128 * o + 128)]) for s, o in zip(("la%d", "lb%d", "lc%d"), others)]
+        lands += [(s, n, [R("z%d_q" % k, 128 * o, 128 * o + 128)])
+                  for s, o, n in zip(("la%d", "lb%d", "lc%d"), others, (1, 1, 1 + (DIRECT[k] < 128)))]
         for sem, n, regs in lands:
             total[sem % k] = n * len(eng)
             note("rem", (sem % k, n * len(eng)), [], regs)
@@ -198,115 +230,105 @@ def rank_program(g, core, T, topo):
     wait("s", ("dw1", 16))
     dma("s", "dv", V(R("vt")), T.v[:, :], [R("vt")], [])
 
-    (P, LANE, P31, P120, P96, P7, G16, B4, IPW, IS, GRP, GRP4, S2, WG0, WG1, PLB, NZ, CAB, LM2, ISB, F1, F2) = [cf(k) for k in range(22)]
+    LO4, L8, LO16, LO32, HI4, HI8, HI16 = [cf(k) for k in (0, 1, 3, 7, 8, 9, 11)]
+    P, B4, IPW, IS, G28, WG0, WG1, PW, NZ, CAB, ISB, F2 = [cf(k) for k in range(16, 28)]
     iota(P, [[0, 1]], 0, 1)
     iota(R("jb"), [[1, 256]], 0, 0)
     iota(R("iu", 0, 8), [[16, 8]], 1, 0)
     iota(R("iu", 8, 16), [[0, 8]], 15, 0)
-    iota(R("ci", 0, 1), [[0, 1]], 0, 1)
     iota(R("ft"), [[0, 4 * CUT]], 0, 0)
     for grp in range(8):
-        b, f = (grp, 1) if grp < 5 else (grp - 3, 8)
+        b, f = (grp, 4) if grp < 5 else (grp - 3, 128)
         iota(R("rq", 16 * grp, 16 * grp + 16), [[f << b + 1, 16 >> b], [f, 1 << b]], f << b, 0)
-    iota(R("cc", 0, 16), [[-128, 2], [32, 8]], 0, 0)
-    iota(R("cc", 16, 32), [[0, 2], [1, 8]], 0, 0)
-    iota(R("r16"), [[0, 8], [1, 16]], 0, 0)
-    iota(R("kb"), [[0, 1024]], 0, 0)
+    iota(R("cc", 0, 16), [[-512, 2], [128, 8]], 0, 0)
+    iota(R("cc", 16, 32), [[0, 2], [16, 8]], 0, 0)
+    iota(R("r8"), [[0, 8], [8, 16]], 0, 0)
+    iota(R("kb"), [[0, 516]], 0, 0)
+    op("g", lambda: g.affine_select(V(R("ke")), V(R("kb")), [[-1, 516]], A.not_equal, 1.0, 3, 4), [R("ke")], [R("kb")])
     iota(R("vv", 64, 544), [[0, 480]], 0, 0)
-    iota(R("ib"), [[256, 2], [16, 8]], 0, 0)
-    for e in range(2):
-        dma("s", "dk%d" % e, V(R("ke", 1024 * e, 1024 * e + 1024)), V(R("kb")), [R("ke", 1024 * e, 1024 * e + 1024)], [R("kb")])
+    iota(R("ib"), [[2048, 2], [128, 8]], 0, 0)
+    iota(R("jq"), [[2, 36], [0, 4]], 10, 0)
 
-    memset(R("kh", 0, 1024), 0.0)
-    act(R("kh", 1024, 2048), R("kh", 0, 1024))
-    act(R("kx", 0, 512), R("kh", 1024, 1536))
-    memset(R("xt0", 1792, 1800), 0.0)
-    for k in range(2):
-        memset(R("mk%d" % k, 448, 456), NONE)
+    def fill(o, c):
+        act(o, R("kh", 0, o[2] - o[1]), 0.0, c)
+
+    memset(R("kh"), 0.0)
+    fill(R("xt0", 1792, 1800), 0.0)
+    fill(R("kx", 0, 512), 0.0)
+    for n in ("mk0", "mk1", "sb"):
+        fill(R(n, 448, 456), NONE)
     ts(tab(0, 7), R("jb", 16, 128, 16), P, A.is_gt, 0.5, A.max)
     ts(tab(8), R("jb", 0, 128, 16), P, A.is_equal, 128.0, A.mult)
     red(IPW, tab(0, 7), A.mult)
     red(IS, tab(8), A.max)
-    memset(R("sb", 448, 456), NONE)
+    ts(R("ci", 0, 8), R("jb", 4, 33, 4), P, A.mult)
     ts(R("ijt"), R("jb"), IPW, A.mult, IS, A.mult)
     copy(R("ou"), R("iu"))
     ts(R("iju"), R("ijt"), 128, A.bitwise_and)
     quant("u", 0, 128, R("ut"))
     pick("up", 0, 256, "u", 128, R("ou"))
-    ts(R("kh", 0, 1024, 4), R("iju"), -2.0 ** 23, A.mult)
-    act(R("kh", 1025, 2048, 4), R("kh", 0, 1024, 4))
+    ts(R("kh", 1, 1025, 4), R("iju"), -2.0 ** 23, A.mult)
+    fill(R("an", 448, 512), 0.0)
+    fill(R("yy", 512, 528), 0.0)
+    for k in range(ROUNDS):
+        fill(R("xt%d" % (k + 1), 1792, 1800), 0.0)
 
     def const_lanes():
-        for k, bits in enumerate((15, 31, 120, 96, 7, 112, 3)):
-            ts(R("ci", k + 1, k + 2), R("ci", 0, 1), bits, A.bitwise_and)
-        copy(R("cf", 1, 8), R("ci", 1, 8))
+        ts(R("ci", 8, 16), R("ci", 0, 8), 127, A.bitwise_and)
+        ts(R("ci", 16, 24), R("ci", 0, 8), 3968, A.bitwise_and)
+        copy(R("cf", 0, 16), R("ci", 8, 24))
 
     def const_index(h):
         if h == 0:
             for e in range(2):
-                ts(R("kx", e, 320, 4), R("rq", 0, 80), P31, A.is_equal)
-            act(R("kx", 512, 1024), R("kx", 0, 512))
+                ts(R("kx", e, 320, 4), R("rq", 0, 80), LO4, A.is_equal)
             return
         for e in range(4):
             lo = 512 * (e // 2)
-            ts(R("kx", lo + 322 + e % 2, lo + 512, 4), R("rq", 80, 128), 128.0 * (e // 2), A.subtract, P120, A.is_equal)
+            ts(R("kx", lo + 322 + e % 2, lo + 512, 4), R("rq", 80, 128), 2048.0 * (e // 2), A.subtract, HI16, A.is_equal)
 
     def const_columns():
-        ts(R("m32", 0, 32, 2), R("cc", 0, 16), P96, A.is_equal)
-        ts(R("m32", 1, 32, 2), R("cc", 16, 32), P7, A.is_equal)
+        ts(R("m32", 0, 32, 2), R("cc", 0, 16), HI4, A.is_equal)
+        ts(R("m32", 1, 32, 2), R("cc", 16, 32), LO16, A.is_equal)
 
     def const_masks():
-        ts(R("lm"), R("r16"), LANE, A.is_equal)
-        ts(R("kp"), R("r16"), 1.0, A.min)
+        ts(R("lm"), R("r8"), L8, A.is_equal)
+        ts(R("kp"), R("r8"), 1.0, A.min)
+        ts(G28, HI8, 0.0625, A.mult, 16.0, A.add)
 
     def const_flags():
-        ts(GRP, G16, 0.0625, A.mult)
-        ts(CAB, LANE, 0.0, A.not_equal, 100.0, A.mult)
-        memset(R("an", 448, 512), 0.0)
-        ts(CAB, CAB, GRP, A.add, 2.0, A.add)
-        for e in range(2):
-            ts(R("kb", 512 * e + e, 512 * e + 512, 4), R("r16"), CAB, A.is_equal)
-        quant("kb", 0, 256, R("kb"))
-
-    def diagonal():
-        for b in range(4):
-            act(R("ke", 512 * b + b, 512 * b + 512, 4), R("id"))
+        ts(CAB, L8, 32.0, A.mult, G28, A.add)
+        for c in range(2):
+            quant("ke", 128 * c, 128 * c + 128, R("ke", 3 - c, 515 - c))
+        ts(R("kb", 1, 513, 4), R("r8"), CAB, A.is_equal)
+        for c in range(2, 4):
+            quant("ke", 128 * c, 128 * c + 128, R("ke", 3 - c, 515 - c))
+        for c in range(2):
+            quant("kb", 128 * c, 128 * c + 128, R("kb", 1 - c, 513 - c))
 
     def const_weights():
-        memset(tab(0, 16), 2.0)
-        memset(tab(16, 16), 0.0)
-        ts(tab(80, 16), R("r16", 0, 16), LANE, A.is_equal)
-        scan(tab(32, 16), tab(0, 16), tab(16, 16), 0.5, A.mult, A.add)
-        ts(LM2, LANE, 2.0, A.subtract)
         ts(ISB, P, 80.0, A.is_ge)
-        memset(tab(42, 6), 0.0)
-        ts(F2, LANE, 5.0, A.is_lt, 15.875, A.mult)
-        copy(tab(64, 16), tab(32, 16))
-        ts(F1, LM2, GRP, A.is_gt, 0.5, A.mult)
-        memset(tab(64, 1), 512.0)
-        ts(F2, F2, 0.875, A.subtract, ISB, A.mult)
-        tt(tab(0, 16), tab(80, 16), tab(64, 16), A.mult)
-        ts(F1, LM2, GRP, A.is_lt, F1, A.add)
-        red(WG0, tab(0, 16), A.add)
-        ts(F1, F2, 1.0, A.add, F1, A.mult)
-        ts(S2, B4, 512.0, A.add)
-        ts(GRP4, GRP, 4.0, A.mult)
-        tt(WG0, WG0, F1, A.mult)
+        ts(F2, L8, 40.0, A.is_lt, 15.875, A.mult)
+        ts(tab(16, 10), R("r8", 0, 10), L8, A.is_lt)
+        ts(tab(26, 1), L8, 80.0, A.is_ge, -1.0, A.mult)
+        ts(tab(27, 1), L8, G28, A.is_gt, -0.5, A.mult)
+        ts(tab(28, 1), L8, 0.0, A.is_equal, 511.0, A.mult)
+        ts(tab(29, 1), F2, 0.875, A.subtract, ISB, A.mult)
+        ts(B4, LO32, 0.03125, A.mult)
+        ts(tab(0, 14), tab(16, 14), 1.0, A.add)
+        ts(R("b16"), R("ib"), L8, A.add, 2.0 ** -10, A.mult)
+        red(WG0, tab(0, 14), A.mult)
         for e in range(4):
-            ts(R("ko", e, 512, 4), R("jq", 128 * e, 128 * e + 128), GRP4, A.is_equal, WG0, A.mult)
+            ts(R("ko", e, 512, 4), R("jq", 12 - 4 * e, 140 - 4 * e), G28, A.is_equal, WG0, A.mult)
         quant("ko", 0, 128, R("ko"))
 
     def const_wl():
-        tt(NZ, LM2, GRP, A.not_equal)
-        tt(tab(0, 16), tab(80, 16), tab(32, 16), A.mult)
-        ts(tab(96), R("jb", 0, 8), P, A.is_equal)
-        ts(NZ, LANE, 0.0, A.not_equal, NZ, A.mult)
-        red(WG1, tab(0, 16), A.add)
-        tt(tab(96), tab(96), tab(32), A.mult)
-        ts(WG1, WG1, NZ, A.mult, 0.25, A.mult)
-        red(PLB, tab(96), A.add)
-        ts(R("id"), R("jb", 0, 128), GRP, A.is_equal, WG1, A.mult)
-        diagonal()
+        red(PW, tab(0, 11), A.mult)
+        ts(NZ, L8, G28, A.not_equal, L8, A.min)
+        ts(WG1, PW, NZ, A.mult, 0.25, A.mult)
+        for e in range(4):
+            ts(R("kw", e, 512, 4), R("jw", 96 - 32 * e, 224 - 32 * e), G28, A.is_equal, WG1, A.mult)
+        quant("kw", 0, 128, R("kw"))
 
     chunks = ((0, CUT), (CUT, COLS))
     ends = ((0, TAIL), (TAIL, COLS))
@@ -317,9 +339,9 @@ def rank_program(g, core, T, topo):
         quant("x%d" % k, lo, hi, R("xt%d" % k, 4 * lo, 4 * hi))
 
     quant_state(0, 0)
-    quant("kh", 0, 256, R("kh", 0, 1024))
+    quant("kh", 0, 256, R("kh", 1, 1025))
     quant_state(0, 1)
-    quant("kh", 256, 512, R("kh", 1024, 2048))
+    quant("kh", 256, 512, R("kh", 0, 1024))
     const_lanes()
 
     for k in range(ROUNDS):
@@ -342,11 +364,13 @@ def rank_program(g, core, T, topo):
             act(R("bc", lo, hi), R("b%d" % (2 * c), 0, hi - lo))
             if k:
                 strengths(("b4", "b7")[c], lo, hi)
-                for b in range(2):
-                    layer(b, "b%d" % (5 + b), lo, hi + 2 * c)
-                    scaled(b, "b%d" % (5 + b), lo, hi + 2 * c)
+                layer(0, "b5", lo, hi + 2 * c)
+                scaled(0, "b5", lo, hi + 2 * c)
         if k == 0:
             strengths("b4", 0, COLS)
+        else:
+            layer(1, "b6", 0, 450)
+            scaled(1, "b6", 0, 450)
         for c, (lo, hi) in enumerate(chunks):
             n = hi - lo
             tt(R("ft", c, c + 4 * n - 3, 4), R("b%d" % (2 * c + 1), 0, n), R("bc", lo, hi), A.is_le)
@@ -355,10 +379,12 @@ def rank_program(g, core, T, topo):
         for h in range(2):
             for c, (lo, hi) in enumerate(chunks):
                 mm(banks[h][c], "kh", 128 * (2 * c + h), "f", 0, hi - lo)
+            if k == 0:
+                layer(h, "b%d" % (5 + h), 0, 450)
         if k == 0:
             const_index(0)
+            act(R("kx", 512, 1024), R("kx", 0, 512))
             for b in range(2):
-                layer(b, "b%d" % (5 + b), 0, 450)
                 scaled(b, "b%d" % (5 + b), 0, 450)
         layer(2, "b1", 0, 450)
         layer(3, "b3", 0, 450)
@@ -391,18 +417,20 @@ def rank_program(g, core, T, topo):
         copy(R("of1"), R("b5", 0, 8))
         for b in (0, 3, 1, 2):
             gather("va"[b // 2], R("hh", b, 512, 4), R("hp", PLANE * b, PLANE * b + 450), R("of1"))
-        quant(Z, 128 * r, 128 * r + 128, R("hh"))
         mine = R(S, STRONG[r], STRONG[r] + 8)
         op("v", lambda: g.vector.tensor_tensor(V(R("gm")), V(R("sb", 0, 450)).indirect(V(R("of1"))), V(R("lm")), A.mult),
            [R("gm")], [R("sb", 0, 450), R("of1"), R("lm")])
+        quant(Z, 128 * r, 128 * r + 128, R("hh"))
         scan(R("gs"), R("kp"), R("gm"), 0.0, A.mult, A.add)
         copy(mine, R("gs", 15, 128, 16))
         codes = R(Z + "_q", 128 * r, 128 * r + 128)
+        deps("g", "rem", [codes], [])
+        remote(g, T, topo, [(V(codes).bitcast(dt.uint8), [T.cores[others[0]]], eng, "la%d" % k),
+                            (V(codes).bitcast(dt.uint8), [helper], rest, "lh%d" % k)])
+        total["sent"] = total.get("sent", 0) + len(eng) + len(rest)
         send(R(Z + "_s", 128 * r, 128 * r + 128), False, others, "lp%d" % k)
-        send(codes, True, others[0:1], "la%d" % k)
         send(mine, False, others, "lt%d" % k)
-        send(codes, True, others[1:2], "lb%d" % k)
-        send(codes, True, others[2:3], "lc%d" % k)
+        send(R(Z + "_q", 128 * r, 128 * r + DIRECT[k]), True, others[2:3], "lc%d" % k)
 
         def unpack(o, first, queue):
             for b in range(4):
@@ -411,30 +439,29 @@ def rank_program(g, core, T, topo):
                 (copy if queue[b] == "v" else act)(R("yp", 512 * b + 128 * o, 512 * b + 128 * o + 128), R(bank, 0, 128))
 
         if k == 0:
-            iota(R("jq"), [[-1, 4], [1, 32], [0, 4]], 0, 0)
-            ts(R("id"), R("jb", 0, 128), P, A.is_equal)
-            diagonal()
+            iota(R("jw"), [[8, 224]], -752, 0)
             const_flags()
         for c, (lo, hi) in enumerate(chunks):
-            act(R("ww", lo, hi), R("ft", c, c + 4 * (hi - lo) - 3, 4), -1.0, 1.0)
-        if k == 0:
-            quant("ke", 0, 512, R("ke"))
-        for c, (lo, hi) in enumerate(chunks):
-            mm("b%d" % (6 + c), "kb", 128 * c, "f", 0, hi - lo)
-            tt(R("an", lo, hi), R("ww", lo, hi), R("b%d" % (6 + c), 0, hi - lo), A.is_gt)
-        quant("a", 0, 128, R("an"))
+            o, i = R("an", lo, hi), R("b%d" % (6 + c), 0, hi - lo)
+            mm(i[0], "kb", 128 * c, "f", 0, hi - lo, True, False)
+            mm(i[0], "ke", 128 * c, "f", 0, hi - lo, False, True)
+            op("a", lambda: g.scalar.activation(V(o), V(i), ACT.Relu, bias=1.0, scale=-1.0), [o], [i])
         unpack(r, 0, "aaaa")
         if k == 0:
             const_weights()
-            memset(R("yy", 512, 528), 0.0)
-            ts(R("b16"), R("ib"), LANE, A.add, 0.0078125, A.mult)
-        memset(R("xt%d" % (k + 1), 1792, 1800), 0.0)
-        mm("b4", "ko", 0, "a", 0, 128)
-        ts(R("ofx"), R("b4", 0, 112), B4, A.add, S2, A.min)
         if last:
             quant("v", 0, 128, R("vt"))
             const_wl()
-            quant("kw", 0, 512, R("ke"))
+        quant("a", 0, 128, R("an"))
+        mm("b4", "ko", 0, "a", 0, 128)
+        if last:
+            mm("b5", "kw", 0, "a", 0, 128)
+        ts(R("ofx"), R("b4", 0, 112), 512.0, A.min, B4, A.add)
+        if last:
+            for e in range(4):
+                op("a", lambda: g.scalar.activation(T.wlb[0:8, e:COLS:4], T.b5[32 * e:32 * e + 8, 0:112], ACT.Identity,
+                                                    bias=T.cf[32 * e:32 * e + 8, PW[1]:PW[2]]), [R("wlb", e, COLS, 4)], [R("b5"), PW])
+            dma("s", "stored", T.wl[:, :], T.wlb[0:8, 0:COLS], [], [R("wlb")])
         unpack(others[0], 0, "aaaa")
         tt(R("sel"), R(S, 16, 32), R(S, 0, 16), A.is_gt)
         tt(R("mx"), R(S, 16, 32), R(S, 0, 16), A.max)
@@ -447,12 +474,6 @@ def rank_program(g, core, T, topo):
         unpack(others[2], 0, "vava")
         for b in range(4):
             gather("va"[b % 2], R("yy", b, 512, 4), R("yp", 512 * b, 512 * b + 512), R("oft"))
-        if last:
-            for b in range(4):
-                mm("b%d" % (4 + b), "kw", 128 * b, "a", 0, 128)
-                o, i = R("wlb", b, COLS, 4), R("b%d" % (4 + b), 0, 112)
-                op("a", lambda: g.scalar.activation(V(o), V(i), ACT.Identity, bias=V(PLB)), [o], [i, PLB])
-            dma("s", "stored", T.wl[:, :], T.wlb[0:8, 0:COLS], [], [R("wlb")])
         for c, (lo, hi) in enumerate(ends if last else chunks):
             o, i, f = R("xt%d" % (k + 1), 4 * lo, 4 * hi), R(state, 4 * lo, 4 * hi), R("ofx", lo // 4, hi // 4)
             op("v", lambda: g.vector.tensor_tensor(V(o), V(R("yy")).indirect(V(f)), V(i), A.add), [o], [R("yy"), f, i])

@@ -3,8 +3,8 @@ from concourse.mybir import dt, AluOpType, AxisListType, ActivationFunctionType
 
 F8, U8, U16, I32, F32, BF = "float8_e4m3fn_x4", "uint8", "uint16", "int32", "float32", "bfloat16"
 ROUNDS, COLS = 2, 448
-CUT, TAIL = 256, 320
-DIRECT = (128, 64)
+CUT, TAIL = 256, 256
+DIRECT = ((128, 0), (128, 0))
 PLANE = 464
 SMALL, NONE, LEAST = 2.0 ** -42, -2.0 ** 29, -2.0 ** 34
 SCRATCH = {}
@@ -25,12 +25,12 @@ for _k in range(2):
     buf("mk%d" % _k, 456, F32)
     buf("ru%d" % _k, 456, F32)
     buf("jk%d" % _k, 448, BF)
-for _n, _w in (("u", 128), ("v", 128), ("up", 256), ("w", 512), ("f", CUT), ("i", 136), ("a", 128),
-               ("kh", 512), ("kx", 256), ("kb", 256), ("ko", 128), ("ke", 512), ("kw", 128)):
+for _n, _w in (("u", 128), ("v", 128), ("up", 256), ("w", 512), ("f", COLS), ("i", 136), ("a", 128),
+               ("kh", 256), ("kx", 256), ("kb", 128), ("ko", 128), ("ke", 512), ("kw", 128)):
     buf(_n + "_q", _w, F8)
     buf(_n + "_s", _w, U8)
-for _n, _w in (("ut", 512), ("vt", 512), ("ft", 4 * CUT), ("vv", 544), ("hp", 4 * PLANE), ("hh", 512), ("yp", 2048),
-               ("yy", 528), ("an", 512), ("kh", 1028), ("kx", 1024), ("kb", 516), ("ko", 512), ("kw", 512), ("ke", 516),
+for _n, _w in (("ut", 512), ("vt", 512), ("ft", 4 * COLS), ("vv", 580), ("hp", 4 * PLANE), ("hh", 512), ("yp", 2048),
+               ("yy", 528), ("gy", 4 * (COLS - CUT)), ("an", 512), ("kh", 1024), ("kx", 1024), ("kb", 512), ("ko", 512), ("kw", 512), ("ke", 516),
                ("jb", 256), ("jq", 144), ("jw", 224), ("r8", 128), ("rq", 128), ("cc", 32), ("lm", 128), ("kp", 128)):
     buf(_n, _w, BF)
 for _n, _w in (("bc", 448), ("sb", 456), ("ix", 2), ("xb", 32), ("gm", 128), ("gs", 128), ("sel", 16), ("mx", 16), ("gg", 16),
@@ -67,12 +67,14 @@ def remote(g, T, topo, transfers):
 def helper_program(g, core, r, T, topo):
     eng, sent = topo.engines(core, T.cores[r ^ 2]), 0
     for k in range(ROUNDS):
-        g.wait_ge(T.sem["lh%d" % k], len(on_chip(T.cores[r], T, topo)))
-        for d, lo, sem in ((2, 0, "lb%d"), (3, DIRECT[k], "lc%d")):
+        if min(DIRECT[k]) < 128:
+            g.wait_ge(T.sem["lh%d" % k], len(on_chip(T.cores[r], T, topo)))
+        for d, lo, sem in ((2, DIRECT[k][0], "lb%d"), (3, DIRECT[k][1], "lc%d")):
             if lo < 128:
                 remote(g, T, topo, [(T["z%d_q" % k][:, 128 * r + lo:128 * r + 128].bitcast(dt.uint8), [T.cores[r ^ d]], eng, sem % k)])
                 sent += len(eng)
-    g.wait_ge(T.sem.sent, sent)
+    if sent:
+        g.wait_ge(T.sem.sent, sent)
 
 
 def rank_program(g, core, T, topo):
@@ -214,7 +216,7 @@ def rank_program(g, core, T, topo):
         lands = [("lp%d", 3, [R("z%d_s" % k, 128 * o, 128 * o + 128) for o in others]),
                  ("lt%d", 3, [R("lst%d" % k, STRONG[o], STRONG[o] + 8) for o in others])]
         lands += [(s, n, [R("z%d_q" % k, 128 * o, 128 * o + 128)])
-                  for s, o, n in zip(("la%d", "lb%d", "lc%d"), others, (1, 1, 1 + (DIRECT[k] < 128)))]
+                  for s, o, n in zip(("la%d", "lb%d", "lc%d"), others, [1] + [1 + (0 < n < 128) for n in DIRECT[k]])]
         for sem, n, regs in lands:
             total[sem % k] = n * len(eng)
             note("rem", (sem % k, n * len(eng)), [], regs)
@@ -236,16 +238,21 @@ def rank_program(g, core, T, topo):
     iota(R("jb"), [[1, 256]], 0, 0)
     iota(R("iu", 0, 8), [[16, 8]], 1, 0)
     iota(R("iu", 8, 16), [[0, 8]], 15, 0)
-    iota(R("ft"), [[0, 4 * CUT]], 0, 0)
+    iota(R("ft", 0, 4 * CUT), [[0, 4 * CUT]], 0, 0)
     for grp in range(8):
         b, f = (grp, 4) if grp < 5 else (grp - 3, 128)
         iota(R("rq", 16 * grp, 16 * grp + 16), [[f << b + 1, 16 >> b], [f, 1 << b]], f << b, 0)
     iota(R("cc", 0, 16), [[-512, 2], [128, 8]], 0, 0)
     iota(R("cc", 16, 32), [[0, 2], [16, 8]], 0, 0)
     iota(R("r8"), [[0, 8], [8, 16]], 0, 0)
-    iota(R("kb"), [[0, 516]], 0, 0)
-    op("g", lambda: g.affine_select(V(R("ke")), V(R("kb")), [[-1, 516]], A.not_equal, 1.0, 3, 4), [R("ke")], [R("kb")])
-    iota(R("vv", 64, 544), [[0, 480]], 0, 0)
+    iota(R("vv", 64, 580), [[0, 516]], 0, 0)
+
+    def ones(o, pattern, base):
+        i = R("vv", 64, 64 + o[2])
+        op("g", lambda: g.affine_select(V(o), V(i), pattern, A.not_equal, 1.0, base, 4), [o], [i])
+
+    ones(R("ke"), [[-1, 516]], 3)
+    ones(R("kb"), [[0, 8], [-64, 16], [1, 4]], 128)
     iota(R("ib"), [[2048, 2], [128, 8]], 0, 0)
     iota(R("jq"), [[2, 36], [0, 4]], 10, 0)
 
@@ -254,9 +261,7 @@ def rank_program(g, core, T, topo):
 
     memset(R("kh"), 0.0)
     fill(R("xt0", 1792, 1800), 0.0)
-    fill(R("kx", 0, 512), 0.0)
-    for n in ("mk0", "mk1", "sb"):
-        fill(R(n, 448, 456), NONE)
+    fill(R("kx"), 0.0)
     ts(tab(0, 7), R("jb", 16, 128, 16), P, A.is_gt, 0.5, A.max)
     ts(tab(8), R("jb", 0, 128, 16), P, A.is_equal, 128.0, A.mult)
     red(IPW, tab(0, 7), A.mult)
@@ -267,11 +272,8 @@ def rank_program(g, core, T, topo):
     ts(R("iju"), R("ijt"), 128, A.bitwise_and)
     quant("u", 0, 128, R("ut"))
     pick("up", 0, 256, "u", 128, R("ou"))
-    ts(R("kh", 1, 1025, 4), R("iju"), -2.0 ** 23, A.mult)
-    fill(R("an", 448, 512), 0.0)
-    fill(R("yy", 512, 528), 0.0)
-    for k in range(ROUNDS):
-        fill(R("xt%d" % (k + 1), 1792, 1800), 0.0)
+    ts(R("kh", 0, 1024, 4), R("iju"), -2.0 ** 23, A.mult)
+    act(R("ft", 4 * CUT, 4 * COLS), R("kx", 0, 4 * (COLS - CUT)))
 
     def const_lanes():
         ts(R("ci", 8, 16), R("ci", 0, 8), 127, A.bitwise_and)
@@ -279,13 +281,10 @@ def rank_program(g, core, T, topo):
         copy(R("cf", 0, 16), R("ci", 8, 24))
 
     def const_index(h):
-        if h == 0:
-            for e in range(2):
-                ts(R("kx", e, 320, 4), R("rq", 0, 80), LO4, A.is_equal)
-            return
-        for e in range(4):
-            lo = 512 * (e // 2)
-            ts(R("kx", lo + 322 + e % 2, lo + 512, 4), R("rq", 80, 128), 2048.0 * (e // 2), A.subtract, HI16, A.is_equal)
+        lo = 512 * h
+        for e in range(2):
+            ts(R("kx", lo + e, lo + 320, 4), R("rq", 0, 80), LO4, A.is_equal)
+            ts(R("kx", lo + 322 + e, lo + 512, 4), R("rq", 80, 128), 2048.0 * h, A.subtract, HI16, A.is_equal)
 
     def const_columns():
         ts(R("m32", 0, 32, 2), R("cc", 0, 16), HI4, A.is_equal)
@@ -297,14 +296,9 @@ def rank_program(g, core, T, topo):
         ts(G28, HI8, 0.0625, A.mult, 16.0, A.add)
 
     def const_flags():
-        ts(CAB, L8, 32.0, A.mult, G28, A.add)
-        for c in range(2):
-            quant("ke", 128 * c, 128 * c + 128, R("ke", 3 - c, 515 - c))
-        ts(R("kb", 1, 513, 4), R("r8"), CAB, A.is_equal)
-        for c in range(2, 4):
-            quant("ke", 128 * c, 128 * c + 128, R("ke", 3 - c, 515 - c))
-        for c in range(2):
-            quant("kb", 128 * c, 128 * c + 128, R("kb", 1 - c, 513 - c))
+        quant("kb", 0, 128, R("kb"))
+        for b in range(4):
+            quant("ke", 128 * b, 128 * b + 128, R("ke", 3 - b, 515 - b))
 
     def const_weights():
         ts(ISB, P, 80.0, A.is_ge)
@@ -322,10 +316,12 @@ def rank_program(g, core, T, topo):
             ts(R("ko", e, 512, 4), R("jq", 12 - 4 * e, 140 - 4 * e), G28, A.is_equal, WG0, A.mult)
         quant("ko", 0, 128, R("ko"))
 
-    def const_wl():
-        red(PW, tab(0, 11), A.mult)
-        ts(NZ, L8, G28, A.not_equal, L8, A.min)
-        ts(WG1, PW, NZ, A.mult, 0.25, A.mult)
+    def const_wl(part):
+        if part == 0:
+            red(PW, tab(0, 11), A.mult)
+            ts(NZ, L8, G28, A.not_equal, L8, A.min)
+            ts(WG1, PW, NZ, A.mult, 0.25, A.mult)
+            return
         for e in range(4):
             ts(R("kw", e, 512, 4), R("jw", 96 - 32 * e, 224 - 32 * e), G28, A.is_equal, WG1, A.mult)
         quant("kw", 0, 128, R("kw"))
@@ -339,9 +335,8 @@ def rank_program(g, core, T, topo):
         quant("x%d" % k, lo, hi, R("xt%d" % k, 4 * lo, 4 * hi))
 
     quant_state(0, 0)
-    quant("kh", 0, 256, R("kh", 1, 1025))
+    quant("kh", 0, 256, R("kh"))
     quant_state(0, 1)
-    quant("kh", 256, 512, R("kh", 0, 1024))
     const_lanes()
 
     for k in range(ROUNDS):
@@ -362,58 +357,64 @@ def rank_program(g, core, T, topo):
             mm("b%d" % (2 * c), "up", 0, X, lo, hi - lo)
             mm("b%d" % (2 * c + 1), "u", 0, X, lo, hi - lo)
             act(R("bc", lo, hi), R("b%d" % (2 * c), 0, hi - lo))
-            if k:
-                strengths(("b4", "b7")[c], lo, hi)
-                layer(0, "b5", lo, hi + 2 * c)
-                scaled(0, "b5", lo, hi + 2 * c)
-        if k == 0:
-            strengths("b4", 0, COLS)
-        else:
-            layer(1, "b6", 0, 450)
-            scaled(1, "b6", 0, 450)
-        for c, (lo, hi) in enumerate(chunks):
-            n = hi - lo
-            tt(R("ft", c, c + 4 * n - 3, 4), R("b%d" % (2 * c + 1), 0, n), R("bc", lo, hi), A.is_le)
-        quant("f", 0, CUT, R("ft"))
-        banks = [["b0", "b2"], ["b4", "b7"]]
-        for h in range(2):
-            for c, (lo, hi) in enumerate(chunks):
-                mm(banks[h][c], "kh", 128 * (2 * c + h), "f", 0, hi - lo)
-            if k == 0:
-                layer(h, "b%d" % (5 + h), 0, 450)
-        if k == 0:
-            const_index(0)
-            act(R("kx", 512, 1024), R("kx", 0, 512))
+            strengths(("b4", "b7")[c], lo, hi)
+            if k and c == 0:
+                for b in range(2):
+                    layer(b, "b%d" % (5 + b), lo, hi)
+        if k:
             for b in range(2):
-                scaled(b, "b%d" % (5 + b), 0, 450)
+                scaled(b, "b%d" % (5 + b), 0, CUT)
+        else:
+            for n in ("mk0", "mk1", "sb"):
+                fill(R(n, 448, 456), NONE)
+        banks = [["b0", "b2"], ["b4", "b7"]]
+        for c, (lo, hi) in enumerate(chunks):
+            tt(R("ft", 4 * lo, 4 * hi, 4), R("b%d" % (2 * c + 1), 0, hi - lo), R("bc", lo, hi), A.is_le)
+            quant("f", lo, hi, R("ft", 4 * lo, 4 * hi))
+            for h in range(2):
+                mm(banks[h][c], "kh", 128 * h, "f", lo, hi - lo)
+            if c == 0 and k == 0:
+                layer(0, "b5", 0, 450)
+                scaled(0, "b5", 0, 450)
+        for b in range(1 - k, 2):
+            layer(b, "b%d" % (5 + b), CUT * k, 450)
+            scaled(b, "b%d" % (5 + b), CUT * k, 450)
         layer(2, "b1", 0, 450)
         layer(3, "b3", 0, 450)
-        if k:
-            scaled(2, "b1", 0, 450)
+
+        def add(h, c):
+            lo, hi = chunks[c]
+            tt(R("mk%d" % h, lo, hi), R(banks[h][c], 0, hi - lo), R("sb", lo, hi), A.add)
+
+        add(0, 0)
+        add(1, 0)
         for h in range(2):
             m, u = "mk%d" % h, "ru%d" % h
-            for c, (lo, hi) in enumerate(chunks):
-                tt(R(m, lo, hi), R(banks[h][c], 0, hi - lo), R("sb", lo, hi), A.add)
+            add(h, 1)
             scan(R(u, 0, 449), R(m, 0, 449), R(m, 0, 449), LEAST, A.max, A.max)
-            if k == 0 and h == 1:
-                const_index(1)
             i, j = R("ix", h, h + 1), R("jk%d" % h)
             op("a", lambda: g.scalar.activation(V(j), V(R(u, 0, COLS)), ACT.Sign, bias=V(R(u, COLS, COLS + 1)), scale=-1.0,
                                                 accum_out=V(i)), [j, i], [R(u, 0, 449)])
+        scaled(2, "b1", 0, 450)
         if k == 0:
-            scaled(2, "b1", 0, 450)
-            quant("kx", 0, 256, R("kx"))
+            const_index(0)
+            const_index(1)
             const_columns()
+            quant("kx", 0, 256, R("kx"))
+        if last:
+            const_wl(0)
         scaled(3, "b3", 0, 450)
         for h in range(2):
             ts(R("xb", 16 * h, 16 * h + 16), R("m32", 16 * h, 16 * h + 16), R("ix", h, h + 1), A.mult)
         ts(R("vv", 0, 64, 2), R("xb"), 402653184.0, A.add, -402653184.0, A.add)
         tt(R("vv", 1, 64, 2), R("xb"), R("vv", 0, 64, 2), A.subtract)
-        quant("i", 0, 136, R("vv"))
+        quant("i", 0, 136, R("vv", 0, 544))
         mm("b5", "kx", 0, "i", 0, 128, True, False)
         mm("b5", "kx", 128, "i", 8, 128, False, True)
         if k == 0:
             const_masks()
+        if last:
+            quant("v", 0, 128, R("vt"))
         copy(R("of1"), R("b5", 0, 8))
         for b in (0, 3, 1, 2):
             gather("va"[b // 2], R("hh", b, 512, 4), R("hp", PLANE * b, PLANE * b + 450), R("of1"))
@@ -424,45 +425,47 @@ def rank_program(g, core, T, topo):
         scan(R("gs"), R("kp"), R("gm"), 0.0, A.mult, A.add)
         copy(mine, R("gs", 15, 128, 16))
         codes = R(Z + "_q", 128 * r, 128 * r + 128)
-        deps("g", "rem", [codes], [])
-        remote(g, T, topo, [(V(codes).bitcast(dt.uint8), [T.cores[others[0]]], eng, "la%d" % k),
-                            (V(codes).bitcast(dt.uint8), [helper], rest, "lh%d" % k)])
-        total["sent"] = total.get("sent", 0) + len(eng) + len(rest)
+        if min(DIRECT[k]) < 128:
+            deps("g", "rem", [codes], [])
+            remote(g, T, topo, [(V(codes).bitcast(dt.uint8), [T.cores[others[0]]], eng, "la%d" % k),
+                                (V(codes).bitcast(dt.uint8), [helper], rest, "lh%d" % k)])
+            total["sent"] = total.get("sent", 0) + len(eng) + len(rest)
+        else:
+            send(codes, True, others[0:1], "la%d" % k)
         send(R(Z + "_s", 128 * r, 128 * r + 128), False, others, "lp%d" % k)
         send(mine, False, others, "lt%d" % k)
-        send(R(Z + "_q", 128 * r, 128 * r + DIRECT[k]), True, others[2:3], "lc%d" % k)
+        for n, o, sem in zip(DIRECT[k], others[1:], ("lb%d", "lc%d")):
+            if n:
+                send(R(Z + "_q", 128 * r, 128 * r + n), True, [o], sem % k)
 
-        def unpack(o, first, queue):
+        def unpack(o, n, first, queue):
             for b in range(4):
-                bank = "b%d" % (first + b)
-                mm(bank, "ke", 128 * b, Z, 128 * o, 128)
-                (copy if queue[b] == "v" else act)(R("yp", 512 * b + 128 * o, 512 * b + 128 * o + 128), R(bank, 0, 128))
+                bank = "b%d" % first[b]
+                mm(bank, "ke", 128 * b, Z, 128 * o, n)
+                (copy if queue[b] == "v" else act)(R("yp", 512 * b + 128 * o, 512 * b + 128 * o + n), R(bank, 0, n))
+
+        def lists():
+            mm("b7", "ko", 0, "a", 0, 128)
+            ts(R("ofx"), R("b7", 0, 112), 512.0, A.min, B4, A.add)
 
         if k == 0:
             iota(R("jw"), [[8, 224]], -752, 0)
+            fill(R("an", 448, 512), 0.0)
+            fill(R("yy", 512, 528), 0.0)
             const_flags()
-        for c, (lo, hi) in enumerate(chunks):
-            o, i = R("an", lo, hi), R("b%d" % (6 + c), 0, hi - lo)
-            mm(i[0], "kb", 128 * c, "f", 0, hi - lo, True, False)
-            mm(i[0], "ke", 128 * c, "f", 0, hi - lo, False, True)
-            op("a", lambda: g.scalar.activation(V(o), V(i), ACT.Relu, bias=1.0, scale=-1.0), [o], [i])
-        unpack(r, 0, "aaaa")
+        o, i = R("an", 0, COLS), R("b6", 0, COLS)
+        mm("b6", "kb", 0, "f", 0, COLS, True, False)
+        mm("b6", "ke", 0, "f", 0, COLS, False, True)
+        op("a", lambda: g.scalar.activation(V(o), V(i), ACT.Relu, bias=1.0, scale=-1.0), [o], [i])
+        unpack(r, 128, (0, 1, 2, 3), "aaaa")
         if k == 0:
             const_weights()
-        if last:
-            quant("v", 0, 128, R("vt"))
-            const_wl()
         quant("a", 0, 128, R("an"))
-        mm("b4", "ko", 0, "a", 0, 128)
+        if k:
+            lists()
         if last:
-            mm("b5", "kw", 0, "a", 0, 128)
-        ts(R("ofx"), R("b4", 0, 112), 512.0, A.min, B4, A.add)
-        if last:
-            for e in range(4):
-                op("a", lambda: g.scalar.activation(T.wlb[0:8, e:COLS:4], T.b5[32 * e:32 * e + 8, 0:112], ACT.Identity,
-                                                    bias=T.cf[32 * e:32 * e + 8, PW[1]:PW[2]]), [R("wlb", e, COLS, 4)], [R("b5"), PW])
-            dma("s", "stored", T.wl[:, :], T.wlb[0:8, 0:COLS], [], [R("wlb")])
-        unpack(others[0], 0, "aaaa")
+            const_wl(1)
+        unpack(others[0], 128, (0, 1, 2, 3), "aaaa")
         tt(R("sel"), R(S, 16, 32), R(S, 0, 16), A.is_gt)
         tt(R("mx"), R(S, 16, 32), R(S, 0, 16), A.max)
         tt(R("gg"), R("sel"), R("b16"), A.add)
@@ -470,13 +473,27 @@ def rank_program(g, core, T, topo):
         tt(R("e8"), R("f8"), R("gg", 8, 16), A.mult)
         tt(R("o8"), R("e8"), R("gg", 0, 8), A.max)
         ts(R("oft"), R("o8"), 128.0, A.mult)
-        unpack(others[1], 4, "vava")
-        unpack(others[2], 0, "vava")
+        if k == 0:
+            lists()
+        unpack(others[1], 128, (4, 5, 6, 0), "avav")
+        unpack(others[2], 128, (1, 2, 3, 4), "avav")
         for b in range(4):
-            gather("va"[b % 2], R("yy", b, 512, 4), R("yp", 512 * b, 512 * b + 512), R("oft"))
+            gather("av"[b % 2], R("yy", b, 512, 4), R("yp", 512 * b, 512 * b + 512), R("oft"))
+        lo = TAIL if last else CUT
+        gather("a", R("gy", 0, 4 * (COLS - lo)), R("yy"), R("ofx", lo // 4, COLS // 4))
+        fill(R("xt%d" % (k + 1), 1792, 1800), 0.0)
+        if last:
+            mm("b5", "kw", 0, "a", 0, 128)
+            for e in range(4):
+                op("a", lambda: g.scalar.activation(T.wlb[0:8, e:COLS:4], T.b5[32 * e:32 * e + 8, 0:112], ACT.Identity,
+                                                    bias=T.cf[32 * e:32 * e + 8, PW[1]:PW[2]]), [R("wlb", e, COLS, 4)], [R("b5"), PW])
+            dma("s", "stored", T.wl[:, :], T.wlb[0:8, 0:COLS], [], [R("wlb")])
         for c, (lo, hi) in enumerate(ends if last else chunks):
             o, i, f = R("xt%d" % (k + 1), 4 * lo, 4 * hi), R(state, 4 * lo, 4 * hi), R("ofx", lo // 4, hi // 4)
-            op("v", lambda: g.vector.tensor_tensor(V(o), V(R("yy")).indirect(V(f)), V(i), A.add), [o], [R("yy"), f, i])
+            if c:
+                tt(o, R("gy", 0, 4 * (hi - lo)), i, A.add)
+            else:
+                op("v", lambda: g.vector.tensor_tensor(V(o), V(R("yy")).indirect(V(f)), V(i), A.add), [o], [R("yy"), f, i])
             quant_state(k + 1, c)
 
     for c, (lo, hi) in enumerate(ends):

@@ -5,6 +5,7 @@ F8, U8, U16, I32, F32, BF = "float8_e4m3fn_x4", "uint8", "uint16", "int32", "flo
 ROUNDS, COLS = 2, 448
 CUT, TAIL = 256, 256
 DIRECT = ((128, 0), (128, 0))
+HEAD, LAST = 192, 360
 PLANE = 464
 SMALL, NONE, LEAST = 2.0 ** -42, -2.0 ** 29, -2.0 ** 34
 SCRATCH = {}
@@ -30,7 +31,7 @@ for _n, _w in (("u", 128), ("v", 128), ("up", 256), ("w", 512), ("f", COLS), ("i
     buf(_n + "_q", _w, F8)
     buf(_n + "_s", _w, U8)
 for _n, _w in (("ut", 512), ("vt", 512), ("ft", 4 * COLS), ("vv", 580), ("hp", 4 * PLANE), ("hh", 512), ("yp", 2048),
-               ("yy", 528), ("gy", 4 * (COLS - CUT)), ("an", 512), ("kh", 1024), ("kx", 1024), ("kb", 512), ("ko", 512), ("kw", 512), ("ke", 516),
+               ("yy", 528), ("gy", 4 * COLS), ("an", 512), ("kh", 1024), ("kx", 1024), ("kb", 512), ("ko", 512), ("kw", 512), ("ke", 516),
                ("jb", 256), ("jq", 144), ("jw", 224), ("r8", 128), ("rq", 128), ("cc", 32), ("lm", 128), ("kp", 128)):
     buf(_n, _w, BF)
 for _n, _w in (("bc", 448), ("sb", 456), ("ix", 2), ("xb", 32), ("gm", 128), ("gs", 128), ("sel", 16), ("mx", 16), ("gg", 16),
@@ -238,7 +239,7 @@ def rank_program(g, core, T, topo):
     iota(R("jb"), [[1, 256]], 0, 0)
     iota(R("iu", 0, 8), [[16, 8]], 1, 0)
     iota(R("iu", 8, 16), [[0, 8]], 15, 0)
-    iota(R("ft", 0, 4 * CUT), [[0, 4 * CUT]], 0, 0)
+    iota(R("ft", 0, 2 * CUT), [[0, 2 * CUT]], 0, 0)
     for grp in range(8):
         b, f = (grp, 4) if grp < 5 else (grp - 3, 128)
         iota(R("rq", 16 * grp, 16 * grp + 16), [[f << b + 1, 16 >> b], [f, 1 << b]], f << b, 0)
@@ -260,6 +261,7 @@ def rank_program(g, core, T, topo):
         act(o, R("kh", 0, o[2] - o[1]), 0.0, c)
 
     memset(R("kh"), 0.0)
+    memset(R("ft", 2 * CUT, 4 * CUT), 0.0)
     fill(R("xt0", 1792, 1800), 0.0)
     fill(R("kx"), 0.0)
     ts(tab(0, 7), R("jb", 16, 128, 16), P, A.is_gt, 0.5, A.max)
@@ -275,56 +277,47 @@ def rank_program(g, core, T, topo):
     ts(R("kh", 0, 1024, 4), R("iju"), -2.0 ** 23, A.mult)
     act(R("ft", 4 * CUT, 4 * COLS), R("kx", 0, 4 * (COLS - CUT)))
 
-    def const_lanes():
-        ts(R("ci", 8, 16), R("ci", 0, 8), 127, A.bitwise_and)
-        ts(R("ci", 16, 24), R("ci", 0, 8), 3968, A.bitwise_and)
-        copy(R("cf", 0, 16), R("ci", 8, 24))
+    def spare_first():
+        yield ts(R("ci", 8, 16), R("ci", 0, 8), 127, A.bitwise_and)
+        yield ts(R("ci", 16, 24), R("ci", 0, 8), 3968, A.bitwise_and)
+        yield copy(R("cf", 0, 16), R("ci", 8, 24))
+        for lo in (0, 512):
+            for e in range(2):
+                yield ts(R("kx", lo + e, lo + 320, 4), R("rq", 0, 80), LO4, A.is_equal)
+                yield ts(R("kx", lo + 322 + e, lo + 512, 4), R("rq", 80, 128), 4.0 * lo, A.subtract, HI16, A.is_equal)
+        yield ts(R("m32", 0, 32, 2), R("cc", 0, 16), HI4, A.is_equal)
+        yield ts(R("m32", 1, 32, 2), R("cc", 16, 32), LO16, A.is_equal)
+        yield quant("kx", 0, 256, R("kx"))
+        yield ts(R("lm"), R("r8"), L8, A.is_equal)
+        yield ts(R("kp"), R("r8"), 1.0, A.min)
+        yield ts(G28, HI8, 0.0625, A.mult, 16.0, A.add)
+        for b in range(2):
+            yield quant("ke", 128 * b, 128 * b + 128, R("ke", 3 - b, 515 - b))
+        yield quant("kb", 0, 128, R("kb"))
+        yield ts(ISB, P, 80.0, A.is_ge)
+        yield ts(F2, L8, 40.0, A.is_lt, 15.875, A.mult)
+        yield ts(tab(16, 10), R("r8", 0, 10), L8, A.is_lt)
+        for b in range(2, 4):
+            yield quant("ke", 128 * b, 128 * b + 128, R("ke", 3 - b, 515 - b))
+        yield ts(tab(26, 1), L8, 80.0, A.is_ge, -1.0, A.mult)
+        yield ts(tab(27, 1), L8, G28, A.is_gt, -0.5, A.mult)
+        yield ts(tab(28, 1), L8, 0.0, A.is_equal, 511.0, A.mult)
+        yield ts(tab(29, 1), F2, 0.875, A.subtract, ISB, A.mult)
+        yield ts(B4, LO32, 0.03125, A.mult)
+        yield ts(tab(0, 14), tab(16, 14), 1.0, A.add)
+        yield ts(R("b16"), R("ib"), L8, A.add, 2.0 ** -10, A.mult)
+        yield red(WG0, tab(0, 14), A.mult)
 
-    def const_index(h):
-        lo = 512 * h
-        for e in range(2):
-            ts(R("kx", lo + e, lo + 320, 4), R("rq", 0, 80), LO4, A.is_equal)
-            ts(R("kx", lo + 322 + e, lo + 512, 4), R("rq", 80, 128), 2048.0 * h, A.subtract, HI16, A.is_equal)
-
-    def const_columns():
-        ts(R("m32", 0, 32, 2), R("cc", 0, 16), HI4, A.is_equal)
-        ts(R("m32", 1, 32, 2), R("cc", 16, 32), LO16, A.is_equal)
-
-    def const_masks():
-        ts(R("lm"), R("r8"), L8, A.is_equal)
-        ts(R("kp"), R("r8"), 1.0, A.min)
-        ts(G28, HI8, 0.0625, A.mult, 16.0, A.add)
-
-    def const_flags():
-        quant("kb", 0, 128, R("kb"))
-        for b in range(4):
-            quant("ke", 128 * b, 128 * b + 128, R("ke", 3 - b, 515 - b))
-
-    def const_weights():
-        ts(ISB, P, 80.0, A.is_ge)
-        ts(F2, L8, 40.0, A.is_lt, 15.875, A.mult)
-        ts(tab(16, 10), R("r8", 0, 10), L8, A.is_lt)
-        ts(tab(26, 1), L8, 80.0, A.is_ge, -1.0, A.mult)
-        ts(tab(27, 1), L8, G28, A.is_gt, -0.5, A.mult)
-        ts(tab(28, 1), L8, 0.0, A.is_equal, 511.0, A.mult)
-        ts(tab(29, 1), F2, 0.875, A.subtract, ISB, A.mult)
-        ts(B4, LO32, 0.03125, A.mult)
-        ts(tab(0, 14), tab(16, 14), 1.0, A.add)
-        ts(R("b16"), R("ib"), L8, A.add, 2.0 ** -10, A.mult)
-        red(WG0, tab(0, 14), A.mult)
+    def spare_last():
+        yield red(PW, tab(0, 11), A.mult)
+        yield ts(NZ, L8, G28, A.not_equal, L8, A.min)
+        yield ts(WG1, PW, NZ, A.mult, 0.25, A.mult)
+        yield quant("v", 0, 128, R("vt"))
         for e in range(4):
-            ts(R("ko", e, 512, 4), R("jq", 12 - 4 * e, 140 - 4 * e), G28, A.is_equal, WG0, A.mult)
-        quant("ko", 0, 128, R("ko"))
+            yield ts(R("kw", e, 512, 4), R("jw", 96 - 32 * e, 224 - 32 * e), G28, A.is_equal, WG1, A.mult)
+        yield quant("kw", 0, 128, R("kw"))
 
-    def const_wl(part):
-        if part == 0:
-            red(PW, tab(0, 11), A.mult)
-            ts(NZ, L8, G28, A.not_equal, L8, A.min)
-            ts(WG1, PW, NZ, A.mult, 0.25, A.mult)
-            return
-        for e in range(4):
-            ts(R("kw", e, 512, 4), R("jw", 96 - 32 * e, 224 - 32 * e), G28, A.is_equal, WG1, A.mult)
-        quant("kw", 0, 128, R("kw"))
+    spare = [spare_first(), spare_last()]
 
     chunks = ((0, CUT), (CUT, COLS))
     ends = ((0, TAIL), (TAIL, COLS))
@@ -337,11 +330,16 @@ def rank_program(g, core, T, topo):
     quant_state(0, 0)
     quant("kh", 0, 256, R("kh"))
     quant_state(0, 1)
-    const_lanes()
 
     for k in range(ROUNDS):
         X, state, Z, S = "x%d" % k, "xt%d" % k, "z%d" % k, "lst%d" % k
         last = k == ROUNDS - 1
+
+        def slot(*n):
+            for _ in range(n[k]):
+                next(spare[k])
+
+        slot(3, 0)
 
         def layer(b, bank, lo, hi):
             mm(bank, "w", 128 * b, X, lo, hi - lo)
@@ -357,65 +355,51 @@ def rank_program(g, core, T, topo):
             mm("b%d" % (2 * c), "up", 0, X, lo, hi - lo)
             mm("b%d" % (2 * c + 1), "u", 0, X, lo, hi - lo)
             act(R("bc", lo, hi), R("b%d" % (2 * c), 0, hi - lo))
-            strengths(("b4", "b7")[c], lo, hi)
-            if k and c == 0:
-                for b in range(2):
-                    layer(b, "b%d" % (5 + b), lo, hi)
-        if k:
-            for b in range(2):
-                scaled(b, "b%d" % (5 + b), 0, CUT)
-        else:
+            if k:
+                strengths(("b4", "b7")[c], lo, hi)
+        wb = ("b5", "b6", "b1", "b3")
+        if k == 0:
+            strengths("b5", 0, COLS)
             for n in ("mk0", "mk1", "sb"):
                 fill(R(n, 448, 456), NONE)
+        else:
+            layer(0, wb[0], 0, 450)
+            scaled(0, wb[0], 0, 450)
         banks = [["b0", "b2"], ["b4", "b7"]]
         for c, (lo, hi) in enumerate(chunks):
             tt(R("ft", 4 * lo, 4 * hi, 4), R("b%d" % (2 * c + 1), 0, hi - lo), R("bc", lo, hi), A.is_le)
+            slot(1, 1)
             quant("f", lo, hi, R("ft", 4 * lo, 4 * hi))
             for h in range(2):
                 mm(banks[h][c], "kh", 128 * h, "f", lo, hi - lo)
-            if c == 0 and k == 0:
-                layer(0, "b5", 0, 450)
-                scaled(0, "b5", 0, 450)
-        for b in range(1 - k, 2):
-            layer(b, "b%d" % (5 + b), CUT * k, 450)
-            scaled(b, "b%d" % (5 + b), CUT * k, 450)
-        layer(2, "b1", 0, 450)
-        layer(3, "b3", 0, 450)
-
-        def add(h, c):
-            lo, hi = chunks[c]
-            tt(R("mk%d" % h, lo, hi), R(banks[h][c], 0, hi - lo), R("sb", lo, hi), A.add)
-
-        add(0, 0)
-        add(1, 0)
+        for b in range(k, 4):
+            layer(b, wb[b], 0, 450)
+        scaled(k, wb[k], 0, 450)
+        for c, (lo, hi) in enumerate(chunks):
+            for h in range(2):
+                tt(R("mk%d" % h, lo, hi), R(banks[h][c], 0, hi - lo), R("sb", lo, hi), A.add)
         for h in range(2):
             m, u = "mk%d" % h, "ru%d" % h
-            add(h, 1)
             scan(R(u, 0, 449), R(m, 0, 449), R(m, 0, 449), LEAST, A.max, A.max)
             i, j = R("ix", h, h + 1), R("jk%d" % h)
             op("a", lambda: g.scalar.activation(V(j), V(R(u, 0, COLS)), ACT.Sign, bias=V(R(u, COLS, COLS + 1)), scale=-1.0,
                                                 accum_out=V(i)), [j, i], [R(u, 0, 449)])
-        scaled(2, "b1", 0, 450)
-        if k == 0:
-            const_index(0)
-            const_index(1)
-            const_columns()
-            quant("kx", 0, 256, R("kx"))
-        if last:
-            const_wl(0)
-        scaled(3, "b3", 0, 450)
+        for b in range(k + 1, 4):
+            scaled(b, wb[b], 0, 450)
+        slot(9, 6)
         for h in range(2):
             ts(R("xb", 16 * h, 16 * h + 16), R("m32", 16 * h, 16 * h + 16), R("ix", h, h + 1), A.mult)
+        slot(1, 0)
         ts(R("vv", 0, 64, 2), R("xb"), 402653184.0, A.add, -402653184.0, A.add)
+        slot(1, 0)
         tt(R("vv", 1, 64, 2), R("xb"), R("vv", 0, 64, 2), A.subtract)
+        slot(1, 0)
         quant("i", 0, 136, R("vv", 0, 544))
         mm("b5", "kx", 0, "i", 0, 128, True, False)
         mm("b5", "kx", 128, "i", 8, 128, False, True)
-        if k == 0:
-            const_masks()
-        if last:
-            quant("v", 0, 128, R("vt"))
+        slot(3, 1)
         copy(R("of1"), R("b5", 0, 8))
+        slot(1, 0)
         for b in (0, 3, 1, 2):
             gather("va"[b // 2], R("hh", b, 512, 4), R("hp", PLANE * b, PLANE * b + 450), R("of1"))
         mine = R(S, STRONG[r], STRONG[r] + 8)
@@ -423,6 +407,7 @@ def rank_program(g, core, T, topo):
            [R("gm")], [R("sb", 0, 450), R("of1"), R("lm")])
         quant(Z, 128 * r, 128 * r + 128, R("hh"))
         scan(R("gs"), R("kp"), R("gm"), 0.0, A.mult, A.add)
+        slot(2, 0)
         copy(mine, R("gs", 15, 128, 16))
         codes = R(Z + "_q", 128 * r, 128 * r + 128)
         if min(DIRECT[k]) < 128:
@@ -452,19 +437,28 @@ def rank_program(g, core, T, topo):
             iota(R("jw"), [[8, 224]], -752, 0)
             fill(R("an", 448, 512), 0.0)
             fill(R("yy", 512, 528), 0.0)
-            const_flags()
+        slot(2, 0)
         o, i = R("an", 0, COLS), R("b6", 0, COLS)
         mm("b6", "kb", 0, "f", 0, COLS, True, False)
         mm("b6", "ke", 0, "f", 0, COLS, False, True)
         op("a", lambda: g.scalar.activation(V(o), V(i), ACT.Relu, bias=1.0, scale=-1.0), [o], [i])
         unpack(r, 128, (0, 1, 2, 3), "aaaa")
-        if k == 0:
-            const_weights()
+        fill(R("xt%d" % (k + 1), 1792, 1800), 0.0)
+        slot(8, 0)
         quant("a", 0, 128, R("an"))
-        if k:
+        if k == 0:
+            for e in range(4):
+                ts(R("ko", e, 512, 4), R("jq", 12 - 4 * e, 140 - 4 * e), G28, A.is_equal, WG0, A.mult)
+            quant("ko", 0, 128, R("ko"))
+        else:
             lists()
         if last:
-            const_wl(1)
+            mm("b5", "kw", 0, "a", 0, 128)
+            for e in range(4):
+                op("v", lambda: g.vector.tensor_scalar(T.wlb[0:8, e:COLS:4], T.b5[32 * e:32 * e + 8, 0:112],
+                                                       T.cf[32 * e:32 * e + 8, PW[1]:PW[2]], None, A.add),
+                   [R("wlb", e, COLS, 4)], [R("b5"), PW])
+            dma("s", "stored", T.wl[:, :], T.wlb[0:8, 0:COLS], [], [R("wlb")])
         unpack(others[0], 128, (0, 1, 2, 3), "aaaa")
         tt(R("sel"), R(S, 16, 32), R(S, 0, 16), A.is_gt)
         tt(R("mx"), R(S, 16, 32), R(S, 0, 16), A.max)
@@ -479,27 +473,21 @@ def rank_program(g, core, T, topo):
         unpack(others[2], 128, (1, 2, 3, 4), "avav")
         for b in range(4):
             gather("av"[b % 2], R("yy", b, 512, 4), R("yp", 512 * b, 512 * b + 512), R("oft"))
-        lo = TAIL if last else CUT
-        gather("a", R("gy", 0, 4 * (COLS - lo)), R("yy"), R("ofx", lo // 4, COLS // 4))
-        fill(R("xt%d" % (k + 1), 1792, 1800), 0.0)
-        if last:
-            mm("b5", "kw", 0, "a", 0, 128)
-            for e in range(4):
-                op("a", lambda: g.scalar.activation(T.wlb[0:8, e:COLS:4], T.b5[32 * e:32 * e + 8, 0:112], ACT.Identity,
-                                                    bias=T.cf[32 * e:32 * e + 8, PW[1]:PW[2]]), [R("wlb", e, COLS, 4)], [R("b5"), PW])
-            dma("s", "stored", T.wl[:, :], T.wlb[0:8, 0:COLS], [], [R("wlb")])
-        for c, (lo, hi) in enumerate(ends if last else chunks):
-            o, i, f = R("xt%d" % (k + 1), 4 * lo, 4 * hi), R(state, 4 * lo, 4 * hi), R("ofx", lo // 4, hi // 4)
-            if c:
-                tt(o, R("gy", 0, 4 * (hi - lo)), i, A.add)
-            else:
-                op("v", lambda: g.vector.tensor_tensor(V(o), V(R("yy")).indirect(V(f)), V(i), A.add), [o], [R("yy"), f, i])
-            quant_state(k + 1, c)
+        cut = TAIL if last else CUT
+        pieces = ((HEAD, cut), (cut, LAST), (LAST, COLS))
+        for lo, hi in pieces:
+            gather("a", R("gy", 4 * lo, 4 * hi), R("yy"), R("ofx", lo // 4, hi // 4))
+        o, i, f = R("xt%d" % (k + 1), 0, 4 * HEAD), R(state, 0, 4 * HEAD), R("ofx", 0, HEAD // 4)
+        op("v", lambda: g.vector.tensor_tensor(V(o), V(R("yy")).indirect(V(f)), V(i), A.add), [o], [R("yy"), f, i])
+        for c, (lo, hi) in enumerate(pieces):
+            tt(R("xt%d" % (k + 1), 4 * lo, 4 * hi), R("gy", 4 * lo, 4 * hi), R(state, 4 * lo, 4 * hi), A.add)
+            if c != 1:
+                quant_state(k + 1, c // 2)
 
     for c, (lo, hi) in enumerate(ends):
         dma("s", "stored", T.oc[:, 4 * lo:4 * hi], V(R("x2_q", lo, hi)).bitcast(dt.uint8), [], [R("x2_q", lo, hi)])
         mm("b%d" % c, "v", 0, "x2", lo, hi - lo)
-        act(R("yo", lo, hi), R("b%d" % c, 0, hi - lo))
+        (copy if c else act)(R("yo", lo, hi), R("b%d" % c, 0, hi - lo))
         if c:
             for q in range(4):
                 dma("s", "stored", T.osc[4 * q:4 * q + 4, :], T.x2_s[32 * q:32 * q + 4, 0:COLS], [], [R("x2_s", 0, COLS)])

@@ -3,9 +3,15 @@ from concourse.mybir import dt, AluOpType, AxisListType, ActivationFunctionType
 
 F8, U8, U16, I32, F32, BF = "float8_e4m3fn_x4", "uint8", "uint16", "int32", "float32", "bfloat16"
 ROUNDS, COLS = 2, 448
-CUT, TAIL = 256, 256
-DIRECT = ((128, 0), (128, 0))
-HEAD, LAST = 192, 360
+CUT = 256
+CUTS = ((0, 256, COLS), (0, 256, COLS), (0, 256, COLS))
+SEARCH = ("q0 p0 x0 q1 t0 t1 k0 c0 s1 f0 w0 h0 s1 c1 s1 f1 w1 w2 w3 h1 m00 m01 m10 m11 r10 r11",
+          "d0 q0 t0 d1 d2 q1 t1 w0 h0 c0 s1 f0 s1 c1 s1 f1 w1 w2 w3 h1 m00 m01 m10 m11 r10 r11")
+VIA = ("s", "q")
+TAKE = ("aaaa" "avav" "AAAa" "vava", "aaaa" "avav" "aVaa" "VaVa")
+WISH = (0, 0)
+RUN = 452
+PIECES = (192, 256, 360, COLS)
 PLANE = 464
 SMALL, NONE, LEAST = 2.0 ** -42, -2.0 ** 29, -2.0 ** 34
 SCRATCH = {}
@@ -22,31 +28,29 @@ for _k in range(3):
 for _k in range(2):
     buf("z%d_q" % _k, 512, F8)
     buf("z%d_s" % _k, 512, U8)
-    buf("lst%d" % _k, 32, F32)
-    buf("mk%d" % _k, 456, F32)
-    buf("ru%d" % _k, 456, F32)
-    buf("jk%d" % _k, 448, BF)
+    buf("lst%d" % _k, 16, F32)
+    buf("jk%d" % _k, 448, F32)
 for _n, _w in (("u", 128), ("v", 128), ("up", 256), ("w", 512), ("f", COLS), ("i", 136), ("a", 128),
-               ("kh", 256), ("kx", 256), ("kb", 128), ("ko", 128), ("ke", 512), ("kw", 128)):
+               ("kh", 256), ("kx", 128), ("kb", 128), ("ko", 128), ("ke", 512), ("kw", 128)):
     buf(_n + "_q", _w, F8)
     buf(_n + "_s", _w, U8)
-for _n, _w in (("ut", 512), ("vt", 512), ("ft", 4 * COLS), ("vv", 580), ("hp", 4 * PLANE), ("hh", 512), ("yp", 2048),
-               ("yy", 528), ("gy", 4 * COLS), ("an", 512), ("kh", 1024), ("kx", 1024), ("kb", 512), ("ko", 512), ("kw", 512), ("ke", 516),
-               ("jb", 256), ("jq", 144), ("jw", 224), ("r8", 128), ("rq", 128), ("cc", 32), ("lm", 128), ("kp", 128)):
+for _n, _w in (("ut", 512), ("vt", 512), ("ft", 64 + 4 * CUT), ("hp", 4 * PLANE), ("hh", 512), ("yp", 2048),
+               ("yy", 1024), ("gy", 4 * COLS), ("kh", 1024), ("kx", 516), ("kb", 512), ("ko", 512), ("kw", 512), ("ke", 516),
+               ("jm", 16), ("js", 16), ("jq", 144), ("jw", 224), ("jn", 128), ("r8", 128), ("rq", 128), ("cc", 32), ("lm", 128),
+               ("am", 128), ("dg", 128)):
     buf(_n, _w, BF)
-for _n, _w in (("bc", 448), ("sb", 456), ("ix", 2), ("xb", 32), ("gm", 128), ("gs", 128), ("sel", 16), ("mx", 16), ("gg", 16),
-               ("f8", 8), ("e8", 8), ("o8", 8), ("yo", 448), ("wlb", 448), ("cf", 32), ("b16", 16),
-               ("ib", 16), ("m32", 32), ("tab", 32)):
+for _n, _w in (("bc", 448), ("sb", 456), ("mk", 2 * RUN), ("ru", 2 * RUN), ("ix", 2), ("xb", 32), ("gm", 128), ("gs", 128), ("rw", 8),
+               ("tx", 64), ("tb", 256), ("yo", 448), ("wlb", 448), ("cf", 40), ("c8", 8), ("m32", 32), ("tab", 32)):
     buf(_n, _w, F32)
-for _n, _w in (("ci", 24), ("ijt", 256), ("iju", 256), ("iu", 16)):
+for _n, _w in (("ci", 24), ("ijt", 16), ("iju", 16), ("iu", 16)):
     buf(_n, _w, I32)
-for _n, _w in (("ou", 16), ("of1", 8), ("oft", 8), ("ofx", 112)):
+for _n, _w in (("ou", 16), ("oh", 16), ("of1", 8), ("oc8", 8), ("oft", 8), ("ofx", 112)):
     buf(_n, _w, U16)
 PSUM = ["b%d" % _k for _k in range(8)]
 for _n in PSUM:
     buf(_n, 512, F32, "psum")
 SEMAPHORES = (["v", "a", "t", "gp", "sent", "stored", "dx0", "dx1", "du", "dv", "dw0", "dw1", "dws"]
-              + ["%s%d" % (n, k) for n in ("lp", "lt", "la", "lb", "lc", "lh") for k in range(2)])
+              + ["%s%d" % (n, k) for n in ("lp", "ls", "lt", "la", "lb", "lc", "lh") for k in range(2)])
 
 
 def helper_of(core, topo):
@@ -66,14 +70,14 @@ def remote(g, T, topo, transfers):
 
 
 def helper_program(g, core, r, T, topo):
-    eng, sent = topo.engines(core, T.cores[r ^ 2]), 0
+    eng, sent = topo.engines(core, T.cores[r ^ 3]), 0
     for k in range(ROUNDS):
-        if min(DIRECT[k]) < 128:
+        if VIA[k]:
             g.wait_ge(T.sem["lh%d" % k], len(on_chip(T.cores[r], T, topo)))
-        for d, lo, sem in ((2, DIRECT[k][0], "lb%d"), (3, DIRECT[k][1], "lc%d")):
-            if lo < 128:
-                remote(g, T, topo, [(T["z%d_q" % k][:, 128 * r + lo:128 * r + 128].bitcast(dt.uint8), [T.cores[r ^ d]], eng, sem % k)])
-                sent += len(eng)
+            view = T["z%d_%s" % (k, VIA[k])][:, 128 * r:128 * r + 128]
+            remote(g, T, topo, [(view.bitcast(dt.uint8) if VIA[k] == "q" else view, [T.cores[r ^ 3]], eng,
+                                 ("lc%d" if VIA[k] == "q" else "ls%d") % k)])
+            sent += len(eng)
     if sent:
         g.wait_ge(T.sem.sent, sent)
 
@@ -164,10 +168,19 @@ def rank_program(g, core, T, topo):
         op("v", lambda: g.vector.tensor_reduce(V(o), V(i), AxisListType.X, f), [o], [i])
 
     def scan(o, i, j, init, f1, f2):
-        op("v", lambda: g.vector.tensor_tensor_scan(V(o), V(i), V(j), init, f1, f2), [o], [i, j])
+        col = isinstance(init, tuple)
+        op("v", lambda: g.vector.tensor_tensor_scan(V(o), V(i), V(j), V(init) if col else init, f1, f2), [o], [i, j] + [init] * col)
 
     def act(o, i, scale=1.0, bias=0.0):
         op("a", lambda: g.scalar.activation(V(o), V(i), ACT.Copy, bias=bias, scale=scale), [o], [i])
+
+    def line(o, i, scale, bias):
+        v = lambda s: V(s) if isinstance(s, tuple) else s
+        op("a", lambda: g.scalar.activation(V(o), V(i), ACT.Identity, bias=v(bias), scale=v(scale)), [o],
+           [i] + [s for s in (scale, bias) if isinstance(s, tuple)])
+
+    def count(o, i, top, n):
+        op("a", lambda: g.scalar.activation(V(o), V(i), ACT.Sign, bias=V(top), scale=-1.0, accum_out=V(n)), [o, n], [i, top])
 
     def gather(q, o, w, f):
         if q == "v":
@@ -207,25 +220,27 @@ def rank_program(g, core, T, topo):
     helper = helper_of(core, topo)
     rest = on_chip(core, T, topo)
 
-    def send(piece, codes, to, sem):
+    def send(piece, codes, to, sem, via=None):
         deps("g", "rem", [piece], [])
-        remote(g, T, topo, [(V(piece).bitcast(dt.uint8) if codes else V(piece), [T.cores[o] for o in to], eng, sem)])
-        total["sent"] = total.get("sent", 0) + len(eng)
+        view = V(piece).bitcast(dt.uint8) if codes else V(piece)
+        remote(g, T, topo, [(view, [T.cores[o] for o in to], eng, sem)] + [(view, [helper], rest, via)] * bool(via))
+        total["sent"] = total.get("sent", 0) + len(eng) + len(rest) * bool(via)
 
-    STRONG = [0, 16, 8, 24]
+    STRONG = [0, 4, 8, 12]
     for k in range(ROUNDS):
-        lands = [("lp%d", 3, [R("z%d_s" % k, 128 * o, 128 * o + 128) for o in others]),
-                 ("lt%d", 3, [R("lst%d" % k, STRONG[o], STRONG[o] + 8) for o in others])]
-        lands += [(s, n, [R("z%d_q" % k, 128 * o, 128 * o + 128)])
-                  for s, o, n in zip(("la%d", "lb%d", "lc%d"), others, [1] + [1 + (0 < n < 128) for n in DIRECT[k]])]
+        n = 3 - (VIA[k] == "s")
+        lands = [("lp%d", n, [R("z%d_s" % k, 128 * o, 128 * o + 128) for o in others[:n]]),
+                 ("ls%d", 3 - n, [R("z%d_s" % k, 128 * o, 128 * o + 128) for o in others[n:]]),
+                 ("lt%d", 3, [R("lst%d" % k, STRONG[o], STRONG[o] + 4) for o in others])]
+        lands += [(s, 1, [R("z%d_q" % k, 128 * o, 128 * o + 128)]) for s, o in zip(("la%d", "lb%d", "lc%d"), others)]
         for sem, n, regs in lands:
             total[sem % k] = n * len(eng)
             note("rem", (sem % k, n * len(eng)), [], regs)
 
-    dma("s", "dx0", T.xt0[:, 0:4 * CUT], T.x[:, 0:4 * CUT], [R("xt0", 0, 4 * CUT)], [])
-    dma("a", "du", V(R("ut")), T.u[:, :], [R("ut")], [])
-    dma("s", "dx1", T.xt0[:, 4 * CUT:1792], T.x[:, 4 * CUT:1792], [R("xt0", 4 * CUT, 1792)], [])
-    wait("s", ("dx0", 16))
+    dma("s", "du", V(R("ut")), T.u[:, :], [R("ut")], [])
+    for c, (lo, hi) in enumerate(zip(CUTS[0], CUTS[0][1:])):
+        dma("s", "dx%d" % c, T.xt0[:, 4 * lo:4 * hi], T.x[:, 4 * lo:4 * hi], [R("xt0", 4 * lo, 4 * hi)], [])
+    wait("s", ("du", 16))
     dma("s", "dws", V(R("w_s")), T.ws[:, :], [R("w_s")], [])
     for e in range(2):
         o = R("w_q", 256 * e, 256 * e + 256)
@@ -234,79 +249,78 @@ def rank_program(g, core, T, topo):
     dma("s", "dv", V(R("vt")), T.v[:, :], [R("vt")], [])
 
     LO4, L8, LO16, LO32, HI4, HI8, HI16 = [cf(k) for k in (0, 1, 3, 7, 8, 9, 11)]
-    P, B4, IPW, IS, G28, WG0, WG1, PW, NZ, CAB, ISB, F2 = [cf(k) for k in range(16, 28)]
-    iota(P, [[0, 1]], 0, 1)
-    iota(R("jb"), [[1, 256]], 0, 0)
-    iota(R("iu", 0, 8), [[16, 8]], 1, 0)
-    iota(R("iu", 8, 16), [[0, 8]], 15, 0)
-    iota(R("ft", 0, 2 * CUT), [[0, 2 * CUT]], 0, 0)
-    for grp in range(8):
-        b, f = (grp, 4) if grp < 5 else (grp - 3, 128)
-        iota(R("rq", 16 * grp, 16 * grp + 16), [[f << b + 1, 16 >> b], [f, 1 << b]], f << b, 0)
-    iota(R("cc", 0, 16), [[-512, 2], [128, 8]], 0, 0)
-    iota(R("cc", 16, 32), [[0, 2], [16, 8]], 0, 0)
-    iota(R("r8"), [[0, 8], [8, 16]], 0, 0)
-    iota(R("vv", 64, 580), [[0, 516]], 0, 0)
-
-    def ones(o, pattern, base):
-        i = R("vv", 64, 64 + o[2])
-        op("g", lambda: g.affine_select(V(o), V(i), pattern, A.not_equal, 1.0, base, 4), [o], [i])
-
-    ones(R("ke"), [[-1, 516]], 3)
-    ones(R("kb"), [[0, 8], [-64, 16], [1, 4]], 128)
-    iota(R("ib"), [[2048, 2], [128, 8]], 0, 0)
-    iota(R("jq"), [[2, 36], [0, 4]], 10, 0)
+    P, B4, IPW, IS, G28, WG0, WG1, PW, NZ, HB, ISB, F2, STP, DG = [cf(k) for k in range(16, 30)]
 
     def fill(o, c):
         act(o, R("kh", 0, o[2] - o[1]), 0.0, c)
 
     memset(R("kh"), 0.0)
-    memset(R("ft", 2 * CUT, 4 * CUT), 0.0)
-    fill(R("xt0", 1792, 1800), 0.0)
     fill(R("kx"), 0.0)
-    ts(tab(0, 7), R("jb", 16, 128, 16), P, A.is_gt, 0.5, A.max)
-    ts(tab(8), R("jb", 0, 128, 16), P, A.is_equal, 128.0, A.mult)
+    fill(R("ft", 64 + 2 * CUT, 64 + 4 * CUT), 0.0)
+    iota(P, [[0, 1]], 0, 1)
+    iota(R("js", 0, 8), [[16, 8]], 0, 0)
+    iota(R("js", 8, 16), [[4, 8]], 4, 0)
+    iota(R("jm"), [[256, 2], [512, 4], [128, 2]], 0, 0)
+    iota(R("iu", 0, 8), [[16, 8]], 1, 0)
+    iota(R("iu", 8, 16), [[0, 8]], 15, 0)
+    iota(R("ft", 64, 64 + 2 * CUT), [[0, 2 * CUT]], 0, 0)
+    iota(R("xt0", 1792, 1800), [[0, 8]], 0, 0)
+    iota(R("cc", 0, 16), [[-64, 2], [64, 8]], 0, 0)
+    iota(R("cc", 16, 32), [[0, 2], [16, 8]], 0, 0)
+    for grp in range(8):
+        b, f = (grp, 4) if grp < 5 else (grp - 3, 32)
+        iota(R("rq", 16 * grp, 16 * grp + 16), [[f << b + 1, 16 >> b], [f, 1 << b]], f << b, 0)
+
+    def ones(o, pattern, base):
+        i = R("kx", 0, o[2])
+        op("g", lambda: g.affine_select(V(o), V(i), pattern, A.not_equal, 1.0, base, 4), [o], [i])
+
+    ones(R("ke"), [[-1, 516]], 3)
+    ones(R("kb"), [[0, 8], [-64, 16], [1, 4]], 128)
+    iota(R("r8"), [[0, 8], [8, 16]], 0, 0)
+    ts(tab(0, 7), R("js", 1, 8), P, A.is_gt, 1.0, A.add)
+    ts(R("ci", 0, 8), R("js", 8, 16), P, A.mult)
     red(IPW, tab(0, 7), A.mult)
-    red(IS, tab(8), A.max)
-    ts(R("ci", 0, 8), R("jb", 4, 33, 4), P, A.mult)
-    ts(R("ijt"), R("jb"), IPW, A.mult, IS, A.mult)
+    ts(R("ci", 8, 16), R("ci", 0, 8), 127, A.bitwise_and)
+    ts(R("ci", 16, 24), R("ci", 0, 8), 3968, A.bitwise_and)
+    ts(ISB, P, 80.0, A.is_ge)
+    copy(R("cf", 0, 16), R("ci", 8, 24))
     copy(R("ou"), R("iu"))
-    ts(R("iju"), R("ijt"), 128, A.bitwise_and)
+    ts(R("ijt"), R("jm"), L8, A.add, IPW, A.mult)
+    ts(IS, L8, 0.0, A.is_equal, 128.0, A.mult)
+    ts(R("iju"), R("ijt"), 1024, A.bitwise_and, 10, A.logical_shift_right)
+    ts(R("c8", 0, 2), R("js", 0, 2), IS, A.mult, -2.0 ** 19, A.mult)
+    copy(R("oh"), R("iju"))
+    gather("a", R("kh", 0, 1024, 4), R("c8", 0, 2), R("oh"))
     quant("u", 0, 128, R("ut"))
-    pick("up", 0, 256, "u", 128, R("ou"))
-    ts(R("kh", 0, 1024, 4), R("iju"), -2.0 ** 23, A.mult)
-    act(R("ft", 4 * CUT, 4 * COLS), R("kx", 0, 4 * (COLS - CUT)))
+    memset(R("mk", COLS, 2 * RUN, RUN), NONE)
+    pick("up", 0, 128, "u", 128, R("ou", 0, 8))
 
     def spare_first():
-        yield ts(R("ci", 8, 16), R("ci", 0, 8), 127, A.bitwise_and)
-        yield ts(R("ci", 16, 24), R("ci", 0, 8), 3968, A.bitwise_and)
-        yield copy(R("cf", 0, 16), R("ci", 8, 24))
-        for lo in (0, 512):
-            for e in range(2):
-                yield ts(R("kx", lo + e, lo + 320, 4), R("rq", 0, 80), LO4, A.is_equal)
-                yield ts(R("kx", lo + 322 + e, lo + 512, 4), R("rq", 80, 128), 4.0 * lo, A.subtract, HI16, A.is_equal)
         yield ts(R("m32", 0, 32, 2), R("cc", 0, 16), HI4, A.is_equal)
         yield ts(R("m32", 1, 32, 2), R("cc", 16, 32), LO16, A.is_equal)
-        yield quant("kx", 0, 256, R("kx"))
-        yield ts(R("lm"), R("r8"), L8, A.is_equal)
-        yield ts(R("kp"), R("r8"), 1.0, A.min)
-        yield ts(G28, HI8, 0.0625, A.mult, 16.0, A.add)
-        for b in range(2):
-            yield quant("ke", 128 * b, 128 * b + 128, R("ke", 3 - b, 515 - b))
-        yield quant("kb", 0, 128, R("kb"))
-        yield ts(ISB, P, 80.0, A.is_ge)
+        yield ts(tab(10, 1), L8, 80.0, A.is_lt)
+        for h in range(2):
+            yield ts(R("kx", h, 320, 4), R("rq", 0, 80), LO4, A.is_equal)
+        for h in range(2):
+            yield ts(R("kx", 322 + h, 512, 4), R("rq", 80, 128), 128.0 * h, A.subtract, HB, A.is_equal)
         yield ts(F2, L8, 40.0, A.is_lt, 15.875, A.mult)
-        yield ts(tab(16, 10), R("r8", 0, 10), L8, A.is_lt)
+        yield quant("kx", 0, 128, R("kx", 0, 512))
+        yield ts(tab(13, 1), F2, 0.875, A.subtract, ISB, A.mult)
+        yield tt(R("dg"), R("ke", 3, 515, 4), R("rq"), A.mult)
+        yield ts(tab(11, 1), L8, G28, A.is_le, 0.5, A.max)
+        yield quant("ke", 0, 128, R("ke", 3, 515))
+        yield quant("kb", 0, 128, R("kb"))
+        yield quant("ke", 128, 256, R("ke", 2, 514))
+        yield ts(tab(0, 10), R("r8", 0, 10), L8, A.is_lt, 1.0, A.add)
+        yield ts(tab(12, 1), tab(13, 1), 1.0, A.add)
+        yield ts(R("lm"), R("r8"), L8, A.is_equal)
         for b in range(2, 4):
             yield quant("ke", 128 * b, 128 * b + 128, R("ke", 3 - b, 515 - b))
-        yield ts(tab(26, 1), L8, 80.0, A.is_ge, -1.0, A.mult)
-        yield ts(tab(27, 1), L8, G28, A.is_gt, -0.5, A.mult)
-        yield ts(tab(28, 1), L8, 0.0, A.is_equal, 511.0, A.mult)
-        yield ts(tab(29, 1), F2, 0.875, A.subtract, ISB, A.mult)
-        yield ts(B4, LO32, 0.03125, A.mult)
-        yield ts(tab(0, 14), tab(16, 14), 1.0, A.add)
-        yield ts(R("b16"), R("ib"), L8, A.add, 2.0 ** -10, A.mult)
-        yield red(WG0, tab(0, 14), A.mult)
+        yield red(WG1, tab(0, 13), A.mult)
+        yield tt(R("am"), R("lm"), R("jn"), A.mult)
+        yield ts(WG0, IS, 4.0, A.mult, WG1, A.max)
+        yield ts(R("oc8"), R("c8"), 0.25, A.mult)
 
     def spare_last():
         yield red(PW, tab(0, 11), A.mult)
@@ -319,17 +333,7 @@ def rank_program(g, core, T, topo):
 
     spare = [spare_first(), spare_last()]
 
-    chunks = ((0, CUT), (CUT, COLS))
-    ends = ((0, TAIL), (TAIL, COLS))
-
-    def quant_state(k, c):
-        lo, hi = (ends if k == ROUNDS else chunks)[c]
-        hi += 2 * c
-        quant("x%d" % k, lo, hi, R("xt%d" % k, 4 * lo, 4 * hi))
-
-    quant_state(0, 0)
-    quant("kh", 0, 256, R("kh"))
-    quant_state(0, 1)
+    ends = list(zip(CUTS[ROUNDS], CUTS[ROUNDS][1:]))
 
     for k in range(ROUNDS):
         X, state, Z, S = "x%d" % k, "xt%d" % k, "z%d" % k, "lst%d" % k
@@ -339,158 +343,176 @@ def rank_program(g, core, T, topo):
             for _ in range(n[k]):
                 next(spare[k])
 
-        slot(3, 0)
+        chunks, done = list(zip(CUTS[k], CUTS[k][1:])), [0, 0]
+        wb = ("b7", "b0", "b1", "b2") if len(chunks) == 3 else ("b6", "b7", "b4", "b5")
 
-        def layer(b, bank, lo, hi):
-            mm(bank, "w", 128 * b, X, lo, hi - lo)
-
-        def scaled(b, bank, lo, hi):
-            act(R("hp", PLANE * b + lo, PLANE * b + hi), R(bank, 0, hi - lo), 0.03125)
-
-        def strengths(bank, lo, hi):
-            mm(bank, "up", 128, X, lo, hi - lo)
-            act(R("sb", lo, hi), R(bank, 0, hi - lo), SMALL)
-
-        for c, (lo, hi) in enumerate(chunks):
+        def scores(c):
+            lo, hi = chunks[c]
+            end = hi + 2 * (hi == COLS)
+            quant(X, lo, end, R(state, 4 * lo, 4 * end))
             mm("b%d" % (2 * c), "up", 0, X, lo, hi - lo)
             mm("b%d" % (2 * c + 1), "u", 0, X, lo, hi - lo)
             act(R("bc", lo, hi), R("b%d" % (2 * c), 0, hi - lo))
-            if k:
-                strengths(("b4", "b7")[c], lo, hi)
-        wb = ("b5", "b6", "b1", "b3")
+
+        def strengths(c):
+            lo, hi = chunks[c]
+            bank = "b%d" % (2 * len(chunks) + c % 2)
+            mm(bank, "up", 128, X, lo, hi - lo)
+            act(R("sb", lo, hi), R(bank, 0, hi - lo), SMALL)
+
+        def absent(c):
+            lo, hi = chunks[c]
+            tt(R("ft", 64, 64 + 4 * (hi - lo), 4), R("b%d" % (2 * c + 1), 0, hi - lo), R("bc", lo, hi), A.is_le)
+
+        def flags(c):
+            lo, hi = chunks[c]
+            quant("f", lo, hi, R("ft", 64, 64 + 4 * (hi - lo)))
+            for h in range(2):
+                mm("b%d" % (2 * c + h), "kh", 128 * h, "f", lo, hi - lo)
+
+        def masked(c, h):
+            lo, hi = chunks[c]
+            tt(R("mk", RUN * h + lo, RUN * h + hi), R("b%d" % (2 * c + h), 0, hi - lo), R("sb", lo, hi), A.add)
+
+        def running(c, h):
+            lo, hi = RUN * h + done[h], RUN * h + chunks[c][1] + (chunks[c][1] == COLS)
+            scan(R("ru", lo, hi), R("mk", lo, hi), R("mk", lo, hi), R("ru", lo - 1, lo) if done[h] else LEAST, A.max, A.max)
+            done[h] = chunks[c][1]
+            if done[h] == COLS:
+                count(R("jk%d" % h), R("ru", RUN * h, hi - 1), R("ru", hi - 1, hi), R("ix", h, h + 1))
+
+        def added(c):
+            lo, hi = PIECES[c:c + 2]
+            tt(R(state, 4 * lo, 4 * hi), R("gy", 4 * lo, 4 * hi), R("xt%d" % (k - 1), 4 * lo, 4 * hi), A.add)
+
+        def small(c):
+            fill(R("yy", 512, 576), 0.0)
+            line(HB, HI16, 0.25, HI4)
+            line(G28, HI8, 0.0625, 16.0)
+            line(B4, LO32, 0.03125, 0.0)
+            line(STP, ISB, -7.75, 8.0)
+
+        steps = {"q": scores, "t": strengths, "c": absent, "f": flags, "m": masked, "r": running, "d": added, "k": small,
+                 "p": lambda n: pick("up", 128, 256, "u", 128, R("ou", 8, 16)),
+                 "x": lambda n: quant("kh", 0, 256, R("kh")),
+                 "s": lambda n: slot(n, n), "w": lambda b: mm(wb[b], "w", 128 * b, X, 0, 450),
+                 "h": lambda b: act(R("hp", PLANE * b, PLANE * b + 450), R(wb[b], 0, 450), 0.03125)}
+        for step in SEARCH[k].split():
+            steps[step[0]](*map(int, step[1:]))
+        mine = R(S, STRONG[r], STRONG[r] + 4)
+        copy(mine, R("ru", COLS - RUN // 2, COLS + RUN + 1, RUN // 2))
+        send(mine, False, others, "lt%d" % k)
         if k == 0:
-            strengths("b5", 0, COLS)
-            for n in ("mk0", "mk1", "sb"):
-                fill(R(n, 448, 456), NONE)
-        else:
-            layer(0, wb[0], 0, 450)
-            scaled(0, wb[0], 0, 450)
-        banks = [["b0", "b2"], ["b4", "b7"]]
-        for c, (lo, hi) in enumerate(chunks):
-            tt(R("ft", 4 * lo, 4 * hi, 4), R("b%d" % (2 * c + 1), 0, hi - lo), R("bc", lo, hi), A.is_le)
-            slot(1, 1)
-            quant("f", lo, hi, R("ft", 4 * lo, 4 * hi))
-            for h in range(2):
-                mm(banks[h][c], "kh", 128 * h, "f", lo, hi - lo)
-        for b in range(k, 4):
-            layer(b, wb[b], 0, 450)
-        scaled(k, wb[k], 0, 450)
-        for c, (lo, hi) in enumerate(chunks):
-            for h in range(2):
-                tt(R("mk%d" % h, lo, hi), R(banks[h][c], 0, hi - lo), R("sb", lo, hi), A.add)
+            iota(R("jq"), [[2, 36], [0, 4]], 10, 0)
+            iota(R("jn"), [[4, 128]], 4, 0)
+            iota(R("xt1", 1792, 1800), [[0, 8]], 0, 0)
+        for b in range(2, 4):
+            steps["h"](b)
+        slot(6, 3)
         for h in range(2):
-            m, u = "mk%d" % h, "ru%d" % h
-            scan(R(u, 0, 449), R(m, 0, 449), R(m, 0, 449), LEAST, A.max, A.max)
-            i, j = R("ix", h, h + 1), R("jk%d" % h)
-            op("a", lambda: g.scalar.activation(V(j), V(R(u, 0, COLS)), ACT.Sign, bias=V(R(u, COLS, COLS + 1)), scale=-1.0,
-                                                accum_out=V(i)), [j, i], [R(u, 0, 449)])
-        for b in range(k + 1, 4):
-            scaled(b, wb[b], 0, 450)
-        slot(9, 6)
-        for h in range(2):
-            ts(R("xb", 16 * h, 16 * h + 16), R("m32", 16 * h, 16 * h + 16), R("ix", h, h + 1), A.mult)
+            ts(R("xb", h, 32, 2), R("m32", 16 * h, 16 * h + 16), R("ix", h, h + 1), A.mult)
         slot(1, 0)
-        ts(R("vv", 0, 64, 2), R("xb"), 402653184.0, A.add, -402653184.0, A.add)
+        ts(R("ft", 0, 32), R("xb"), 402653184.0, A.add, -402653184.0, A.add)
         slot(1, 0)
-        tt(R("vv", 1, 64, 2), R("xb"), R("vv", 0, 64, 2), A.subtract)
+        tt(R("ft", 32, 64), R("xb"), R("ft", 0, 32), A.subtract)
         slot(1, 0)
-        quant("i", 0, 136, R("vv", 0, 544))
-        mm("b5", "kx", 0, "i", 0, 128, True, False)
-        mm("b5", "kx", 128, "i", 8, 128, False, True)
-        slot(3, 1)
-        copy(R("of1"), R("b5", 0, 8))
-        slot(1, 0)
+        quant("i", 0, 136, R("ft", 0, 544))
+        mm("b3", "kx", 0, "i", 0, 128, True, False)
+        mm("b3", "kx", 0, "i", 8, 128, False, True)
+        slot(2, 2)
+        mm("b6", "ke", 0, "f", 0, COLS, True, False)
+        mm("b6", "kb", 0, "f", 0, COLS, False, True)
+        copy(R("of1"), R("b3", 0, 8))
         for b in (0, 3, 1, 2):
             gather("va"[b // 2], R("hh", b, 512, 4), R("hp", PLANE * b, PLANE * b + 450), R("of1"))
-        mine = R(S, STRONG[r], STRONG[r] + 8)
-        op("v", lambda: g.vector.tensor_tensor(V(R("gm")), V(R("sb", 0, 450)).indirect(V(R("of1"))), V(R("lm")), A.mult),
-           [R("gm")], [R("sb", 0, 450), R("of1"), R("lm")])
-        quant(Z, 128 * r, 128 * r + 128, R("hh"))
-        scan(R("gs"), R("kp"), R("gm"), 0.0, A.mult, A.add)
-        slot(2, 0)
-        copy(mine, R("gs", 15, 128, 16))
-        codes = R(Z + "_q", 128 * r, 128 * r + 128)
-        if min(DIRECT[k]) < 128:
-            deps("g", "rem", [codes], [])
-            remote(g, T, topo, [(V(codes).bitcast(dt.uint8), [T.cores[others[0]]], eng, "la%d" % k),
-                                (V(codes).bitcast(dt.uint8), [helper], rest, "lh%d" % k)])
-            total["sent"] = total.get("sent", 0) + len(eng) + len(rest)
-        else:
-            send(codes, True, others[0:1], "la%d" % k)
-        send(R(Z + "_s", 128 * r, 128 * r + 128), False, others, "lp%d" % k)
-        send(mine, False, others, "lt%d" % k)
-        for n, o, sem in zip(DIRECT[k], others[1:], ("lb%d", "lc%d")):
-            if n:
-                send(R(Z + "_q", 128 * r, 128 * r + n), True, [o], sem % k)
 
-        def unpack(o, n, first, queue):
+        def wished():
+            o, i = R("yy", 576, 1024), R("b6", 0, COLS)
+            op("a", lambda: g.scalar.activation(V(o), V(i), ACT.Relu, bias=1.0, scale=-1.0), [o], [i])
+
+        if not WISH[k]:
+            wished()
+        slot(1, 0)
+        quant(Z, 128 * r, 128 * r + 128, R("hh"))
+        codes, scales = R(Z + "_q", 128 * r, 128 * r + 128), R(Z + "_s", 128 * r, 128 * r + 128)
+        if VIA[k] == "q":
+            send(codes, True, others[0:1], "la%d" % k, "lh%d" % k)
+        send(scales, False, others[:3 - (VIA[k] == "s")], "lp%d" % k, "lh%d" % k if VIA[k] == "s" else None)
+        for d in range(VIA[k] == "q", 3 - (VIA[k] == "q")):
+            send(codes, True, [others[d]], ("la%d", "lb%d", "lc%d")[d] % k)
+
+        def unpack(o, first, queue, ahead):
             for b in range(4):
-                bank = "b%d" % first[b]
-                mm(bank, "ke", 128 * b, Z, 128 * o, n)
-                (copy if queue[b] == "v" else act)(R("yp", 512 * b + 128 * o, 512 * b + 128 * o + n), R(bank, 0, n))
+                bank = "b%d" % ((first + b) % 6)
+                mm(bank, "ke", 128 * b, Z, 128 * o, 128)
+                if queue[b].isupper():
+                    ahead.pop(0)()
+                (copy if queue[b] in "vV" else act)(R("yp", 512 * b + o, 512 * b + 512, 4), R(bank, 0, 128))
 
         def lists():
             mm("b7", "ko", 0, "a", 0, 128)
-            ts(R("ofx"), R("b7", 0, 112), 512.0, A.min, B4, A.add)
+            ts(R("ofx"), R("b7", 16, 128), 512.0, A.min, B4, A.add)
 
+        tw = R("jk0", 0, 64)
+        for h in range(2):
+            i, o = R(S, 1 + 2 * h, 16, 4), R("rw", 4 * h, 4 * h + 4)
+            scan(o, i, i, LEAST, A.max, A.max)
+            count(R("jk1", 4 * h, 4 * h + 4), o, R("rw", 4 * h + 3, 4 * h + 4), R("jk0", 32 * h, 32 * h + 1))
+        if k == 0:
+            op("a", lambda: g.scalar.activation(V(R("gs")), V(R("dg")), ACT.Copy, accum_out=V(DG)), [R("gs"), DG], [R("dg")])
+        if WISH[k]:
+            wished()
+        if k == 0:
+            line(R("c8"), R("js", 0, 8), STP, DG)
+        slot(3, 1)
+        op("v", lambda: g.vector.transpose(V(R("tx")), V(tw)), [R("tx")], [tw])
+        for q in range(4):
+            o = R("tb", 64 * q, 64 * q + 64)
+            op("g", lambda: g.partition_broadcast(V(o), T.tx[32 * q:32 * q + 1, :], 128), [o], [R("tx")])
         if k == 0:
             iota(R("jw"), [[8, 224]], -752, 0)
-            fill(R("an", 448, 512), 0.0)
-            fill(R("yy", 512, 528), 0.0)
         slot(2, 0)
-        o, i = R("an", 0, COLS), R("b6", 0, COLS)
-        mm("b6", "kb", 0, "f", 0, COLS, True, False)
-        mm("b6", "ke", 0, "f", 0, COLS, False, True)
-        op("a", lambda: g.scalar.activation(V(o), V(i), ACT.Relu, bias=1.0, scale=-1.0), [o], [i])
-        unpack(r, 128, (0, 1, 2, 3), "aaaa")
-        fill(R("xt%d" % (k + 1), 1792, 1800), 0.0)
-        slot(8, 0)
-        quant("a", 0, 128, R("an"))
+        unpack(r, 0, TAKE[k][0:4], [])
+        slot(4, 0)
         if k == 0:
             for e in range(4):
                 ts(R("ko", e, 512, 4), R("jq", 12 - 4 * e, 140 - 4 * e), G28, A.is_equal, WG0, A.mult)
+        quant("a", 0, 128, R("yy", 512, 1024))
+        if k == 0:
             quant("ko", 0, 128, R("ko"))
         else:
             lists()
-        if last:
-            mm("b5", "kw", 0, "a", 0, 128)
+            mm("b6", "kw", 0, "a", 0, 128)
             for e in range(4):
-                op("v", lambda: g.vector.tensor_scalar(T.wlb[0:8, e:COLS:4], T.b5[32 * e:32 * e + 8, 0:112],
-                                                       T.cf[32 * e:32 * e + 8, PW[1]:PW[2]], None, A.add),
-                   [R("wlb", e, COLS, 4)], [R("b5"), PW])
+                op("a", lambda: g.scalar.activation(T.wlb[0:8, e:COLS:4], T.b6[32 * e:32 * e + 8, 16:128], ACT.Identity,
+                                                    bias=T.cf[32 * e:32 * e + 8, PW[1]:PW[2]]), [R("wlb", e, COLS, 4)], [R("b6"), PW])
             dma("s", "stored", T.wl[:, :], T.wlb[0:8, 0:COLS], [], [R("wlb")])
-        unpack(others[0], 128, (0, 1, 2, 3), "aaaa")
-        tt(R("sel"), R(S, 16, 32), R(S, 0, 16), A.is_gt)
-        tt(R("mx"), R(S, 16, 32), R(S, 0, 16), A.max)
-        tt(R("gg"), R("sel"), R("b16"), A.add)
-        tt(R("f8"), R("mx", 8, 16), R("mx", 0, 8), A.is_gt)
-        tt(R("e8"), R("f8"), R("gg", 8, 16), A.mult)
-        tt(R("o8"), R("e8"), R("gg", 0, 8), A.max)
-        ts(R("oft"), R("o8"), 128.0, A.mult)
-        if k == 0:
-            lists()
-        unpack(others[1], 128, (4, 5, 6, 0), "avav")
-        unpack(others[2], 128, (1, 2, 3, 4), "avav")
+        places = [lambda: op("v", lambda: g.vector.tensor_tensor(V(R("gm")), V(R("tb")).indirect(V(R("oc8"))), V(R("am")), A.add),
+                             [R("gm")], [R("tb"), R("oc8"), R("am")]),
+                  lambda: scan(R("gs"), R("gm"), R("gm"), 0.0, A.max, A.max),
+                  lambda: ts(R("oft"), R("gs", 15, 128, 16), -4.0, A.add)]
+        for d in range(3):
+            unpack(others[d], (4, 2, 0)[d], TAKE[k][4 + 4 * d:8 + 4 * d], places)
+            if k + d == 0:
+                lists()
         for b in range(4):
             gather("av"[b % 2], R("yy", b, 512, 4), R("yp", 512 * b, 512 * b + 512), R("oft"))
-        cut = TAIL if last else CUT
-        pieces = ((HEAD, cut), (cut, LAST), (LAST, COLS))
-        for lo, hi in pieces:
-            gather("a", R("gy", 4 * lo, 4 * hi), R("yy"), R("ofx", lo // 4, hi // 4))
-        o, i, f = R("xt%d" % (k + 1), 0, 4 * HEAD), R(state, 0, 4 * HEAD), R("ofx", 0, HEAD // 4)
-        op("v", lambda: g.vector.tensor_tensor(V(o), V(R("yy")).indirect(V(f)), V(i), A.add), [o], [R("yy"), f, i])
-        for c, (lo, hi) in enumerate(pieces):
-            tt(R("xt%d" % (k + 1), 4 * lo, 4 * hi), R("gy", 4 * lo, 4 * hi), R(state, 4 * lo, 4 * hi), A.add)
-            if c != 1:
-                quant_state(k + 1, c // 2)
+        head, yy = PIECES[0], R("yy", 0, 528)
+        for lo, hi in zip(PIECES, PIECES[1:]):
+            gather("a", R("gy", 4 * lo, 4 * hi), yy, R("ofx", lo // 4, hi // 4))
+        o, i, f = R("xt%d" % (k + 1), 0, 4 * head), R(state, 0, 4 * head), R("ofx", 0, head // 4)
+        op("v", lambda: g.vector.tensor_tensor(V(o), V(yy).indirect(V(f)), V(i), A.add), [o], [yy, f, i])
 
     for c, (lo, hi) in enumerate(ends):
+        for a, b in zip(PIECES, PIECES[1:]):
+            if lo < b <= hi:
+                tt(R("xt2", 4 * a, 4 * b), R("gy", 4 * a, 4 * b), R("xt1", 4 * a, 4 * b), A.add)
+        quant("x2", lo, hi, R("xt2", 4 * lo, 4 * hi))
         dma("s", "stored", T.oc[:, 4 * lo:4 * hi], V(R("x2_q", lo, hi)).bitcast(dt.uint8), [], [R("x2_q", lo, hi)])
         mm("b%d" % c, "v", 0, "x2", lo, hi - lo)
+        for q in range(4 * c):
+            dma("as"[q % 2], "stored", T.osc[4 * q:4 * q + 4, :], T.x2_s[32 * q:32 * q + 4, 0:COLS], [], [R("x2_s", 0, COLS)])
         (copy if c else act)(R("yo", lo, hi), R("b%d" % c, 0, hi - lo))
-        if c:
-            for q in range(4):
-                dma("s", "stored", T.osc[4 * q:4 * q + 4, :], T.x2_s[32 * q:32 * q + 4, 0:COLS], [], [R("x2_s", 0, COLS)])
-        dma("s", "stored", T.y[:, lo:hi], V(R("yo", lo, hi)), [], [R("yo", lo, hi)])
+        dma("sa"[c], "stored", T.y[:, lo:hi], V(R("yo", lo, hi)), [], [R("yo", lo, hi)])
     for s in sorted(total):
         wait("g", (s, total[s]))

from concourse.bass import DstId, RemoteDMATransfer
from concourse.mybir import dt, AluOpType, AxisListType, ActivationFunctionType

F8, U8, U16, I32, F32, BF = "float8_e4m3fn_x4", "uint8", "uint16", "int32", "float32", "bfloat16"
ROUNDS, COLS = 2, 448
CUT = 256
CUTS = ((0, 256, COLS), (0, 256, COLS), (0, 256, COLS))
SEARCH = ("q0 p0 x0 q1 t0 t1 k0 c0 s1 f0 w0 h0 s1 c1 s1 f1 w1 w2 w3 h1 m00 m01 m10 m11 r10 r11",
          "d0 q0 t0 d1 d2 q1 t1 w0 h0 c0 s1 f0 s1 c1 s1 f1 w1 w2 w3 h1 m00 m01 m10 m11 r10 r11")
VIA = ("s", "q")
TAKE = ("aaaa" "avav" "AAAa" "vava", "aaaa" "avav" "aVaa" "VaVa")
WISH = (0, 0)
RUN = 452
PIECES = (192, 256, 360, COLS)
PLANE = 464
SMALL, NONE, LEAST = 2.0 ** -42, -2.0 ** 29, -2.0 ** 34
SCRATCH = {}


def buf(name, n, dtype, where="sbuf"):
    SCRATCH[name] = (where, [128, n], dtype)


for _k in range(3):
    buf("xt%d" % _k, 1800, BF)
    buf("x%d_q" % _k, 450, F8)
    buf("x%d_s" % _k, 450, U8)
for _k in range(2):
    buf("z%d_q" % _k, 512, F8)
    buf("z%d_s" % _k, 512, U8)
    buf("lst%d" % _k, 16, F32)
    buf("jk%d" % _k, 448, F32)
for _n, _w in (("u", 128), ("v", 128), ("up", 256), ("w", 512), ("f", COLS), ("i", 136), ("a", 128),
               ("kh", 256), ("kx", 128), ("kb", 128), ("ko", 128), ("ke", 512), ("kw", 128)):
    buf(_n + "_q", _w, F8)
    buf(_n + "_s", _w, U8)
for _n, _w in (("ut", 512), ("vt", 512), ("ft", 64 + 4 * CUT), ("hp", 4 * PLANE), ("hh", 512), ("yp", 2048),
               ("yy", 1024), ("gy", 4 * COLS), ("kh", 1024), ("kx", 516), ("kb", 512), ("ko", 512), ("kw", 512), ("ke", 516),
               ("jm", 16), ("js", 16), ("jq", 144), ("jw", 224), ("jn", 128), ("r8", 128), ("rq", 128), ("cc", 32), ("lm", 128),
               ("am", 128), ("dg", 128)):
    buf(_n, _w, BF)
for _n, _w in (("bc", 448), ("sb", 456), ("mk", 2 * RUN), ("ru", 2 * RUN), ("ix", 2), ("xb", 32), ("gm", 128), ("gs", 128), ("rw", 8),
               ("tx", 64), ("tb", 256), ("yo", 448), ("wlb", 448), ("cf", 40), ("c8", 8), ("m32", 32), ("tab", 32)):
    buf(_n, _w, F32)
for _n, _w in (("ci", 24), ("ijt", 16), ("iju", 16), ("iu", 16)):
    buf(_n, _w, I32)
for _n, _w in (("ou", 16), ("oh", 16), ("of1", 8), ("oc8", 8), ("oft", 8), ("ofx", 112)):
    buf(_n, _w, U16)
PSUM = ["b%d" % _k for _k in range(8)]
for _n in PSUM:
    buf(_n, 512, F32, "psum")
SEMAPHORES = (["v", "a", "t", "gp", "sent", "stored", "dx0", "dx1", "du", "dv", "dw0", "dw1", "dws"]
              + ["%s%d" % (n, k) for n in ("lp", "ls", "lt", "la", "lb", "lc", "lh") for k in range(2)])


def helper_of(core, topo):
    return [c for c in topo.cores_of(core) if topo.die(c) != topo.die(core)][0]


def on_chip(core, T, topo):
    far = topo.engines(core, [c for c in T.cores if c != core][0])
    return [e for e in topo.engines(core, helper_of(core, topo)) if e not in far]


def remote(g, T, topo, transfers):
    g.remote_dma_fused([RemoteDMATransfer(dst_ids=[DstId(rid=topo.addr(c)[0], pnc=topo.addr(c)[1]) for c in to],
                                          dma_engine_mask=sum(1 << e for e in engines), remote_sem=T.sem[sem],
                                          srcs=[view], dsts=[view for c in to]) for view, to, engines, sem in transfers],
                       local_sem=T.sem.sent)


def helper_program(g, core, r, T, topo):
    eng, sent = topo.engines(core, T.cores[r ^ 3]), 0
    for k in range(ROUNDS):
        if VIA[k]:
            g.wait_ge(T.sem["lh%d" % k], len(on_chip(T.cores[r], T, topo)))
            view = T["z%d_%s" % (k, VIA[k])][:, 128 * r:128 * r + 128]
            remote(g, T, topo, [(view.bitcast(dt.uint8) if VIA[k] == "q" else view, [T.cores[r ^ 3]], eng,
                                 ("lc%d" if VIA[k] == "q" else "ls%d") % k)])
            sent += len(eng)
    if sent:
        g.wait_ge(T.sem.sent, sent)


def rank_program(g, core, T, topo):
    r = T.rank_of(core)
    if r is None:
        for o, c in enumerate(T.cores):
            if helper_of(c, topo) == core:
                helper_program(g, core, o, T, topo)
        return
    A, ACT = AluOpType, ActivationFunctionType
    queues = {"v": g.vector, "a": g.scalar, "t": g.tensor, "g": g, "s": g.sync}
    own_sem = {"v": "v", "a": "a", "t": "t", "g": "gp"}
    total, know, snap, acc = {}, {q: {} for q in queues}, {}, {}

    def R(name, lo=0, hi=None, step=1):
        return (name, lo, SCRATCH[name][1][1] if hi is None else hi, step)

    def V(x):
        return T[x[0]][:, x[1]:x[2]] if x[3] == 1 else T[x[0]][:, x[1]:x[2]:x[3]]

    def hit(p, q):
        if max(p[1], q[1]) >= min(p[2], q[2]):
            return False
        return p[3] != q[3] or (p[1] - q[1]) % p[3] == 0

    def wait(q, tok):
        sem, val = tok
        if know[q].get(sem, 0) >= val:
            return
        queues[q].wait_ge(T.sem[sem], val)
        for s, x in list(snap.get(tok, {}).items()) + [tok]:
            know[q][s] = max(know[q].get(s, 0), x)

    def deps(q, lane, reads, writes):
        need = set()
        for reg, isw in [(x, False) for x in reads] + [(x, True) for x in writes]:
            for old, oldw, oldlane, tok in acc.get(reg[0], []):
                if reg[0] in PSUM:
                    if oldlane == lane:
                        continue
                elif not (isw or oldw) or not hit(old, reg):
                    continue
                need.add(tok)
        for tok in sorted(need, key=lambda x: -x[1]):
            wait(q, tok)

    def note(lane, tok, reads, writes):
        for reg, isw in [(x, False) for x in reads] + [(x, True) for x in writes]:
            acc.setdefault(reg[0], []).append((reg, isw, lane, tok))

    def op(q, fn, writes, reads):
        deps(q, q, reads, writes)
        s = own_sem[q]
        total[s] = total.get(s, 0) + 1
        tok = (s, total[s])
        fn().then_inc(T.sem[s], 1)
        snap[tok] = dict(know[q])
        note(q, tok, reads, writes)

    def dma(q, sem, out, in_, writes, reads):
        deps(q, "dma", reads, writes)
        total[sem] = total.get(sem, 0) + 16
        queues[q].dma_start(out, in_).then_inc(T.sem[sem], 16)
        tok = (sem, total[sem])
        snap[tok] = dict(know[q])
        note("dma", tok, reads, writes)

    def memset(o, c):
        op("v", lambda: g.vector.memset(V(o), c), [o], [])

    def copy(o, i):
        op("v", lambda: g.vector.tensor_copy(V(o), V(i)), [o], [i])

    def tt(o, i, j, f):
        op("v", lambda: g.vector.tensor_tensor(V(o), V(i), V(j), f), [o], [i, j])

    def ts(o, i, s1, f1, s2=None, f2=None):
        v = lambda s: V(s) if isinstance(s, tuple) else s
        rd = [i] + [s for s in (s1, s2) if isinstance(s, tuple)]
        if f2 is None:
            op("v", lambda: g.vector.tensor_scalar(V(o), V(i), v(s1), None, f1), [o], rd)
        else:
            op("v", lambda: g.vector.tensor_scalar(V(o), V(i), v(s1), v(s2), f1, f2), [o], rd)

    def red(o, i, f):
        op("v", lambda: g.vector.tensor_reduce(V(o), V(i), AxisListType.X, f), [o], [i])

    def scan(o, i, j, init, f1, f2):
        col = isinstance(init, tuple)
        op("v", lambda: g.vector.tensor_tensor_scan(V(o), V(i), V(j), V(init) if col else init, f1, f2), [o], [i, j] + [init] * col)

    def act(o, i, scale=1.0, bias=0.0):
        op("a", lambda: g.scalar.activation(V(o), V(i), ACT.Copy, bias=bias, scale=scale), [o], [i])

    def line(o, i, scale, bias):
        v = lambda s: V(s) if isinstance(s, tuple) else s
        op("a", lambda: g.scalar.activation(V(o), V(i), ACT.Identity, bias=v(bias), scale=v(scale)), [o],
           [i] + [s for s in (scale, bias) if isinstance(s, tuple)])

    def count(o, i, top, n):
        op("a", lambda: g.scalar.activation(V(o), V(i), ACT.Sign, bias=V(top), scale=-1.0, accum_out=V(n)), [o, n], [i, top])

    def gather(q, o, w, f):
        if q == "v":
            op("v", lambda: g.vector.tensor_copy(V(o), V(w).indirect(V(f))), [o], [w, f])
        else:
            op("a", lambda: g.scalar.activation(V(o), V(w).indirect(V(f)), ACT.Copy), [o], [w, f])

    def iota(o, pattern, base, ch):
        if SCRATCH[o[0]][2] == I32:
            op("g", lambda: g.iota(V(o), pattern, base, ch), [o], [])
        else:
            op("g", lambda: g.iota(V(o), pattern, base, ch, allow_small_or_imprecise_dtypes=True), [o], [])

    def quant(m, lo, hi, i):
        q, s = R(m + "_q", lo, hi), R(m + "_s", lo, hi)
        op("v", lambda: g.vector.quantize_mx(V(q), V(s), V(i)), [q, s], [i])

    def mm(bank, w, wlo, m, mlo, n, start=True, stop=True):
        o = R(bank, 0, n)
        i = [R(w + "_q", wlo, wlo + 128), R(w + "_s", wlo, wlo + 128), R(m + "_q", mlo, mlo + n), R(m + "_s", mlo, mlo + n)]
        op("t", lambda: g.tensor.matmul_mx(V(o), V(i[0]), V(i[1]), V(i[2]), V(i[3]), start, stop), [o], i)

    def pick(o, lo, hi, w, wide, f):
        q, wq = R(o + "_q", lo, hi), R(w + "_q", 0, wide)
        op("v", lambda: g.vector.tensor_copy(V(q).bitcast(dt.uint32), V(wq).bitcast(dt.uint32).indirect(V(f))), [q], [wq, f])
        gather("a", R(o + "_s", lo, hi), R(w + "_s", 0, wide), f)

    def cf(k):
        return R("cf", k, k + 1)

    def tab(k, n=8):
        return R("tab", k, k + n)

    others = [r ^ d for d in (1, 2, 3)]
    eng = topo.engines(core, T.cores[others[0]])

    helper = helper_of(core, topo)
    rest = on_chip(core, T, topo)

    def send(piece, codes, to, sem, via=None):
        deps("g", "rem", [piece], [])
        view = V(piece).bitcast(dt.uint8) if codes else V(piece)
        remote(g, T, topo, [(view, [T.cores[o] for o in to], eng, sem)] + [(view, [helper], rest, via)] * bool(via))
        total["sent"] = total.get("sent", 0) + len(eng) + len(rest) * bool(via)

    STRONG = [0, 4, 8, 12]
    for k in range(ROUNDS):
        n = 3 - (VIA[k] == "s")
        lands = [("lp%d", n, [R("z%d_s" % k, 128 * o, 128 * o + 128) for o in others[:n]]),
                 ("ls%d", 3 - n, [R("z%d_s" % k, 128 * o, 128 * o + 128) for o in others[n:]]),
                 ("lt%d", 3, [R("lst%d" % k, STRONG[o], STRONG[o] + 4) for o in others])]
        lands += [(s, 1, [R("z%d_q" % k, 128 * o, 128 * o + 128)]) for s, o in zip(("la%d", "lb%d", "lc%d"), others)]
        for sem, n, regs in lands:
            total[sem % k] = n * len(eng)
            note("rem", (sem % k, n * len(eng)), [], regs)

    dma("s", "du", V(R("ut")), T.u[:, :], [R("ut")], [])
    for c, (lo, hi) in enumerate(zip(CUTS[0], CUTS[0][1:])):
        dma("s", "dx%d" % c, T.xt0[:, 4 * lo:4 * hi], T.x[:, 4 * lo:4 * hi], [R("xt0", 4 * lo, 4 * hi)], [])
    wait("s", ("du", 16))
    dma("s", "dws", V(R("w_s")), T.ws[:, :], [R("w_s")], [])
    for e in range(2):
        o = R("w_q", 256 * e, 256 * e + 256)
        dma("s", "dw%d" % e, V(o).bitcast(dt.uint8), T.wc[:, 1024 * e:1024 * e + 1024], [o], [])
    wait("s", ("dw1", 16))
    dma("s", "dv", V(R("vt")), T.v[:, :], [R("vt")], [])

    LO4, L8, LO16, LO32, HI4, HI8, HI16 = [cf(k) for k in (0, 1, 3, 7, 8, 9, 11)]
    P, B4, IPW, IS, G28, WG0, WG1, PW, NZ, HB, ISB, F2, STP, DG = [cf(k) for k in range(16, 30)]

    def fill(o, c):
        act(o, R("kh", 0, o[2] - o[1]), 0.0, c)

    memset(R("kh"), 0.0)
    fill(R("kx"), 0.0)
    fill(R("ft", 64 + 2 * CUT, 64 + 4 * CUT), 0.0)
    iota(P, [[0, 1]], 0, 1)
    iota(R("js", 0, 8), [[16, 8]], 0, 0)
    iota(R("js", 8, 16), [[4, 8]], 4, 0)
    iota(R("jm"), [[256, 2], [512, 4], [128, 2]], 0, 0)
    iota(R("iu", 0, 8), [[16, 8]], 1, 0)
    iota(R("iu", 8, 16), [[0, 8]], 15, 0)
    iota(R("ft", 64, 64 + 2 * CUT), [[0, 2 * CUT]], 0, 0)
    iota(R("xt0", 1792, 1800), [[0, 8]], 0, 0)
    iota(R("cc", 0, 16), [[-64, 2], [64, 8]], 0, 0)
    iota(R("cc", 16, 32), [[0, 2], [16, 8]], 0, 0)
    for grp in range(8):
        b, f = (grp, 4) if grp < 5 else (grp - 3, 32)
        iota(R("rq", 16 * grp, 16 * grp + 16), [[f << b + 1, 16 >> b], [f, 1 << b]], f << b, 0)

    def ones(o, pattern, base):
        i = R("kx", 0, o[2])
        op("g", lambda: g.affine_select(V(o), V(i), pattern, A.not_equal, 1.0, base, 4), [o], [i])

    ones(R("ke"), [[-1, 516]], 3)
    ones(R("kb"), [[0, 8], [-64, 16], [1, 4]], 128)
    iota(R("r8"), [[0, 8], [8, 16]], 0, 0)
    ts(tab(0, 7), R("js", 1, 8), P, A.is_gt, 1.0, A.add)
    ts(R("ci", 0, 8), R("js", 8, 16), P, A.mult)
    red(IPW, tab(0, 7), A.mult)
    ts(R("ci", 8, 16), R("ci", 0, 8), 127, A.bitwise_and)
    ts(R("ci", 16, 24), R("ci", 0, 8), 3968, A.bitwise_and)
    ts(ISB, P, 80.0, A.is_ge)
    copy(R("cf", 0, 16), R("ci", 8, 24))
    copy(R("ou"), R("iu"))
    ts(R("ijt"), R("jm"), L8, A.add, IPW, A.mult)
    ts(IS, L8, 0.0, A.is_equal, 128.0, A.mult)
    ts(R("iju"), R("ijt"), 1024, A.bitwise_and, 10, A.logical_shift_right)
    ts(R("c8", 0, 2), R("js", 0, 2), IS, A.mult, -2.0 ** 19, A.mult)
    copy(R("oh"), R("iju"))
    gather("a", R("kh", 0, 1024, 4), R("c8", 0, 2), R("oh"))
    quant("u", 0, 128, R("ut"))
    memset(R("mk", COLS, 2 * RUN, RUN), NONE)
    pick("up", 0, 128, "u", 128, R("ou", 0, 8))

    def spare_first():
        yield ts(R("m32", 0, 32, 2), R("cc", 0, 16), HI4, A.is_equal)
        yield ts(R("m32", 1, 32, 2), R("cc", 16, 32), LO16, A.is_equal)
        yield ts(tab(10, 1), L8, 80.0, A.is_lt)
        for h in range(2):
            yield ts(R("kx", h, 320, 4), R("rq", 0, 80), LO4, A.is_equal)
        for h in range(2):
            yield ts(R("kx", 322 + h, 512, 4), R("rq", 80, 128), 128.0 * h, A.subtract, HB, A.is_equal)
        yield ts(F2, L8, 40.0, A.is_lt, 15.875, A.mult)
        yield quant("kx", 0, 128, R("kx", 0, 512))
        yield ts(tab(13, 1), F2, 0.875, A.subtract, ISB, A.mult)
        yield tt(R("dg"), R("ke", 3, 515, 4), R("rq"), A.mult)
        yield ts(tab(11, 1), L8, G28, A.is_le, 0.5, A.max)
        yield quant("ke", 0, 128, R("ke", 3, 515))
        yield quant("kb", 0, 128, R("kb"))
        yield quant("ke", 128, 256, R("ke", 2, 514))
        yield ts(tab(0, 10), R("r8", 0, 10), L8, A.is_lt, 1.0, A.add)
        yield ts(tab(12, 1), tab(13, 1), 1.0, A.add)
        yield ts(R("lm"), R("r8"), L8, A.is_equal)
        for b in range(2, 4):
            yield quant("ke", 128 * b, 128 * b + 128, R("ke", 3 - b, 515 - b))
        yield red(WG1, tab(0, 13), A.mult)
        yield tt(R("am"), R("lm"), R("jn"), A.mult)
        yield ts(WG0, IS, 4.0, A.mult, WG1, A.max)
        yield ts(R("oc8"), R("c8"), 0.25, A.mult)

    def spare_last():
        yield red(PW, tab(0, 11), A.mult)
        yield ts(NZ, L8, G28, A.not_equal, L8, A.min)
        yield ts(WG1, PW, NZ, A.mult, 0.25, A.mult)
        yield quant("v", 0, 128, R("vt"))
        for e in range(4):
            yield ts(R("kw", e, 512, 4), R("jw", 96 - 32 * e, 224 - 32 * e), G28, A.is_equal, WG1, A.mult)
        yield quant("kw", 0, 128, R("kw"))

    spare = [spare_first(), spare_last()]

    ends = list(zip(CUTS[ROUNDS], CUTS[ROUNDS][1:]))

    for k in range(ROUNDS):
        X, state, Z, S = "x%d" % k, "xt%d" % k, "z%d" % k, "lst%d" % k
        last = k == ROUNDS - 1

        def slot(*n):
            for _ in range(n[k]):
                next(spare[k])

        chunks, done = list(zip(CUTS[k], CUTS[k][1:])), [0, 0]
        wb = ("b7", "b0", "b1", "b2") if len(chunks) == 3 else ("b6", "b7", "b4", "b5")

        def scores(c):
            lo, hi = chunks[c]
            end = hi + 2 * (hi == COLS)
            quant(X, lo, end, R(state, 4 * lo, 4 * end))
            mm("b%d" % (2 * c), "up", 0, X, lo, hi - lo)
            mm("b%d" % (2 * c + 1), "u", 0, X, lo, hi - lo)
            act(R("bc", lo, hi), R("b%d" % (2 * c), 0, hi - lo))

        def strengths(c):
            lo, hi = chunks[c]
            bank = "b%d" % (2 * len(chunks) + c % 2)
            mm(bank, "up", 128, X, lo, hi - lo)
            act(R("sb", lo, hi), R(bank, 0, hi - lo), SMALL)

        def absent(c):
            lo, hi = chunks[c]
            tt(R("ft", 64, 64 + 4 * (hi - lo), 4), R("b%d" % (2 * c + 1), 0, hi - lo), R("bc", lo, hi), A.is_le)

        def flags(c):
            lo, hi = chunks[c]
            quant("f", lo, hi, R("ft", 64, 64 + 4 * (hi - lo)))
            for h in range(2):
                mm("b%d" % (2 * c + h), "kh", 128 * h, "f", lo, hi - lo)

        def masked(c, h):
            lo, hi = chunks[c]
            tt(R("mk", RUN * h + lo, RUN * h + hi), R("b%d" % (2 * c + h), 0, hi - lo), R("sb", lo, hi), A.add)

        def running(c, h):
            lo, hi = RUN * h + done[h], RUN * h + chunks[c][1] + (chunks[c][1] == COLS)
            scan(R("ru", lo, hi), R("mk", lo, hi), R("mk", lo, hi), R("ru", lo - 1, lo) if done[h] else LEAST, A.max, A.max)
            done[h] = chunks[c][1]
            if done[h] == COLS:
                count(R("jk%d" % h), R("ru", RUN * h, hi - 1), R("ru", hi - 1, hi), R("ix", h, h + 1))

        def added(c):
            lo, hi = PIECES[c:c + 2]
            tt(R(state, 4 * lo, 4 * hi), R("gy", 4 * lo, 4 * hi), R("xt%d" % (k - 1), 4 * lo, 4 * hi), A.add)

        def small(c):
            fill(R("yy", 512, 576), 0.0)
            line(HB, HI16, 0.25, HI4)
            line(G28, HI8, 0.0625, 16.0)
            line(B4, LO32, 0.03125, 0.0)
            line(STP, ISB, -7.75, 8.0)

        steps = {"q": scores, "t": strengths, "c": absent, "f": flags, "m": masked, "r": running, "d": added, "k": small,
                 "p": lambda n: pick("up", 128, 256, "u", 128, R("ou", 8, 16)),
                 "x": lambda n: quant("kh", 0, 256, R("kh")),
                 "s": lambda n: slot(n, n), "w": lambda b: mm(wb[b], "w", 128 * b, X, 0, 450),
                 "h": lambda b: act(R("hp", PLANE * b, PLANE * b + 450), R(wb[b], 0, 450), 0.03125)}
        for step in SEARCH[k].split():
            steps[step[0]](*map(int, step[1:]))
        mine = R(S, STRONG[r], STRONG[r] + 4)
        copy(mine, R("ru", COLS - RUN // 2, COLS + RUN + 1, RUN // 2))
        send(mine, False, others, "lt%d" % k)
        if k == 0:
            iota(R("jq"), [[2, 36], [0, 4]], 10, 0)
            iota(R("jn"), [[4, 128]], 4, 0)
            iota(R("xt1", 1792, 1800), [[0, 8]], 0, 0)
        for b in range(2, 4):
            steps["h"](b)
        slot(6, 3)
        for h in range(2):
            ts(R("xb", h, 32, 2), R("m32", 16 * h, 16 * h + 16), R("ix", h, h + 1), A.mult)
        slot(1, 0)
        ts(R("ft", 0, 32), R("xb"), 402653184.0, A.add, -402653184.0, A.add)
        slot(1, 0)
        tt(R("ft", 32, 64), R("xb"), R("ft", 0, 32), A.subtract)
        slot(1, 0)
        quant("i", 0, 136, R("ft", 0, 544))
        mm("b3", "kx", 0, "i", 0, 128, True, False)
        mm("b3", "kx", 0, "i", 8, 128, False, True)
        slot(2, 2)
        mm("b6", "ke", 0, "f", 0, COLS, True, False)
        mm("b6", "kb", 0, "f", 0, COLS, False, True)
        copy(R("of1"), R("b3", 0, 8))
        for b in (0, 3, 1, 2):
            gather("va"[b // 2], R("hh", b, 512, 4), R("hp", PLANE * b, PLANE * b + 450), R("of1"))

        def wished():
            o, i = R("yy", 576, 1024), R("b6", 0, COLS)
            op("a", lambda: g.scalar.activation(V(o), V(i), ACT.Relu, bias=1.0, scale=-1.0), [o], [i])

        if not WISH[k]:
            wished()
        slot(1, 0)
        quant(Z, 128 * r, 128 * r + 128, R("hh"))
        codes, scales = R(Z + "_q", 128 * r, 128 * r + 128), R(Z + "_s", 128 * r, 128 * r + 128)
        if VIA[k] == "q":
            send(codes, True, others[0:1], "la%d" % k, "lh%d" % k)
        send(scales, False, others[:3 - (VIA[k] == "s")], "lp%d" % k, "lh%d" % k if VIA[k] == "s" else None)
        for d in range(VIA[k] == "q", 3 - (VIA[k] == "q")):
            send(codes, True, [others[d]], ("la%d", "lb%d", "lc%d")[d] % k)

        def unpack(o, first, queue, ahead):
            for b in range(4):
                bank = "b%d" % ((first + b) % 6)
                mm(bank, "ke", 128 * b, Z, 128 * o, 128)
                if queue[b].isupper():
                    ahead.pop(0)()
                (copy if queue[b] in "vV" else act)(R("yp", 512 * b + o, 512 * b + 512, 4), R(bank, 0, 128))

        def lists():
            mm("b7", "ko", 0, "a", 0, 128)
            ts(R("ofx"), R("b7", 16, 128), 512.0, A.min, B4, A.add)

        tw = R("jk0", 0, 64)
        for h in range(2):
            i, o = R(S, 1 + 2 * h, 16, 4), R("rw", 4 * h, 4 * h + 4)
            scan(o, i, i, LEAST, A.max, A.max)
            count(R("jk1", 4 * h, 4 * h + 4), o, R("rw", 4 * h + 3, 4 * h + 4), R("jk0", 32 * h, 32 * h + 1))
        if k == 0:
            op("a", lambda: g.scalar.activation(V(R("gs")), V(R("dg")), ACT.Copy, accum_out=V(DG)), [R("gs"), DG], [R("dg")])
        if WISH[k]:
            wished()
        if k == 0:
            line(R("c8"), R("js", 0, 8), STP, DG)
        slot(3, 1)
        op("v", lambda: g.vector.transpose(V(R("tx")), V(tw)), [R("tx")], [tw])
        for q in range(4):
            o = R("tb", 64 * q, 64 * q + 64)
            op("g", lambda: g.partition_broadcast(V(o), T.tx[32 * q:32 * q + 1, :], 128), [o], [R("tx")])
        if k == 0:
            iota(R("jw"), [[8, 224]], -752, 0)
        slot(2, 0)
        unpack(r, 0, TAKE[k][0:4], [])
        slot(4, 0)
        if k == 0:
            for e in range(4):
                ts(R("ko", e, 512, 4), R("jq", 12 - 4 * e, 140 - 4 * e), G28, A.is_equal, WG0, A.mult)
        quant("a", 0, 128, R("yy", 512, 1024))
        if k == 0:
            quant("ko", 0, 128, R("ko"))
        else:
            lists()
            mm("b6", "kw", 0, "a", 0, 128)
            for e in range(4):
                op("a", lambda: g.scalar.activation(T.wlb[0:8, e:COLS:4], T.b6[32 * e:32 * e + 8, 16:128], ACT.Identity,
                                                    bias=T.cf[32 * e:32 * e + 8, PW[1]:PW[2]]), [R("wlb", e, COLS, 4)], [R("b6"), PW])
            dma("s", "stored", T.wl[:, :], T.wlb[0:8, 0:COLS], [], [R("wlb")])
        places = [lambda: op("v", lambda: g.vector.tensor_tensor(V(R("gm")), V(R("tb")).indirect(V(R("oc8"))), V(R("am")), A.add),
                             [R("gm")], [R("tb"), R("oc8"), R("am")]),
                  lambda: scan(R("gs"), R("gm"), R("gm"), 0.0, A.max, A.max),
                  lambda: ts(R("oft"), R("gs", 15, 128, 16), -4.0, A.add)]
        for d in range(3):
            unpack(others[d], (4, 2, 0)[d], TAKE[k][4 + 4 * d:8 + 4 * d], places)
            if k + d == 0:
                lists()
        for b in range(4):
            gather("av"[b % 2], R("yy", b, 512, 4), R("yp", 512 * b, 512 * b + 512), R("oft"))
        head, yy = PIECES[0], R("yy", 0, 528)
        for lo, hi in zip(PIECES, PIECES[1:]):
            gather("a", R("gy", 4 * lo, 4 * hi), yy, R("ofx", lo // 4, hi // 4))
        o, i, f = R("xt%d" % (k + 1), 0, 4 * head), R(state, 0, 4 * head), R("ofx", 0, head // 4)
        op("v", lambda: g.vector.tensor_tensor(V(o), V(yy).indirect(V(f)), V(i), A.add), [o], [yy, f, i])

    for c, (lo, hi) in enumerate(ends):
        for a, b in zip(PIECES, PIECES[1:]):
            if lo < b <= hi:
                tt(R("xt2", 4 * a, 4 * b), R("gy", 4 * a, 4 * b), R("xt1", 4 * a, 4 * b), A.add)
        quant("x2", lo, hi, R("xt2", 4 * lo, 4 * hi))
        dma("s", "stored", T.oc[:, 4 * lo:4 * hi], V(R("x2_q", lo, hi)).bitcast(dt.uint8), [], [R("x2_q", lo, hi)])
        mm("b%d" % c, "v", 0, "x2", lo, hi - lo)
        for q in range(4 * c):
            dma("as"[q % 2], "stored", T.osc[4 * q:4 * q + 4, :], T.x2_s[32 * q:32 * q + 4, 0:COLS], [], [R("x2_s", 0, COLS)])
        (copy if c else act)(R("yo", lo, hi), R("b%d" % c, 0, hi - lo))
        dma("sa"[c], "stored", T.y[:, lo:hi], V(R("yo", lo, hi)), [], [R("yo", lo, hi)])
    for s in sorted(total):
        wait("g", (s, total[s]))
